import numpy as np
import ml_dtypes


def mxq(x, axis, fmt="e4m3"):
    dtype, down = {"e4m3": (ml_dtypes.float8_e4m3fn, 7), "e5m2": (ml_dtypes.float8_e5m2, 14)}[fmt]
    v = np.moveaxis(np.asarray(x, np.float32).astype(ml_dtypes.bfloat16).astype(np.float64), axis, -1)
    blocks = v.reshape(v.shape[:-1] + (-1, 32))
    amax = np.abs(blocks).max(-1, keepdims=True)
    byte = np.maximum(np.where(amax > 0, np.frexp(amax)[1] - 1 + 127, 0) - down, 1)
    scale = np.exp2(byte - 127.0)
    codes = (blocks / scale).astype(np.float32).astype(dtype).astype(np.float64)
    return np.moveaxis((codes * scale).reshape(v.shape), -1, axis)


WIDE = False


def mx_kscale(k):
    if not WIDE:
        return np.ones(k)
    levels = np.array([10, -10, 5, -5, 0])
    if k % 512:
        return np.exp2(np.random.permutation(np.resize(levels, k // 32))).repeat(32)
    a = np.empty((k // 512, 16))
    for p in range(k // 512):
        a[p, :8] = np.random.permutation(np.resize(levels, 8))
        for g in range(8):
            far = levels[np.abs(levels - a[p, g]) >= 10]
            a[p, g + 8] = far[np.random.randint(len(far))]
    return np.exp2(a.ravel()).repeat(32)


def f64(x):
    return np.asarray(x).astype(np.float64)


def striped(idx):
    return np.tile(idx.reshape(-1, 16).T, (8, 1)).astype(np.uint16)


def unstriped(offs):
    return offs[:16].T.reshape(-1).astype(np.int64)


E2M1 = np.array([0.0, 0.5, 1.0, 1.5, 2.0, 3.0, 4.0, 6.0, -0.0, -0.5, -1.0, -1.5, -2.0, -3.0, -4.0, -6.0])


def pack_weight(w, fmt):
    k, n = w.shape
    w = f64(np.asarray(w, np.float32).astype(ml_dtypes.bfloat16)).reshape(k // 32, 32, n)
    amax = np.abs(w).max(1)
    if fmt == "e4m3":
        byte = np.frexp(amax)[1] - 1 + 127 - 7
    else:
        mant, ex = np.frexp(amax / 6.0)
        byte = np.where(mant > 0.5, ex, ex - 1) + 127
    byte = np.clip(np.where(amax > 0, byte, 1), 1, 254)
    scaled = (w * np.exp2(127.0 - byte)[:, None, :]).reshape(k, n).astype(np.float32)
    by_word = np.ascontiguousarray(scaled.reshape(k // 512, 128, 4, n).transpose(0, 1, 3, 2))
    if fmt == "e4m3":
        words = by_word.astype(ml_dtypes.float8_e4m3fn).view(np.uint8)
    else:
        c = by_word.astype(ml_dtypes.float4_e2m1fn).view(np.uint8) & 0xF
        words = (c[..., 0::2] | (c[..., 1::2] << 4)).reshape(k // 512, 128, 2 * n)
    return np.ascontiguousarray(words), np.ascontiguousarray(byte.astype(np.uint8).reshape(k // 512, 16, n))


def unpack_weight(words, scales, fmt):
    g, _, n = scales.shape
    words = np.ascontiguousarray(words).reshape(g, 128, n, -1)
    if fmt == "e4m3":
        vals = words.view(ml_dtypes.float8_e4m3fn).astype(np.float64)
    else:
        nib = np.empty((g, 128, n, 4), np.uint8)
        nib[..., 0::2] = words & 0xF
        nib[..., 1::2] = words >> 4
        vals = E2M1[nib]
    vals = vals * np.repeat(np.exp2(scales.astype(np.float64) - 127.0), 8, axis=1)[..., None]
    return vals.transpose(0, 1, 3, 2).reshape(g * 512, n)


def d_relu2(v):
    return 2.0 * np.maximum(v, 0.0)


K, T, E, C, H, N = 512, 1024, 3, 256, 512, 1024


def by_expert(wq, xq):
    return np.concatenate([wq[e].T @ xq[:, e * C:(e + 1) * C] for e in range(E)], axis=1)


def setup_inputs():
    n = np.random.standard_normal
    s = mx_kscale(K)
    v = mx_kscale(N)
    u = mx_kscale(H)
    slot_token = np.random.permutation(T)[:E * C]
    w_slot = np.random.uniform(0.2, 1.0, E * C)
    x = pack_weight(n((K, T)) * s[:, None], "e4m3")
    dy = pack_weight(n((N, T)) * v[:, None], "e4m3")
    m1 = n((E, K, H))
    w1 = [pack_weight(m, "e2m1") for m in m1 / np.sqrt(K) / s[None, :, None]]
    w2t = [pack_weight(m, "e2m1") for m in n((E, N, H)) / np.sqrt(N) / v[None, :, None] * u]
    w1t = [pack_weight(m, "e2m1") for m in m1.transpose(0, 2, 1) / np.sqrt(H) / u[None, :, None]]
    return {
        "x_words": x[0],
        "x_scales": x[1],
        "dy_words": dy[0],
        "dy_scales": dy[1],
        "w1_words": np.stack([m[0] for m in w1]),
        "w1_scales": np.stack([m[1] for m in w1]),
        "w2t_words": np.stack([m[0] for m in w2t]),
        "w2t_scales": np.stack([m[1] for m in w2t]),
        "w1t_words": np.stack([m[0] for m in w1t]),
        "w1t_scales": np.stack([m[1] for m in w1t]),
        "gate": (np.tile(w_slot, (128, 1))).astype(np.float32),
        "offs": striped(slot_token),
    }


def reference(x_words, x_scales, dy_words, dy_scales, w1_words, w1_scales, w2t_words, w2t_scales, w1t_words, w1t_scales, gate, offs):
    w1 = np.stack([unpack_weight(w1_words[e], w1_scales[e], "e2m1") for e in range(E)])
    w2t = np.stack([unpack_weight(w2t_words[e], w2t_scales[e], "e2m1") for e in range(E)])
    w1t = np.stack([unpack_weight(w1t_words[e], w1t_scales[e], "e2m1") for e in range(E)])
    idx = unstriped(offs)
    xq = unpack_weight(x_words, x_scales, "e4m3")[:, idx]
    gq = unpack_weight(dy_words, dy_scales, "e4m3")[:, idx]
    dh = f64(gate[:1]) * by_expert(w2t, gq)
    a = by_expert(w1, xq)
    dx = by_expert(w1t, mxq(dh * d_relu2(a), 0, "e4m3"))
    out = np.zeros((K, T))
    out[:, idx] = dx
    return out

@@ -1,0 +1,155 @@
+from contextlib import ExitStack
+
+import concourse.mybir as mybir
+from concourse.masks import make_identity
+
+K, T, E, C, H, N = 512, 1024, 3, 256, 512, 1024
+S = E * C
+FLOPS = 2 * S * (K * H + N * H + H * K)
+
+F32 = mybir.dt.float32
+BF16 = mybir.dt.bfloat16
+I32 = mybir.dt.int32
+U32 = mybir.dt.uint32
+U16 = mybir.dt.uint16
+U8 = mybir.dt.uint8
+FP8X4 = mybir.dt.float8_e4m3fn_x4
+FP4X4 = mybir.dt.float4_e2m1fn_x4
+MULT = mybir.AluOpType.mult
+RELU = mybir.ActivationFunctionType.Relu
+
+P = 128
+NP = N // 512
+HALVES = C // P
+KB = K // P
+
+
+def tile_moe_rec_mlp_relu2_kernel(
+    tc, x_words, x_scales, dy_words, dy_scales, w1_words, w1_scales, w2t_words, w2t_scales,
+    w1t_words, w1t_scales, gate, offs, out
+):
+    nc = tc.nc
+    with ExitStack() as ctx:
+        keep = ctx.enter_context(tc.tile_pool(name="keep", bufs=1))
+        psum = ctx.enter_context(tc.psum_pool(name="psum", bufs=2))
+
+        offsets = keep.tile([P, S // 16], U16, name="offsets")
+        xw = keep.tile([P, T], I32, name="xw", align_bytes=64)
+        xs = keep.tile([P, T], U8, name="xs", align_bytes=64)
+        dyw = [keep.tile([P, T], I32, name="dyw%d" % s, align_bytes=64) for s in range(NP)]
+        dys = keep.tile([P, T], U8, name="dys", align_bytes=64)
+        w1s = keep.tile([P, E, H], U8, name="w1s", align_bytes=64)
+        w2s = keep.tile([P, E * NP, H], U8, name="w2s", align_bytes=64)
+        w3s = keep.tile([P, E, K], U8, name="w3s", align_bytes=64)
+        gcol = keep.tile([P, S // P], F32, name="gcol")
+        ident = keep.tile([P, P], F32, name="ident")
+        win = [keep.tile([P, T], F32, name="win%d" % kb, align_bytes=64) for kb in range(KB)]
+
+        gxw = keep.tile([P, S], U32, name="gxw", align_bytes=64)
+        gxs = keep.tile([P, S], U8, name="gxs", align_bytes=64)
+        gdw = keep.tile([P, NP, S], U32, name="gdw", align_bytes=64)
+        gds = [keep.tile([P, S], U8, name="gds%d" % s, align_bytes=64) for s in range(NP)]
+        zero = keep.tile([P, 8], F32, name="zero")
+        relu2 = keep.tile([P, S // P, H], F32, name="relu2", align_bytes=64)
+        da = keep.tile([P, S // P, H], BF16, name="da", align_bytes=64)
+        grouped = keep.tile([P, S, 4], BF16, name="grouped", align_bytes=64)
+        daw = keep.tile([P, S], U32, name="daw", align_bytes=64)
+        das = keep.tile([P, S], U8, name="das", align_bytes=64)
+        dxs = keep.tile([P, KB, S], F32, name="dxs", align_bytes=64)
+
+        def load_scales(plane, rows, queue=nc.sync):
+            for q in range(4):
+                queue.dma_start(out=plane[32 * q : 32 * q + 4].bitcast(I32), in_=rows[4 * q : 4 * q + 4].bitcast(I32))
+
+        w1w = keep.tile([P, E, 2 * H], U8, name="w1w", align_bytes=64)
+        w2w = keep.tile([P, E * NP, 2 * H], U8, name="w2w", align_bytes=64)
+        w3w = keep.tile([P, E, 2 * K], U8, name="w3w", align_bytes=64)
+
+        def entries(a, b):
+            return offsets[:, a // 16 : b // 16]
+
+        nc.gpsimd.memset(w1s[:].bitcast(I32), 0)
+        nc.vector.memset(dys[:].bitcast(I32), 0)
+        nc.vector.memset(xs[:].bitcast(I32), 0)
+        nc.vector.memset(zero[:], 0.0)
+        nc.vector.memset(w2s[:].bitcast(I32), 0)
+        nc.vector.memset(w3s[:].bitcast(I32), 0)
+        nc.vector.memset(gds[1][:].bitcast(I32), 0)
+
+        load_scales(w1s, w1_scales.rearrange("e s b n -> b (e s) n"), nc.gpsimd)
+        make_identity(nc, ident[:])
+        load_scales(w3s, w1t_scales.rearrange("e s b n -> b (e s) n"), nc.gpsimd)
+
+        nc.sync.dma_start(offsets[:], offs)
+        nc.sync.dma_start(out=xw[:], in_=x_words[0].rearrange("p t d -> p (t d)").bitcast(I32))
+        for q in range(4):
+            nc.sync.dma_start(out=dys[32 * q : 32 * q + 4 * NP, :].bitcast(I32), in_=dy_scales[:, 4 * q : 4 * q + 4, :].bitcast(I32))
+        load_scales(xs, x_scales[0])
+        for s in range(NP):
+            nc.sync.dma_start(out=dyw[s][:], in_=dy_words[s].rearrange("p t d -> p (t d)").bitcast(I32))
+        nc.sync.dma_start(out=w1w[:].bitcast(I32), in_=w1_words.rearrange("e s p n -> p (e s) n").bitcast(I32))
+        load_scales(w2s, w2t_scales.rearrange("e s b n -> b (e s) n"))
+        w2_rows = w2t_words.rearrange("e s p n -> p (e s) n").bitcast(I32)
+        nc.sync.dma_start(out=w2w[:, :NP, :].bitcast(I32), in_=w2_rows[:, :NP, :])
+
+        nc.vector.tensor_copy(gxw[:], xw[:].bitcast(U32).indirect(offsets[:]))
+        nc.vector.tensor_copy(gds[0][:], dys[:].indirect(offsets[:]))
+        nc.vector.tensor_copy(gxs[:], xs[:].indirect(offsets[:]))
+        nc.sync.dma_start(out=gds[1][0:100, :].bitcast(I32), in_=gds[0][4:104, :].bitcast(I32))
+
+        with nc.allow_non_contiguous_dma(reason="one gate value a slot"):
+            nc.sync.dma_start(out=gcol[:], in_=gate[0].rearrange("(c p) -> p c", p=P))
+        nc.sync.dma_start(out=w2w[:, NP:, :].bitcast(I32), in_=w2_rows[:, NP:, :])
+        nc.sync.dma_start(out=w3w[:].bitcast(I32), in_=w1t_words.rearrange("e s p n -> p (e s) n").bitcast(I32))
+
+        for kb in range(KB):
+            nc.scalar.activation(win[kb][:], zero[:, 0:1].to_broadcast([P, T]), RELU)
+
+        for e in range(E):
+            lo, hi = e * C, (e + 1) * C
+            for s in range(NP):
+                nc.vector.tensor_copy(gdw[:, s, lo:hi], dyw[s][:].bitcast(U32).indirect(entries(lo, hi)))
+            xt = psum.tile([P, HALVES, 2, P], F32, name="xt")
+            for h in range(HALVES):
+                c = e * HALVES + h
+                cols = slice(c * P, (c + 1) * P)
+                a_ps = psum.tile([P, H], F32, name="a_ps")
+                nc.tensor.matmul_mx(out=a_ps[:], lhsT=gxw[:, cols].bitcast(FP8X4), lhsT_scale=gxs[:, cols],
+                                    rhs=w1w[:, e, :].bitcast(FP4X4), rhs_scale=w1s[:, e, :], start=True, stop=True)
+                nc.scalar.activation(relu2[:, c, :], a_ps[:], RELU, scale=2.0)
+                dh_ps = psum.tile([P, H], F32, name="dh_ps")
+                for s in range(NP):
+                    nc.tensor.matmul_mx(out=dh_ps[:], lhsT=gdw[:, s, cols].bitcast(FP8X4), lhsT_scale=gds[s][:, cols],
+                                        rhs=w2w[:, e * NP + s, :].bitcast(FP4X4), rhs_scale=w2s[:, e * NP + s, :],
+                                        start=(s == 0), stop=(s == NP - 1))
+                nc.vector.scalar_tensor_tensor(da[:, c, :], dh_ps[:], gcol[:, c : c + 1], relu2[:, c, :], MULT, MULT)
+                pairs = da[:, c, :].bitcast(F32)
+                for u in range(2):
+                    nc.tensor.transpose(xt[:, h, u, :], pairs[:, u : H // 2 : 2], ident[:])
+            nc.scalar.copy(grouped[:, lo:hi, :].bitcast(F32).rearrange("p (h j) u -> p h j u", h=HALVES),
+                           xt[:].rearrange("p h u j -> p h j u"))
+            nc.vector.quantize_mx(out=daw[:, lo:hi].bitcast(FP8X4), scales=das[:, lo:hi],
+                                  in_=grouped[:, lo:hi, :].rearrange("p j t -> p (j t)"))
+            for kp in range(KB // 2):
+                dx_ps = psum.tile([P, 2, C], F32, name="dx_ps")
+                for v in range(2):
+                    kb = 2 * kp + v
+                    nc.tensor.matmul_mx(out=dx_ps[:, v, :], lhsT=w3w[:, e, 2 * P * kb : 2 * P * (kb + 1)].bitcast(FP4X4),
+                                        lhsT_scale=w3s[:, e, P * kb : P * (kb + 1)],
+                                        rhs=daw[:, lo:hi].bitcast(FP8X4), rhs_scale=das[:, lo:hi], start=True, stop=True)
+                nc.scalar.copy(dxs[:, 2 * kp : 2 * kp + 2, lo:hi], dx_ps[:])
+
+        def scatter(kb, lo, hi):
+            nc.vector.tensor_copy(win[kb][:].indirect(entries(lo, hi)), dxs[:, kb, lo:hi])
+
+        def store(kb):
+            nc.sync.dma_start(out=out[kb * P : (kb + 1) * P, :], in_=win[kb][:])
+
+        for e in range(E):
+            for kb in range(2):
+                scatter(kb, e * C, (e + 1) * C)
+        store(0)
+        store(1)
+        for kb in range(2, KB):
+            scatter(kb, 0, S)
+            store(kb)

@@ -22,6 +22,7 @@ P = 128
 NP = N // 512
 HALVES = C // P
 KB = K // P
+LAST = E - 1
 
 
 def tile_moe_rec_mlp_relu2_kernel(
@@ -31,6 +32,7 @@ def tile_moe_rec_mlp_relu2_kernel(
     nc = tc.nc
     with ExitStack() as ctx:
         keep = ctx.enter_context(tc.tile_pool(name="keep", bufs=1))
+        ring = ctx.enter_context(tc.tile_pool(name="ring", bufs=2))
         psum = ctx.enter_context(tc.psum_pool(name="psum", bufs=2))
 
         offsets = keep.tile([P, S // 16], U16, name="offsets")
@@ -38,68 +40,57 @@ def tile_moe_rec_mlp_relu2_kernel(
         xs = keep.tile([P, T], U8, name="xs", align_bytes=64)
         dyw = [keep.tile([P, T], I32, name="dyw%d" % s, align_bytes=64) for s in range(NP)]
         dys = keep.tile([P, T], U8, name="dys", align_bytes=64)
+        w1w = keep.tile([P, E, 2 * H], U8, name="w1w", align_bytes=64)
         w1s = keep.tile([P, E, H], U8, name="w1s", align_bytes=64)
+        w2w = keep.tile([P, E * NP, 2 * H], U8, name="w2w", align_bytes=64)
         w2s = keep.tile([P, E * NP, H], U8, name="w2s", align_bytes=64)
+        w3w = keep.tile([P, E, 2 * K], U8, name="w3w", align_bytes=64)
         w3s = keep.tile([P, E, K], U8, name="w3s", align_bytes=64)
         gcol = keep.tile([P, S // P], F32, name="gcol")
         ident = keep.tile([P, P], F32, name="ident")
-        win = [keep.tile([P, T], F32, name="win%d" % kb, align_bytes=64) for kb in range(KB)]
-
-        gxw = keep.tile([P, S], U32, name="gxw", align_bytes=64)
-        gxs = keep.tile([P, S], U8, name="gxs", align_bytes=64)
-        gdw = keep.tile([P, NP, S], U32, name="gdw", align_bytes=64)
-        gds = [keep.tile([P, S], U8, name="gds%d" % s, align_bytes=64) for s in range(NP)]
         zero = keep.tile([P, 8], F32, name="zero")
-        relu2 = keep.tile([P, S // P, H], F32, name="relu2", align_bytes=64)
-        da = keep.tile([P, S // P, H], BF16, name="da", align_bytes=64)
-        grouped = keep.tile([P, S, 4], BF16, name="grouped", align_bytes=64)
+        win = [keep.tile([P, T], F32, name="win%d" % kb, align_bytes=64) for kb in range(KB)]
+        gds = [keep.tile([P, S], U8, name="gds%d" % s, align_bytes=64) for s in range(NP)]
         daw = keep.tile([P, S], U32, name="daw", align_bytes=64)
         das = keep.tile([P, S], U8, name="das", align_bytes=64)
-        dxs = keep.tile([P, KB, S], F32, name="dxs", align_bytes=64)
+        grouped = keep.tile([P, S, 4], BF16, name="grouped", align_bytes=64)
 
-        def load_scales(plane, rows, queue=nc.sync):
+        def load_scales(plane, rows, queue):
             for q in range(4):
                 queue.dma_start(out=plane[32 * q : 32 * q + 4].bitcast(I32), in_=rows[4 * q : 4 * q + 4].bitcast(I32))
-
-        w1w = keep.tile([P, E, 2 * H], U8, name="w1w", align_bytes=64)
-        w2w = keep.tile([P, E * NP, 2 * H], U8, name="w2w", align_bytes=64)
-        w3w = keep.tile([P, E, 2 * K], U8, name="w3w", align_bytes=64)
 
         def entries(a, b):
             return offsets[:, a // 16 : b // 16]
 
-        nc.gpsimd.memset(w1s[:].bitcast(I32), 0)
-        nc.vector.memset(dys[:].bitcast(I32), 0)
-        nc.vector.memset(xs[:].bitcast(I32), 0)
+        nc.gpsimd.memset(dys[:].bitcast(I32), 0)
+        nc.gpsimd.memset(xs[:].bitcast(I32), 0)
         nc.vector.memset(zero[:], 0.0)
+        nc.vector.memset(gds[1][:].bitcast(I32), 0)
         nc.vector.memset(w2s[:].bitcast(I32), 0)
         nc.vector.memset(w3s[:].bitcast(I32), 0)
-        nc.vector.memset(gds[1][:].bitcast(I32), 0)
-
+        nc.gpsimd.memset(w1s[:].bitcast(I32), 0)
         load_scales(w1s, w1_scales.rearrange("e s b n -> b (e s) n"), nc.gpsimd)
         make_identity(nc, ident[:])
-        load_scales(w3s, w1t_scales.rearrange("e s b n -> b (e s) n"), nc.gpsimd)
 
         nc.sync.dma_start(offsets[:], offs)
-        nc.sync.dma_start(out=xw[:], in_=x_words[0].rearrange("p t d -> p (t d)").bitcast(I32))
         for q in range(4):
             nc.sync.dma_start(out=dys[32 * q : 32 * q + 4 * NP, :].bitcast(I32), in_=dy_scales[:, 4 * q : 4 * q + 4, :].bitcast(I32))
-        load_scales(xs, x_scales[0])
+        load_scales(xs, x_scales[0], nc.sync)
+        nc.sync.dma_start(out=xw[:], in_=x_words[0].rearrange("p t d -> p (t d)").bitcast(I32))
         for s in range(NP):
             nc.sync.dma_start(out=dyw[s][:], in_=dy_words[s].rearrange("p t d -> p (t d)").bitcast(I32))
-        nc.sync.dma_start(out=w1w[:].bitcast(I32), in_=w1_words.rearrange("e s p n -> p (e s) n").bitcast(I32))
-        load_scales(w2s, w2t_scales.rearrange("e s b n -> b (e s) n"))
-        w2_rows = w2t_words.rearrange("e s p n -> p (e s) n").bitcast(I32)
-        nc.sync.dma_start(out=w2w[:, :NP, :].bitcast(I32), in_=w2_rows[:, :NP, :])
 
-        nc.vector.tensor_copy(gxw[:], xw[:].bitcast(U32).indirect(offsets[:]))
         nc.vector.tensor_copy(gds[0][:], dys[:].indirect(offsets[:]))
-        nc.vector.tensor_copy(gxs[:], xs[:].indirect(offsets[:]))
         nc.sync.dma_start(out=gds[1][0:100, :].bitcast(I32), in_=gds[0][4:104, :].bitcast(I32))
 
+        nc.sync.dma_start(out=w1w[:].bitcast(I32), in_=w1_words.rearrange("e s p n -> p (e s) n").bitcast(I32))
+        load_scales(w2s, w2t_scales.rearrange("e s b n -> b (e s) n"), nc.sync)
+        w2_rows = w2t_words.rearrange("e s p n -> p (e s) n").bitcast(I32)
+        nc.sync.dma_start(out=w2w[:, :NP, :].bitcast(I32), in_=w2_rows[:, :NP, :])
         with nc.allow_non_contiguous_dma(reason="one gate value a slot"):
             nc.sync.dma_start(out=gcol[:], in_=gate[0].rearrange("(c p) -> p c", p=P))
         nc.sync.dma_start(out=w2w[:, NP:, :].bitcast(I32), in_=w2_rows[:, NP:, :])
+        load_scales(w3s, w1t_scales.rearrange("e s b n -> b (e s) n"), nc.sync)
         nc.sync.dma_start(out=w3w[:].bitcast(I32), in_=w1t_words.rearrange("e s p n -> p (e s) n").bitcast(I32))
 
         for kb in range(KB):
@@ -107,49 +98,66 @@ def tile_moe_rec_mlp_relu2_kernel(
 
         for e in range(E):
             lo, hi = e * C, (e + 1) * C
+            gxs = ring.tile([P, C], U8, name="gxs", align_bytes=64)
+            gxw = ring.tile([P, C], U32, name="gxw", align_bytes=64)
+            gdw = [ring.tile([P, C], U32, name="gdw%d" % s, align_bytes=64) for s in range(NP)]
+            nc.vector.tensor_copy(gxs[:], xs[:].indirect(entries(lo, hi)))
+            nc.vector.tensor_copy(gxw[:], xw[:].bitcast(U32).indirect(entries(lo, hi)))
             for s in range(NP):
-                nc.vector.tensor_copy(gdw[:, s, lo:hi], dyw[s][:].bitcast(U32).indirect(entries(lo, hi)))
-            xt = psum.tile([P, HALVES, 2, P], F32, name="xt")
+                nc.vector.tensor_copy(gdw[s][:], dyw[s][:].bitcast(U32).indirect(entries(lo, hi)))
+            da = keep.tile([P, HALVES, H], BF16, name="da%d" % e, align_bytes=64)
+            xt = psum.tile([P, HALVES, 2, P], F32, name="xt", bufs=1)
             for h in range(HALVES):
                 c = e * HALVES + h
-                cols = slice(c * P, (c + 1) * P)
+                cols = slice(h * P, (h + 1) * P)
+                slots = slice(c * P, (c + 1) * P)
                 a_ps = psum.tile([P, H], F32, name="a_ps")
                 nc.tensor.matmul_mx(out=a_ps[:], lhsT=gxw[:, cols].bitcast(FP8X4), lhsT_scale=gxs[:, cols],
                                     rhs=w1w[:, e, :].bitcast(FP4X4), rhs_scale=w1s[:, e, :], start=True, stop=True)
-                nc.scalar.activation(relu2[:, c, :], a_ps[:], RELU, scale=2.0)
+                relu2 = keep.tile([P, H], F32, name="relu%d" % c, align_bytes=64)
+                nc.scalar.activation(relu2[:], a_ps[:], RELU, scale=2.0)
                 dh_ps = psum.tile([P, H], F32, name="dh_ps")
                 for s in range(NP):
-                    nc.tensor.matmul_mx(out=dh_ps[:], lhsT=gdw[:, s, cols].bitcast(FP8X4), lhsT_scale=gds[s][:, cols],
+                    nc.tensor.matmul_mx(out=dh_ps[:], lhsT=gdw[s][:, cols].bitcast(FP8X4), lhsT_scale=gds[s][:, slots],
                                         rhs=w2w[:, e * NP + s, :].bitcast(FP4X4), rhs_scale=w2s[:, e * NP + s, :],
                                         start=(s == 0), stop=(s == NP - 1))
-                nc.vector.scalar_tensor_tensor(da[:, c, :], dh_ps[:], gcol[:, c : c + 1], relu2[:, c, :], MULT, MULT)
-                pairs = da[:, c, :].bitcast(F32)
+                nc.vector.scalar_tensor_tensor(da[:, h, :], dh_ps[:], gcol[:, c : c + 1], relu2[:], MULT, MULT)
+                pairs = da[:, h, :].bitcast(F32)
                 for u in range(2):
                     nc.tensor.transpose(xt[:, h, u, :], pairs[:, u : H // 2 : 2], ident[:])
             nc.scalar.copy(grouped[:, lo:hi, :].bitcast(F32).rearrange("p (h j) u -> p h j u", h=HALVES),
                            xt[:].rearrange("p h u j -> p h j u"))
             nc.vector.quantize_mx(out=daw[:, lo:hi].bitcast(FP8X4), scales=das[:, lo:hi],
                                   in_=grouped[:, lo:hi, :].rearrange("p j t -> p (j t)"))
+
+        first = keep.tile([P, C], F32, name="first", tag="relu%d" % (LAST * HALVES), align_bytes=64)
+        middle = keep.tile([P, 3, C], F32, name="middle", tag="da%d" % LAST, align_bytes=64)
+        final = keep.tile([P, 2, C], F32, name="final", align_bytes=64)
+        whole = keep.tile([P, 2, S], F32, name="whole", align_bytes=64)
+        for e in range(E):
+            lo, hi = e * C, (e + 1) * C
             for kp in range(KB // 2):
-                dx_ps = psum.tile([P, 2, C], F32, name="dx_ps")
+                dx_ps = psum.tile([P, 2, C], F32, name="dx_ps", bufs=3)
                 for v in range(2):
                     kb = 2 * kp + v
                     nc.tensor.matmul_mx(out=dx_ps[:, v, :], lhsT=w3w[:, e, 2 * P * kb : 2 * P * (kb + 1)].bitcast(FP4X4),
                                         lhsT_scale=w3s[:, e, P * kb : P * (kb + 1)],
                                         rhs=daw[:, lo:hi].bitcast(FP8X4), rhs_scale=das[:, lo:hi], start=True, stop=True)
-                nc.scalar.copy(dxs[:, 2 * kp : 2 * kp + 2, lo:hi], dx_ps[:])
+                if kp == 1:
+                    nc.scalar.copy(whole[:, :, lo:hi], dx_ps[:])
+                elif e == 0:
+                    nc.scalar.copy(first[:], dx_ps[:, 0, :])
+                    nc.scalar.copy(middle[:, 0, :], dx_ps[:, 1, :])
+                elif e == 1:
+                    nc.scalar.copy(middle[:, 1:, :], dx_ps[:])
+                else:
+                    nc.scalar.copy(final[:], dx_ps[:])
 
-        def scatter(kb, lo, hi):
-            nc.vector.tensor_copy(win[kb][:].indirect(entries(lo, hi)), dxs[:, kb, lo:hi])
-
-        def store(kb):
+        pieces = [first[:], middle[:, 0, :], middle[:, 1, :], middle[:, 2, :], final[:, 0, :], final[:, 1, :]]
+        for n, piece in enumerate(pieces):
+            e, kb = divmod(n, 2)
+            nc.vector.tensor_copy(win[kb][:].indirect(entries(e * C, (e + 1) * C)), piece)
+        for kb in range(KB):
+            if kb >= 2:
+                nc.vector.tensor_copy(win[kb][:].indirect(offsets[:]), whole[:, kb - 2, :])
             nc.sync.dma_start(out=out[kb * P : (kb + 1) * P, :], in_=win[kb][:])
-
-        for e in range(E):
-            for kb in range(2):
-                scatter(kb, e * C, (e + 1) * C)
-        store(0)
-        store(1)
-        for kb in range(2, KB):
-            scatter(kb, 0, S)
-            store(kb)

@@ -32,7 +32,6 @@ def tile_moe_rec_mlp_relu2_kernel(
     nc = tc.nc
     with ExitStack() as ctx:
         keep = ctx.enter_context(tc.tile_pool(name="keep", bufs=1))
-        ring = ctx.enter_context(tc.tile_pool(name="ring", bufs=2))
         psum = ctx.enter_context(tc.psum_pool(name="psum", bufs=2))
 
         offsets = keep.tile([P, S // 16], U16, name="offsets")
@@ -62,61 +61,66 @@ def tile_moe_rec_mlp_relu2_kernel(
         def entries(a, b):
             return offsets[:, a // 16 : b // 16]
 
-        nc.gpsimd.memset(dys[:].bitcast(I32), 0)
         nc.gpsimd.memset(xs[:].bitcast(I32), 0)
+        nc.gpsimd.memset(dys[:].bitcast(I32), 0)
         nc.vector.memset(zero[:], 0.0)
+        nc.vector.memset(w1s[:].bitcast(I32), 0)
         nc.vector.memset(gds[1][:].bitcast(I32), 0)
         nc.vector.memset(w2s[:].bitcast(I32), 0)
         nc.vector.memset(w3s[:].bitcast(I32), 0)
-        nc.gpsimd.memset(w1s[:].bitcast(I32), 0)
-        load_scales(w1s, w1_scales.rearrange("e s b n -> b (e s) n"), nc.gpsimd)
+
+        w2_rows = w2t_words.rearrange("e s p n -> p (e s) n").bitcast(I32)
+        nc.gpsimd.dma_start(out=w1w[:].bitcast(I32), in_=w1_words.rearrange("e s p n -> p (e s) n").bitcast(I32))
+        nc.gpsimd.dma_start(out=w2w[:, :NP, :].bitcast(I32), in_=w2_rows[:, :NP, :])
         make_identity(nc, ident[:])
 
         nc.sync.dma_start(offsets[:], offs)
+        load_scales(xs, x_scales[0], nc.sync)
         for q in range(4):
             nc.sync.dma_start(out=dys[32 * q : 32 * q + 4 * NP, :].bitcast(I32), in_=dy_scales[:, 4 * q : 4 * q + 4, :].bitcast(I32))
-        load_scales(xs, x_scales[0], nc.sync)
+        load_scales(w1s, w1_scales.rearrange("e s b n -> b (e s) n"), nc.sync)
         nc.sync.dma_start(out=xw[:], in_=x_words[0].rearrange("p t d -> p (t d)").bitcast(I32))
         for s in range(NP):
             nc.sync.dma_start(out=dyw[s][:], in_=dy_words[s].rearrange("p t d -> p (t d)").bitcast(I32))
 
+        load_scales(w2s, w2t_scales.rearrange("e s b n -> b (e s) n"), nc.sync)
+
+        gxs = keep.tile([P, S], U8, name="gxs", align_bytes=64)
+        nc.vector.tensor_copy(gxs[:], xs[:].indirect(offsets[:]))
         nc.vector.tensor_copy(gds[0][:], dys[:].indirect(offsets[:]))
         nc.sync.dma_start(out=gds[1][0:100, :].bitcast(I32), in_=gds[0][4:104, :].bitcast(I32))
 
-        nc.sync.dma_start(out=w1w[:].bitcast(I32), in_=w1_words.rearrange("e s p n -> p (e s) n").bitcast(I32))
-        load_scales(w2s, w2t_scales.rearrange("e s b n -> b (e s) n"), nc.sync)
-        w2_rows = w2t_words.rearrange("e s p n -> p (e s) n").bitcast(I32)
-        nc.sync.dma_start(out=w2w[:, :NP, :].bitcast(I32), in_=w2_rows[:, :NP, :])
         with nc.allow_non_contiguous_dma(reason="one gate value a slot"):
             nc.sync.dma_start(out=gcol[:], in_=gate[0].rearrange("(c p) -> p c", p=P))
         nc.sync.dma_start(out=w2w[:, NP:, :].bitcast(I32), in_=w2_rows[:, NP:, :])
-        load_scales(w3s, w1t_scales.rearrange("e s b n -> b (e s) n"), nc.sync)
         nc.sync.dma_start(out=w3w[:].bitcast(I32), in_=w1t_words.rearrange("e s p n -> p (e s) n").bitcast(I32))
+        load_scales(w3s, w1t_scales.rearrange("e s b n -> b (e s) n"), nc.sync)
 
         for kb in range(KB):
             nc.scalar.activation(win[kb][:], zero[:, 0:1].to_broadcast([P, T]), RELU)
 
         for e in range(E):
             lo, hi = e * C, (e + 1) * C
-            gxs = ring.tile([P, C], U8, name="gxs", align_bytes=64)
-            gxw = ring.tile([P, C], U32, name="gxw", align_bytes=64)
-            gdw = [ring.tile([P, C], U32, name="gdw%d" % s, align_bytes=64) for s in range(NP)]
-            nc.vector.tensor_copy(gxs[:], xs[:].indirect(entries(lo, hi)))
-            nc.vector.tensor_copy(gxw[:], xw[:].bitcast(U32).indirect(entries(lo, hi)))
-            for s in range(NP):
-                nc.vector.tensor_copy(gdw[s][:], dyw[s][:].bitcast(U32).indirect(entries(lo, hi)))
+            if e in (0, LAST):
+                base, end = (0, LAST * C) if e == 0 else (lo, hi)
+                gxw = keep.tile([P, end - base], U32, name="gxw", align_bytes=64)
+                gdw = [keep.tile([P, end - base], U32, name="gdw%d_%d" % (e, s), align_bytes=64,
+                                 tag="gdw%d" % s if e == 0 else "relu%d" % s) for s in range(NP)]
+                nc.vector.tensor_copy(gxw[:], xw[:].bitcast(U32).indirect(entries(base, end)))
+                nc.vector.tensor_copy(gdw[0][:], dyw[0][:].bitcast(U32).indirect(entries(base, end)))
+            nc.vector.tensor_copy(gdw[1][:, lo - base : hi - base], dyw[1][:].bitcast(U32).indirect(entries(lo, hi)))
             da = keep.tile([P, HALVES, H], BF16, name="da%d" % e, align_bytes=64)
             xt = psum.tile([P, HALVES, 2, P], F32, name="xt", bufs=1)
             for h in range(HALVES):
                 c = e * HALVES + h
-                cols = slice(h * P, (h + 1) * P)
+                cols = slice(c * P - base, (c + 1) * P - base)
                 slots = slice(c * P, (c + 1) * P)
-                a_ps = psum.tile([P, H], F32, name="a_ps")
-                nc.tensor.matmul_mx(out=a_ps[:], lhsT=gxw[:, cols].bitcast(FP8X4), lhsT_scale=gxs[:, cols],
+                a_ps = psum.tile([P, H], F32, name="a_ps", tag="a_dx", bufs=3)
+                nc.tensor.matmul_mx(out=a_ps[:], lhsT=gxw[:, cols].bitcast(FP8X4), lhsT_scale=gxs[:, slots],
                                     rhs=w1w[:, e, :].bitcast(FP4X4), rhs_scale=w1s[:, e, :], start=True, stop=True)
                 relu2 = keep.tile([P, H], F32, name="relu%d" % c, align_bytes=64)
                 nc.scalar.activation(relu2[:], a_ps[:], RELU, scale=2.0)
-                dh_ps = psum.tile([P, H], F32, name="dh_ps")
+                dh_ps = psum.tile([P, H], F32, name="dh_ps", bufs=4)
                 for s in range(NP):
                     nc.tensor.matmul_mx(out=dh_ps[:], lhsT=gdw[s][:, cols].bitcast(FP8X4), lhsT_scale=gds[s][:, slots],
                                         rhs=w2w[:, e * NP + s, :].bitcast(FP4X4), rhs_scale=w2s[:, e * NP + s, :],
@@ -137,7 +141,7 @@ def tile_moe_rec_mlp_relu2_kernel(
         for e in range(E):
             lo, hi = e * C, (e + 1) * C
             for kp in range(KB // 2):
-                dx_ps = psum.tile([P, 2, C], F32, name="dx_ps", bufs=3)
+                dx_ps = psum.tile([P, 2, C], F32, name="dx_ps", tag="a_dx", bufs=3)
                 for v in range(2):
                     kb = 2 * kp + v
                     nc.tensor.matmul_mx(out=dx_ps[:, v, :], lhsT=w3w[:, e, 2 * P * kb : 2 * P * (kb + 1)].bitcast(FP4X4),

@@ -69,10 +69,12 @@ def tile_moe_rec_mlp_relu2_kernel(
         nc.vector.memset(w2s[:].bitcast(I32), 0)
         nc.vector.memset(w3s[:].bitcast(I32), 0)
 
+        make_identity(nc, ident[:])
         w2_rows = w2t_words.rearrange("e s p n -> p (e s) n").bitcast(I32)
         nc.gpsimd.dma_start(out=w1w[:].bitcast(I32), in_=w1_words.rearrange("e s p n -> p (e s) n").bitcast(I32))
         nc.gpsimd.dma_start(out=w2w[:, :NP, :].bitcast(I32), in_=w2_rows[:, :NP, :])
-        make_identity(nc, ident[:])
+        with nc.allow_non_contiguous_dma(reason="one gate value a slot"):
+            nc.gpsimd.dma_start(out=gcol[:], in_=gate[0].rearrange("(c p) -> p c", p=P))
 
         nc.sync.dma_start(offsets[:], offs)
         load_scales(xs, x_scales[0], nc.sync)
@@ -90,8 +92,6 @@ def tile_moe_rec_mlp_relu2_kernel(
         nc.vector.tensor_copy(gds[0][:], dys[:].indirect(offsets[:]))
         nc.sync.dma_start(out=gds[1][0:100, :].bitcast(I32), in_=gds[0][4:104, :].bitcast(I32))
 
-        with nc.allow_non_contiguous_dma(reason="one gate value a slot"):
-            nc.sync.dma_start(out=gcol[:], in_=gate[0].rearrange("(c p) -> p c", p=P))
         nc.sync.dma_start(out=w2w[:, NP:, :].bitcast(I32), in_=w2_rows[:, NP:, :])
         nc.sync.dma_start(out=w3w[:].bitcast(I32), in_=w1t_words.rearrange("e s p n -> p (e s) n").bitcast(I32))
         load_scales(w3s, w1t_scales.rearrange("e s b n -> b (e s) n"), nc.sync)

@@ -32,23 +32,27 @@ def tile_moe_rec_mlp_relu2_kernel(
     nc = tc.nc
     with ExitStack() as ctx:
         keep = ctx.enter_context(tc.tile_pool(name="keep", bufs=1))
-        psum = ctx.enter_context(tc.psum_pool(name="psum", bufs=2))
+        psum = ctx.enter_context(tc.psum_pool(name="psum", bufs=1))
 
         offsets = keep.tile([P, S // 16], U16, name="offsets")
         xw = keep.tile([P, T], I32, name="xw", align_bytes=64)
         xs = keep.tile([P, T], U8, name="xs", align_bytes=64)
-        dyw = [keep.tile([P, T], I32, name="dyw%d" % s, align_bytes=64) for s in range(NP)]
+        dyw = keep.tile([P, NP, T], I32, name="dyw", align_bytes=64)
         dys = keep.tile([P, T], U8, name="dys", align_bytes=64)
-        w1w = keep.tile([P, E, 2 * H], U8, name="w1w", align_bytes=64)
+        w1first = keep.tile([P, 2 * H], U8, name="w1first", align_bytes=64)
+        w1rest = keep.tile([P, LAST, 2 * H], U8, name="w1rest", align_bytes=64)
         w1s = keep.tile([P, E, H], U8, name="w1s", align_bytes=64)
-        w2w = keep.tile([P, E * NP, 2 * H], U8, name="w2w", align_bytes=64)
+        w2first = keep.tile([P, NP, 2 * H], U8, name="w2first", align_bytes=64)
+        w2rest = keep.tile([P, LAST * NP, 2 * H], U8, name="w2rest", align_bytes=64)
         w2s = keep.tile([P, E * NP, H], U8, name="w2s", align_bytes=64)
-        w3w = keep.tile([P, E, 2 * K], U8, name="w3w", align_bytes=64)
+        w3first = keep.tile([P, 2 * K], U8, name="w3first", align_bytes=64)
+        w3rest = keep.tile([P, LAST, 2 * K], U8, name="w3rest", align_bytes=64)
         w3s = keep.tile([P, E, K], U8, name="w3s", align_bytes=64)
         gcol = keep.tile([P, S // P], F32, name="gcol")
         ident = keep.tile([P, P], F32, name="ident")
         zero = keep.tile([P, 8], F32, name="zero")
         win = [keep.tile([P, T], F32, name="win%d" % kb, align_bytes=64) for kb in range(KB)]
+        gxsfirst = keep.tile([P, C], U8, name="gxsfirst", align_bytes=64)
         gds = [keep.tile([P, S], U8, name="gds%d" % s, align_bytes=64) for s in range(NP)]
         daw = keep.tile([P, S], U32, name="daw", align_bytes=64)
         das = keep.tile([P, S], U8, name="das", align_bytes=64)
@@ -61,107 +65,114 @@ def tile_moe_rec_mlp_relu2_kernel(
         def entries(a, b):
             return offsets[:, a // 16 : b // 16]
 
-        nc.gpsimd.memset(xs[:].bitcast(I32), 0)
         nc.gpsimd.memset(dys[:].bitcast(I32), 0)
+        nc.gpsimd.memset(xs[:].bitcast(I32), 0)
         nc.vector.memset(zero[:], 0.0)
         nc.vector.memset(w1s[:].bitcast(I32), 0)
         nc.vector.memset(gds[1][:].bitcast(I32), 0)
         nc.vector.memset(w2s[:].bitcast(I32), 0)
         nc.vector.memset(w3s[:].bitcast(I32), 0)
 
-        make_identity(nc, ident[:])
         w2_rows = w2t_words.rearrange("e s p n -> p (e s) n").bitcast(I32)
-        nc.gpsimd.dma_start(out=w1w[:].bitcast(I32), in_=w1_words.rearrange("e s p n -> p (e s) n").bitcast(I32))
-        nc.gpsimd.dma_start(out=w2w[:, :NP, :].bitcast(I32), in_=w2_rows[:, :NP, :])
+        w1_rows = w1_words.rearrange("e s p n -> p (e s) n").bitcast(I32)
+        nc.gpsimd.dma_start(out=w1first[:].bitcast(I32), in_=w1_rows[:, 0, :])
+        nc.gpsimd.dma_start(out=w2first[:].bitcast(I32), in_=w2_rows[:, :NP, :])
+        make_identity(nc, ident[:])
         with nc.allow_non_contiguous_dma(reason="one gate value a slot"):
             nc.gpsimd.dma_start(out=gcol[:], in_=gate[0].rearrange("(c p) -> p c", p=P))
+        w3_rows = w1t_words.rearrange("e s p n -> p (e s) n").bitcast(I32)
+        nc.gpsimd.dma_start(out=w3first[:].bitcast(I32), in_=w3_rows[:, 0, :])
 
         nc.sync.dma_start(offsets[:], offs)
-        load_scales(xs, x_scales[0], nc.sync)
         for q in range(4):
             nc.sync.dma_start(out=dys[32 * q : 32 * q + 4 * NP, :].bitcast(I32), in_=dy_scales[:, 4 * q : 4 * q + 4, :].bitcast(I32))
-        load_scales(w1s, w1_scales.rearrange("e s b n -> b (e s) n"), nc.sync)
         nc.sync.dma_start(out=xw[:], in_=x_words[0].rearrange("p t d -> p (t d)").bitcast(I32))
-        for s in range(NP):
-            nc.sync.dma_start(out=dyw[s][:], in_=dy_words[s].rearrange("p t d -> p (t d)").bitcast(I32))
+        load_scales(xs, x_scales[0], nc.sync)
+        nc.sync.dma_start(out=dyw[:], in_=dy_words.rearrange("s p t d -> p s (t d)").bitcast(I32))
+        load_scales(w1s, w1_scales.rearrange("e s b n -> b (e s) n"), nc.sync)
 
-        load_scales(w2s, w2t_scales.rearrange("e s b n -> b (e s) n"), nc.sync)
-
-        gxs = keep.tile([P, S], U8, name="gxs", align_bytes=64)
-        nc.vector.tensor_copy(gxs[:], xs[:].indirect(offsets[:]))
         nc.vector.tensor_copy(gds[0][:], dys[:].indirect(offsets[:]))
+        nc.vector.tensor_copy(gxsfirst[:], xs[:].indirect(entries(0, C)))
         nc.sync.dma_start(out=gds[1][0:100, :].bitcast(I32), in_=gds[0][4:104, :].bitcast(I32))
-
-        nc.sync.dma_start(out=w2w[:, NP:, :].bitcast(I32), in_=w2_rows[:, NP:, :])
-        nc.sync.dma_start(out=w3w[:].bitcast(I32), in_=w1t_words.rearrange("e s p n -> p (e s) n").bitcast(I32))
+        load_scales(w2s, w2t_scales.rearrange("e s b n -> b (e s) n"), nc.sync)
+        nc.sync.dma_start(out=w1rest[:].bitcast(I32), in_=w1_rows[:, 1:, :])
+        nc.sync.dma_start(out=w2rest[:].bitcast(I32), in_=w2_rows[:, NP:, :])
         load_scales(w3s, w1t_scales.rearrange("e s b n -> b (e s) n"), nc.sync)
+        nc.sync.dma_start(out=w3rest[:].bitcast(I32), in_=w3_rows[:, 1:, :])
 
         for kb in range(KB):
             nc.scalar.activation(win[kb][:], zero[:, 0:1].to_broadcast([P, T]), RELU)
 
-        for e in range(E):
+        gxw = keep.tile([P, S], U32, name="gxw", align_bytes=64)
+        nc.vector.tensor_copy(gxw[:], xw[:].bitcast(U32).indirect(offsets[:]))
+        gxsrest = keep.tile([P, S - C], U8, name="gxsrest", align_bytes=64, tag="w1first")
+        gd_place = [[0, 1], [2, 0], [1, 2]]
+        a_bank = ["A", "B", "A", "B", "C", "D"]
+        dh_bank = ["C", "D", "E", "A", "B", "E"]
+
+        def front(e):
             lo, hi = e * C, (e + 1) * C
-            if e in (0, LAST):
-                base, end = (0, LAST * C) if e == 0 else (lo, hi)
-                gxw = keep.tile([P, end - base], U32, name="gxw", align_bytes=64)
-                gdw = [keep.tile([P, end - base], U32, name="gdw%d_%d" % (e, s), align_bytes=64,
-                                 tag="gdw%d" % s if e == 0 else "relu%d" % s) for s in range(NP)]
-                nc.vector.tensor_copy(gxw[:], xw[:].bitcast(U32).indirect(entries(base, end)))
-                nc.vector.tensor_copy(gdw[0][:], dyw[0][:].bitcast(U32).indirect(entries(base, end)))
-            nc.vector.tensor_copy(gdw[1][:, lo - base : hi - base], dyw[1][:].bitcast(U32).indirect(entries(lo, hi)))
+            gdw = []
+            for s in range(NP):
+                got = keep.tile([P, C], U32, name="gd%d_%d" % (s, e), align_bytes=64, tag="gd%d" % gd_place[e][s])
+                nc.vector.tensor_copy(got[:], dyw[:, s, :].bitcast(U32).indirect(entries(lo, hi)))
+                gdw.append(got)
+            if e == 1:
+                nc.vector.tensor_copy(gxsrest[:], xs[:].indirect(entries(C, S)))
+            w1 = w1first[:] if e == 0 else w1rest[:, e - 1, :]
             da = keep.tile([P, HALVES, H], BF16, name="da%d" % e, align_bytes=64)
-            xt = psum.tile([P, HALVES, 2, P], F32, name="xt", bufs=1)
+            xt = psum.tile([P, HALVES, 2, P], F32, name="xt")
             for h in range(HALVES):
                 c = e * HALVES + h
-                cols = slice(c * P - base, (c + 1) * P - base)
+                cols = slice(h * P, (h + 1) * P)
                 slots = slice(c * P, (c + 1) * P)
-                a_ps = psum.tile([P, H], F32, name="a_ps", tag="a_dx", bufs=3)
-                nc.tensor.matmul_mx(out=a_ps[:], lhsT=gxw[:, cols].bitcast(FP8X4), lhsT_scale=gxs[:, slots],
-                                    rhs=w1w[:, e, :].bitcast(FP4X4), rhs_scale=w1s[:, e, :], start=True, stop=True)
+                a_ps = psum.tile([P, H], F32, name="a_ps", tag=a_bank[c])
+                gxs = gxsfirst[:, cols] if e == 0 else gxsrest[:, c * P - C : (c + 1) * P - C]
+                nc.tensor.matmul_mx(out=a_ps[:], lhsT=gxw[:, slots].bitcast(FP8X4), lhsT_scale=gxs,
+                                    rhs=w1.bitcast(FP4X4), rhs_scale=w1s[:, e, :], start=True, stop=True)
                 relu2 = keep.tile([P, H], F32, name="relu%d" % c, align_bytes=64)
                 nc.scalar.activation(relu2[:], a_ps[:], RELU, scale=2.0)
-                dh_ps = psum.tile([P, H], F32, name="dh_ps", bufs=4)
+                dh_ps = psum.tile([P, H], F32, name="dh_ps", tag=dh_bank[c])
                 for s in range(NP):
+                    w2 = w2first[:, s, :] if e == 0 else w2rest[:, (e - 1) * NP + s, :]
                     nc.tensor.matmul_mx(out=dh_ps[:], lhsT=gdw[s][:, cols].bitcast(FP8X4), lhsT_scale=gds[s][:, slots],
-                                        rhs=w2w[:, e * NP + s, :].bitcast(FP4X4), rhs_scale=w2s[:, e * NP + s, :],
+                                        rhs=w2.bitcast(FP4X4), rhs_scale=w2s[:, e * NP + s, :],
                                         start=(s == 0), stop=(s == NP - 1))
                 nc.vector.scalar_tensor_tensor(da[:, h, :], dh_ps[:], gcol[:, c : c + 1], relu2[:], MULT, MULT)
                 pairs = da[:, h, :].bitcast(F32)
                 for u in range(2):
                     nc.tensor.transpose(xt[:, h, u, :], pairs[:, u : H // 2 : 2], ident[:])
+            return xt
+
+        def pack(e, xt):
+            lo, hi = e * C, (e + 1) * C
             nc.scalar.copy(grouped[:, lo:hi, :].bitcast(F32).rearrange("p (h j) u -> p h j u", h=HALVES),
                            xt[:].rearrange("p h u j -> p h j u"))
             nc.vector.quantize_mx(out=daw[:, lo:hi].bitcast(FP8X4), scales=das[:, lo:hi],
                                   in_=grouped[:, lo:hi, :].rearrange("p j t -> p (j t)"))
 
-        first = keep.tile([P, C], F32, name="first", tag="relu%d" % (LAST * HALVES), align_bytes=64)
-        middle = keep.tile([P, 3, C], F32, name="middle", tag="da%d" % LAST, align_bytes=64)
-        final = keep.tile([P, 2, C], F32, name="final", align_bytes=64)
-        whole = keep.tile([P, 2, S], F32, name="whole", align_bytes=64)
-        for e in range(E):
+        def back(e, kp):
             lo, hi = e * C, (e + 1) * C
-            for kp in range(KB // 2):
-                dx_ps = psum.tile([P, 2, C], F32, name="dx_ps", tag="a_dx", bufs=3)
-                for v in range(2):
-                    kb = 2 * kp + v
-                    nc.tensor.matmul_mx(out=dx_ps[:, v, :], lhsT=w3w[:, e, 2 * P * kb : 2 * P * (kb + 1)].bitcast(FP4X4),
-                                        lhsT_scale=w3s[:, e, P * kb : P * (kb + 1)],
-                                        rhs=daw[:, lo:hi].bitcast(FP8X4), rhs_scale=das[:, lo:hi], start=True, stop=True)
-                if kp == 1:
-                    nc.scalar.copy(whole[:, :, lo:hi], dx_ps[:])
-                elif e == 0:
-                    nc.scalar.copy(first[:], dx_ps[:, 0, :])
-                    nc.scalar.copy(middle[:, 0, :], dx_ps[:, 1, :])
-                elif e == 1:
-                    nc.scalar.copy(middle[:, 1:, :], dx_ps[:])
-                else:
-                    nc.scalar.copy(final[:], dx_ps[:])
+            w3 = w3first[:] if e == 0 else w3rest[:, e - 1, :]
+            dx_ps = psum.tile([P, 2, C], F32, name="dx_ps", tag="dx%d" % kp)
+            for v in range(2):
+                kb = 2 * kp + v
+                nc.tensor.matmul_mx(out=dx_ps[:, v, :], lhsT=w3[:, 2 * P * kb : 2 * P * (kb + 1)].bitcast(FP4X4),
+                                    lhsT_scale=w3s[:, e, P * kb : P * (kb + 1)],
+                                    rhs=daw[:, lo:hi].bitcast(FP8X4), rhs_scale=das[:, lo:hi], start=True, stop=True)
+            dx = keep.tile([P, 2, C], F32, name="dx%d_%d" % (e, kp), align_bytes=64,
+                           tag="da%d" % (e + 1) if kp == 1 and e < LAST else "dx%d_%d" % (e, kp))
+            nc.scalar.copy(dx[:], dx_ps[:])
+            for v in range(2):
+                kb = 2 * kp + v
+                nc.vector.tensor_copy(win[kb][:].indirect(entries(lo, hi)), dx[:, v, :])
+                if e == LAST:
+                    nc.sync.dma_start(out=out[kb * P : (kb + 1) * P, :], in_=win[kb][:])
 
-        pieces = [first[:], middle[:, 0, :], middle[:, 1, :], middle[:, 2, :], final[:, 0, :], final[:, 1, :]]
-        for n, piece in enumerate(pieces):
-            e, kb = divmod(n, 2)
-            nc.vector.tensor_copy(win[kb][:].indirect(entries(e * C, (e + 1) * C)), piece)
-        for kb in range(KB):
-            if kb >= 2:
-                nc.vector.tensor_copy(win[kb][:].indirect(offsets[:]), whole[:, kb - 2, :])
-            nc.sync.dma_start(out=out[kb * P : (kb + 1) * P, :], in_=win[kb][:])
+        pack(0, front(0))
+        for e in range(E):
+            xt = front(e + 1) if e < LAST else None
+            back(e, 0)
+            if e < LAST:
+                pack(e + 1, xt)
+            back(e, 1)

@@ -48,6 +48,7 @@ def tile_moe_rec_mlp_relu2_kernel(
         w3first = keep.tile([P, 2 * K], U8, name="w3first", align_bytes=64)
         w3rest = keep.tile([P, LAST, 2 * K], U8, name="w3rest", align_bytes=64)
         w3s = keep.tile([P, E, K], U8, name="w3s", align_bytes=64)
+        grows = keep.tile([P, P], F32, name="grows")
         gcol = keep.tile([P, S // P], F32, name="gcol")
         ident = keep.tile([P, P], F32, name="ident")
         zero = keep.tile([P, 8], F32, name="zero")
@@ -59,8 +60,8 @@ def tile_moe_rec_mlp_relu2_kernel(
         grouped = keep.tile([P, S, 4], BF16, name="grouped", align_bytes=64)
 
         def load_scales(plane, rows, queue):
-            for q in range(4):
-                queue.dma_start(out=plane[32 * q : 32 * q + 4].bitcast(I32), in_=rows[4 * q : 4 * q + 4].bitcast(I32))
+            for r in range(4):
+                queue.dma_start(out=plane[r:P:32].bitcast(I32), in_=rows[r:16:4].bitcast(I32))
 
         def entries(a, b):
             return offsets[:, a // 16 : b // 16]
@@ -68,6 +69,7 @@ def tile_moe_rec_mlp_relu2_kernel(
         nc.gpsimd.memset(dys[:].bitcast(I32), 0)
         nc.gpsimd.memset(xs[:].bitcast(I32), 0)
         nc.vector.memset(zero[:], 0.0)
+        nc.vector.memset(grows[:], 0.0)
         nc.vector.memset(w1s[:].bitcast(I32), 0)
         nc.vector.memset(gds[1][:].bitcast(I32), 0)
         nc.vector.memset(w2s[:].bitcast(I32), 0)
@@ -76,10 +78,12 @@ def tile_moe_rec_mlp_relu2_kernel(
         w2_rows = w2t_words.rearrange("e s p n -> p (e s) n").bitcast(I32)
         w1_rows = w1_words.rearrange("e s p n -> p (e s) n").bitcast(I32)
         nc.gpsimd.dma_start(out=w1first[:].bitcast(I32), in_=w1_rows[:, 0, :])
-        nc.gpsimd.dma_start(out=w2first[:].bitcast(I32), in_=w2_rows[:, :NP, :])
+        nc.gpsimd.dma_start(out=grows[: S // P, :], in_=gate[0].rearrange("(c p) -> c p", p=P))
         make_identity(nc, ident[:])
-        with nc.allow_non_contiguous_dma(reason="one gate value a slot"):
-            nc.gpsimd.dma_start(out=gcol[:], in_=gate[0].rearrange("(c p) -> p c", p=P))
+        nc.gpsimd.dma_start(out=w2first[:].bitcast(I32), in_=w2_rows[:, :NP, :])
+        gt = psum.tile([P, P], F32, name="gt", tag="xt")
+        nc.tensor.transpose(gt[:], grows[:], ident[:])
+        nc.scalar.copy(gcol[:], gt[:, : S // P])
         w3_rows = w1t_words.rearrange("e s p n -> p (e s) n").bitcast(I32)
         nc.gpsimd.dma_start(out=w3first[:].bitcast(I32), in_=w3_rows[:, 0, :])
 

@@ -77,15 +77,8 @@ def tile_moe_rec_mlp_relu2_kernel(
 
         w2_rows = w2t_words.rearrange("e s p n -> p (e s) n").bitcast(I32)
         w1_rows = w1_words.rearrange("e s p n -> p (e s) n").bitcast(I32)
-        nc.gpsimd.dma_start(out=w1first[:].bitcast(I32), in_=w1_rows[:, 0, :])
-        nc.gpsimd.dma_start(out=grows[: S // P, :], in_=gate[0].rearrange("(c p) -> c p", p=P))
         make_identity(nc, ident[:])
-        nc.gpsimd.dma_start(out=w2first[:].bitcast(I32), in_=w2_rows[:, :NP, :])
-        gt = psum.tile([P, P], F32, name="gt", tag="xt")
-        nc.tensor.transpose(gt[:], grows[:], ident[:])
-        nc.scalar.copy(gcol[:], gt[:, : S // P])
         w3_rows = w1t_words.rearrange("e s p n -> p (e s) n").bitcast(I32)
-        nc.gpsimd.dma_start(out=w3first[:].bitcast(I32), in_=w3_rows[:, 0, :])
 
         nc.sync.dma_start(offsets[:], offs)
         for q in range(4):
@@ -93,16 +86,23 @@ def tile_moe_rec_mlp_relu2_kernel(
         nc.sync.dma_start(out=xw[:], in_=x_words[0].rearrange("p t d -> p (t d)").bitcast(I32))
         load_scales(xs, x_scales[0], nc.sync)
         nc.sync.dma_start(out=dyw[:], in_=dy_words.rearrange("s p t d -> p s (t d)").bitcast(I32))
+        nc.sync.dma_start(out=w1first[:].bitcast(I32), in_=w1_rows[:, 0, :])
         load_scales(w1s, w1_scales.rearrange("e s b n -> b (e s) n"), nc.sync)
-
-        nc.vector.tensor_copy(gds[0][:], dys[:].indirect(offsets[:]))
-        nc.vector.tensor_copy(gxsfirst[:], xs[:].indirect(entries(0, C)))
-        nc.sync.dma_start(out=gds[1][0:100, :].bitcast(I32), in_=gds[0][4:104, :].bitcast(I32))
+        nc.sync.dma_start(out=grows[: S // P, :], in_=gate[0].rearrange("(c p) -> c p", p=P))
+        gt = psum.tile([P, P], F32, name="gt", tag="xt")
+        nc.tensor.transpose(gt[:], grows[:], ident[:])
+        nc.scalar.copy(gcol[:], gt[:, : S // P])
+        nc.sync.dma_start(out=w2first[:].bitcast(I32), in_=w2_rows[:, :NP, :])
         load_scales(w2s, w2t_scales.rearrange("e s b n -> b (e s) n"), nc.sync)
+        nc.vector.tensor_copy(gds[0][:], dys[:].indirect(offsets[:]))
+        nc.sync.dma_start(out=gds[1][0:100, :].bitcast(I32), in_=gds[0][4:104, :].bitcast(I32))
         nc.sync.dma_start(out=w1rest[:].bitcast(I32), in_=w1_rows[:, 1:, :])
-        nc.sync.dma_start(out=w2rest[:].bitcast(I32), in_=w2_rows[:, NP:, :])
         load_scales(w3s, w1t_scales.rearrange("e s b n -> b (e s) n"), nc.sync)
+        nc.sync.dma_start(out=w2rest[:].bitcast(I32), in_=w2_rows[:, NP:, :])
+        nc.sync.dma_start(out=w3first[:].bitcast(I32), in_=w3_rows[:, 0, :])
         nc.sync.dma_start(out=w3rest[:].bitcast(I32), in_=w3_rows[:, 1:, :])
+        nc.vector.tensor_copy(gxsfirst[:], xs[:].indirect(entries(0, C)))
+
 
         for kb in range(KB):
             nc.scalar.activation(win[kb][:], zero[:, 0:1].to_broadcast([P, T]), RELU)

@@ -37,7 +37,7 @@ def tile_moe_rec_mlp_relu2_kernel(
         offsets = keep.tile([P, S // 16], U16, name="offsets")
         xw = keep.tile([P, T], I32, name="xw", align_bytes=64)
         xs = keep.tile([P, T], U8, name="xs", align_bytes=64)
-        dyw = keep.tile([P, NP, T], I32, name="dyw", align_bytes=64)
+        dyw = [keep.tile([P, T], I32, name="dyw%d" % s, align_bytes=64) for s in range(NP)]
         dys = keep.tile([P, T], U8, name="dys", align_bytes=64)
         w1first = keep.tile([P, 2 * H], U8, name="w1first", align_bytes=64)
         w1rest = keep.tile([P, LAST, 2 * H], U8, name="w1rest", align_bytes=64)
@@ -48,7 +48,7 @@ def tile_moe_rec_mlp_relu2_kernel(
         w3first = keep.tile([P, 2 * K], U8, name="w3first", align_bytes=64)
         w3rest = keep.tile([P, LAST, 2 * K], U8, name="w3rest", align_bytes=64)
         w3s = keep.tile([P, E, K], U8, name="w3s", align_bytes=64)
-        grows = keep.tile([P, P], F32, name="grows")
+        grows = keep.tile([P, P], F32, name="grows", align_bytes=64)
         gcol = keep.tile([P, S // P], F32, name="gcol")
         ident = keep.tile([P, P], F32, name="ident")
         zero = keep.tile([P, 8], F32, name="zero")
@@ -57,10 +57,9 @@ def tile_moe_rec_mlp_relu2_kernel(
         gds = [keep.tile([P, S], U8, name="gds%d" % s, align_bytes=64) for s in range(NP)]
         daw = keep.tile([P, S], U32, name="daw", align_bytes=64)
         das = keep.tile([P, S], U8, name="das", align_bytes=64)
-        grouped = keep.tile([P, S, 4], BF16, name="grouped", align_bytes=64)
 
-        def load_scales(plane, rows, queue):
-            for r in range(4):
+        def load_scales(plane, rows, queue, which=range(4)):
+            for r in which:
                 queue.dma_start(out=plane[r:P:32].bitcast(I32), in_=rows[r:16:4].bitcast(I32))
 
         def entries(a, b):
@@ -78,6 +77,8 @@ def tile_moe_rec_mlp_relu2_kernel(
         w2_rows = w2t_words.rearrange("e s p n -> p (e s) n").bitcast(I32)
         w1_rows = w1_words.rearrange("e s p n -> p (e s) n").bitcast(I32)
         make_identity(nc, ident[:])
+        w1_planes = w1_scales.rearrange("e s b n -> b (e s) n")
+        w2_planes = w2t_scales.rearrange("e s b n -> b (e s) n")
         w3_rows = w1t_words.rearrange("e s p n -> p (e s) n").bitcast(I32)
 
         nc.sync.dma_start(offsets[:], offs)
@@ -85,21 +86,24 @@ def tile_moe_rec_mlp_relu2_kernel(
             nc.sync.dma_start(out=dys[32 * q : 32 * q + 4 * NP, :].bitcast(I32), in_=dy_scales[:, 4 * q : 4 * q + 4, :].bitcast(I32))
         nc.sync.dma_start(out=xw[:], in_=x_words[0].rearrange("p t d -> p (t d)").bitcast(I32))
         load_scales(xs, x_scales[0], nc.sync)
-        nc.sync.dma_start(out=dyw[:], in_=dy_words.rearrange("s p t d -> p s (t d)").bitcast(I32))
+        nc.sync.dma_start(out=dyw[0][:], in_=dy_words[0].rearrange("p t d -> p (t d)").bitcast(I32))
         nc.sync.dma_start(out=w1first[:].bitcast(I32), in_=w1_rows[:, 0, :])
-        load_scales(w1s, w1_scales.rearrange("e s b n -> b (e s) n"), nc.sync)
+        load_scales(w1s[:, :1, :], w1_planes[:, :1, :], nc.sync)
+        nc.sync.dma_start(out=dyw[1][:], in_=dy_words[1].rearrange("p t d -> p (t d)").bitcast(I32))
         nc.sync.dma_start(out=grows[: S // P, :], in_=gate[0].rearrange("(c p) -> c p", p=P))
-        gt = psum.tile([P, P], F32, name="gt", tag="xt")
+        gt = psum.tile([P, P], F32, name="gt", tag="X")
         nc.tensor.transpose(gt[:], grows[:], ident[:])
         nc.scalar.copy(gcol[:], gt[:, : S // P])
         nc.sync.dma_start(out=w2first[:].bitcast(I32), in_=w2_rows[:, :NP, :])
-        load_scales(w2s, w2t_scales.rearrange("e s b n -> b (e s) n"), nc.sync)
         nc.vector.tensor_copy(gds[0][:], dys[:].indirect(offsets[:]))
         nc.sync.dma_start(out=gds[1][0:100, :].bitcast(I32), in_=gds[0][4:104, :].bitcast(I32))
-        nc.sync.dma_start(out=w1rest[:].bitcast(I32), in_=w1_rows[:, 1:, :])
-        load_scales(w3s, w1t_scales.rearrange("e s b n -> b (e s) n"), nc.sync)
-        nc.sync.dma_start(out=w2rest[:].bitcast(I32), in_=w2_rows[:, NP:, :])
+        load_scales(w2s[:, :NP, :], w2_planes[:, :NP, :], nc.sync)
         nc.sync.dma_start(out=w3first[:].bitcast(I32), in_=w3_rows[:, 0, :])
+        load_scales(w3s, w1t_scales.rearrange("e s b n -> b (e s) n"), nc.sync)
+        load_scales(w1s[:, 1:, :], w1_planes[:, 1:, :], nc.sync)
+        nc.sync.dma_start(out=w1rest[:].bitcast(I32), in_=w1_rows[:, 1:, :])
+        load_scales(w2s[:, NP:, :], w2_planes[:, NP:, :], nc.sync)
+        nc.sync.dma_start(out=w2rest[:].bitcast(I32), in_=w2_rows[:, NP:, :])
         nc.sync.dma_start(out=w3rest[:].bitcast(I32), in_=w3_rows[:, 1:, :])
         nc.vector.tensor_copy(gxsfirst[:], xs[:].indirect(entries(0, C)))
 
@@ -109,8 +113,8 @@ def tile_moe_rec_mlp_relu2_kernel(
 
         gxw = keep.tile([P, S], U32, name="gxw", align_bytes=64)
         nc.vector.tensor_copy(gxw[:], xw[:].bitcast(U32).indirect(offsets[:]))
-        gxsrest = keep.tile([P, S - C], U8, name="gxsrest", align_bytes=64, tag="w1first")
-        gd_place = [[0, 1], [2, 0], [1, 2]]
+        gxsrest = keep.tile([P, S - C], U8, name="gxsrest", align_bytes=64, tag="grows")
+        gd_place = [["gdA", "gdB"], ["gdC", "gdA"], ["gdB", "grouped0"]]
         a_bank = ["A", "B", "A", "B", "C", "D"]
         dh_bank = ["C", "D", "E", "A", "B", "E"]
 
@@ -118,14 +122,13 @@ def tile_moe_rec_mlp_relu2_kernel(
             lo, hi = e * C, (e + 1) * C
             gdw = []
             for s in range(NP):
-                got = keep.tile([P, C], U32, name="gd%d_%d" % (s, e), align_bytes=64, tag="gd%d" % gd_place[e][s])
-                nc.vector.tensor_copy(got[:], dyw[:, s, :].bitcast(U32).indirect(entries(lo, hi)))
+                got = keep.tile([P, C], U32, name="gd%d_%d" % (s, e), align_bytes=64, tag=gd_place[e][s])
+                nc.vector.tensor_copy(got[:], dyw[s][:].bitcast(U32).indirect(entries(lo, hi)))
                 gdw.append(got)
             if e == 1:
                 nc.vector.tensor_copy(gxsrest[:], xs[:].indirect(entries(C, S)))
             w1 = w1first[:] if e == 0 else w1rest[:, e - 1, :]
             da = keep.tile([P, HALVES, H], BF16, name="da%d" % e, align_bytes=64)
-            xt = psum.tile([P, HALVES, 2, P], F32, name="xt")
             for h in range(HALVES):
                 c = e * HALVES + h
                 cols = slice(h * P, (h + 1) * P)
@@ -143,40 +146,54 @@ def tile_moe_rec_mlp_relu2_kernel(
                                         rhs=w2.bitcast(FP4X4), rhs_scale=w2s[:, e * NP + s, :],
                                         start=(s == 0), stop=(s == NP - 1))
                 nc.vector.scalar_tensor_tensor(da[:, h, :], dh_ps[:], gcol[:, c : c + 1], relu2[:], MULT, MULT)
+            return da
+
+        def pack(da, lo, halves, bank):
+            hi = lo + P * len(halves)
+            xt = psum.tile([P, len(halves), 2, P], F32, name="xt", tag=bank)
+            for n, h in enumerate(halves):
                 pairs = da[:, h, :].bitcast(F32)
                 for u in range(2):
-                    nc.tensor.transpose(xt[:, h, u, :], pairs[:, u : H // 2 : 2], ident[:])
-            return xt
-
-        def pack(e, xt):
-            lo, hi = e * C, (e + 1) * C
-            nc.scalar.copy(grouped[:, lo:hi, :].bitcast(F32).rearrange("p (h j) u -> p h j u", h=HALVES),
+                    nc.tensor.transpose(xt[:, n, u, :], pairs[:, u : H // 2 : 2], ident[:])
+            grouped = keep.tile([P, hi - lo, 4], BF16, name="grouped%d" % lo, align_bytes=64)
+            nc.scalar.copy(grouped[:].bitcast(F32).rearrange("p (h j) u -> p h j u", h=len(halves)),
                            xt[:].rearrange("p h u j -> p h j u"))
             nc.vector.quantize_mx(out=daw[:, lo:hi].bitcast(FP8X4), scales=das[:, lo:hi],
-                                  in_=grouped[:, lo:hi, :].rearrange("p j t -> p (j t)"))
+                                  in_=grouped[:].rearrange("p j t -> p (j t)"))
 
-        def back(e, kp):
-            lo, hi = e * C, (e + 1) * C
+        def back(lo, hi, blocks, bank):
+            e = lo // C
             w3 = w3first[:] if e == 0 else w3rest[:, e - 1, :]
-            dx_ps = psum.tile([P, 2, C], F32, name="dx_ps", tag="dx%d" % kp)
-            for v in range(2):
-                kb = 2 * kp + v
+            dx_ps = psum.tile([P, len(blocks), hi - lo], F32, name="dx_ps", tag=bank)
+            for v, kb in enumerate(blocks):
                 nc.tensor.matmul_mx(out=dx_ps[:, v, :], lhsT=w3[:, 2 * P * kb : 2 * P * (kb + 1)].bitcast(FP4X4),
                                     lhsT_scale=w3s[:, e, P * kb : P * (kb + 1)],
                                     rhs=daw[:, lo:hi].bitcast(FP8X4), rhs_scale=das[:, lo:hi], start=True, stop=True)
-            dx = keep.tile([P, 2, C], F32, name="dx%d_%d" % (e, kp), align_bytes=64,
-                           tag="da%d" % (e + 1) if kp == 1 and e < LAST else "dx%d_%d" % (e, kp))
-            nc.scalar.copy(dx[:], dx_ps[:])
-            for v in range(2):
-                kb = 2 * kp + v
+            return dx_ps
+
+        def scatter(lo, hi, blocks, sums, place):
+            dx = keep.tile([P, len(blocks), hi - lo], F32, name="dx", align_bytes=64, tag=place)
+            nc.scalar.copy(dx[:], sums)
+            for v, kb in enumerate(blocks):
                 nc.vector.tensor_copy(win[kb][:].indirect(entries(lo, hi)), dx[:, v, :])
-                if e == LAST:
+                if hi == S:
                     nc.sync.dma_start(out=out[kb * P : (kb + 1) * P, :], in_=win[kb][:])
 
-        pack(0, front(0))
-        for e in range(E):
-            xt = front(e + 1) if e < LAST else None
-            back(e, 0)
-            if e < LAST:
-                pack(e + 1, xt)
-            back(e, 1)
+        da = front(0)
+        pack(da, 0, [0], "X")
+        pack(da, P, [1], "Z")
+        sums = back(0, P, [0, 1, 2, 3], "Y")
+        scatter(0, P, [0], sums[:, :1, :], "dxA")
+        scatter(0, P, [1, 2, 3], sums[:, 1:, :], "dxB")
+        da = front(1)
+        sums = back(P, C, [0, 1, 2, 3], "X")
+        scatter(P, C, [0], sums[:, :1, :], "dxC")
+        scatter(P, C, [1], sums[:, 1:2, :], "relu2")
+        pack(da, C, [0, 1], "Y")
+        scatter(P, C, [2, 3], sums[:, 2:, :], "da1")
+        da = front(2)
+        scatter(C, 2 * C, [0, 1], back(C, 2 * C, [0, 1], "Z")[:], "dxD")
+        pack(da, 2 * C, [0, 1], "Z")
+        scatter(C, 2 * C, [2, 3], back(C, 2 * C, [2, 3], "X")[:], "da2")
+        scatter(2 * C, S, [0, 1], back(2 * C, S, [0, 1], "Y")[:], "dxE")
+        scatter(2 * C, S, [2, 3], back(2 * C, S, [2, 3], "X")[:], "dxF")

@@ -41,10 +41,10 @@ def tile_moe_rec_mlp_relu2_kernel(
         dys = keep.tile([P, T], U8, name="dys", align_bytes=64)
         w1first = keep.tile([P, 2 * H], U8, name="w1first", align_bytes=64)
         w1rest = keep.tile([P, LAST, 2 * H], U8, name="w1rest", align_bytes=64)
-        w1s = keep.tile([P, E, H], U8, name="w1s", align_bytes=64)
+        w1s = [keep.tile([P, n, H], U8, name="w1s%d" % n, align_bytes=64) for n in (1, LAST)]
         w2first = keep.tile([P, NP, 2 * H], U8, name="w2first", align_bytes=64)
         w2rest = keep.tile([P, LAST * NP, 2 * H], U8, name="w2rest", align_bytes=64)
-        w2s = keep.tile([P, E * NP, H], U8, name="w2s", align_bytes=64)
+        w2s = [keep.tile([P, n * NP, H], U8, name="w2s%d" % n, align_bytes=64) for n in (1, LAST)]
         w3first = keep.tile([P, 2 * K], U8, name="w3first", align_bytes=64)
         w3rest = keep.tile([P, LAST, 2 * K], U8, name="w3rest", align_bytes=64)
         w3s = keep.tile([P, E, K], U8, name="w3s", align_bytes=64)
@@ -69,10 +69,12 @@ def tile_moe_rec_mlp_relu2_kernel(
         nc.gpsimd.memset(xs[:].bitcast(I32), 0)
         nc.vector.memset(zero[:], 0.0)
         nc.vector.memset(grows[:], 0.0)
-        nc.vector.memset(w1s[:].bitcast(I32), 0)
+        nc.vector.memset(w1s[0][:].bitcast(I32), 0)
         nc.vector.memset(gds[1][:].bitcast(I32), 0)
-        nc.vector.memset(w2s[:].bitcast(I32), 0)
+        nc.vector.memset(w2s[0][:].bitcast(I32), 0)
         nc.vector.memset(w3s[:].bitcast(I32), 0)
+        nc.vector.memset(w1s[1][:].bitcast(I32), 0)
+        nc.vector.memset(w2s[1][:].bitcast(I32), 0)
 
         w2_rows = w2t_words.rearrange("e s p n -> p (e s) n").bitcast(I32)
         w1_rows = w1_words.rearrange("e s p n -> p (e s) n").bitcast(I32)
@@ -88,7 +90,7 @@ def tile_moe_rec_mlp_relu2_kernel(
         load_scales(xs, x_scales[0], nc.sync)
         nc.sync.dma_start(out=dyw[0][:], in_=dy_words[0].rearrange("p t d -> p (t d)").bitcast(I32))
         nc.sync.dma_start(out=w1first[:].bitcast(I32), in_=w1_rows[:, 0, :])
-        load_scales(w1s[:, :1, :], w1_planes[:, :1, :], nc.sync)
+        load_scales(w1s[0], w1_planes[:, :1, :], nc.sync)
         nc.sync.dma_start(out=dyw[1][:], in_=dy_words[1].rearrange("p t d -> p (t d)").bitcast(I32))
         nc.sync.dma_start(out=grows[: S // P, :], in_=gate[0].rearrange("(c p) -> c p", p=P))
         gt = psum.tile([P, P], F32, name="gt", tag="X")
@@ -97,12 +99,12 @@ def tile_moe_rec_mlp_relu2_kernel(
         nc.sync.dma_start(out=w2first[:].bitcast(I32), in_=w2_rows[:, :NP, :])
         nc.vector.tensor_copy(gds[0][:], dys[:].indirect(offsets[:]))
         nc.sync.dma_start(out=gds[1][0:100, :].bitcast(I32), in_=gds[0][4:104, :].bitcast(I32))
-        load_scales(w2s[:, :NP, :], w2_planes[:, :NP, :], nc.sync)
+        load_scales(w2s[0], w2_planes[:, :NP, :], nc.sync)
         nc.sync.dma_start(out=w3first[:].bitcast(I32), in_=w3_rows[:, 0, :])
         load_scales(w3s, w1t_scales.rearrange("e s b n -> b (e s) n"), nc.sync)
-        load_scales(w1s[:, 1:, :], w1_planes[:, 1:, :], nc.sync)
+        load_scales(w1s[1], w1_planes[:, 1:, :], nc.sync)
         nc.sync.dma_start(out=w1rest[:].bitcast(I32), in_=w1_rows[:, 1:, :])
-        load_scales(w2s[:, NP:, :], w2_planes[:, NP:, :], nc.sync)
+        load_scales(w2s[1], w2_planes[:, NP:, :], nc.sync)
         nc.sync.dma_start(out=w2rest[:].bitcast(I32), in_=w2_rows[:, NP:, :])
         nc.sync.dma_start(out=w3rest[:].bitcast(I32), in_=w3_rows[:, 1:, :])
         nc.vector.tensor_copy(gxsfirst[:], xs[:].indirect(entries(0, C)))
@@ -136,14 +138,14 @@ def tile_moe_rec_mlp_relu2_kernel(
                 a_ps = psum.tile([P, H], F32, name="a_ps", tag=a_bank[c])
                 gxs = gxsfirst[:, cols] if e == 0 else gxsrest[:, c * P - C : (c + 1) * P - C]
                 nc.tensor.matmul_mx(out=a_ps[:], lhsT=gxw[:, slots].bitcast(FP8X4), lhsT_scale=gxs,
-                                    rhs=w1.bitcast(FP4X4), rhs_scale=w1s[:, e, :], start=True, stop=True)
+                                    rhs=w1.bitcast(FP4X4), rhs_scale=w1s[0][:, 0, :] if e == 0 else w1s[1][:, e - 1, :], start=True, stop=True)
                 relu2 = keep.tile([P, H], F32, name="relu%d" % c, align_bytes=64)
                 nc.scalar.activation(relu2[:], a_ps[:], RELU, scale=2.0)
                 dh_ps = psum.tile([P, H], F32, name="dh_ps", tag=dh_bank[c])
                 for s in range(NP):
                     w2 = w2first[:, s, :] if e == 0 else w2rest[:, (e - 1) * NP + s, :]
                     nc.tensor.matmul_mx(out=dh_ps[:], lhsT=gdw[s][:, cols].bitcast(FP8X4), lhsT_scale=gds[s][:, slots],
-                                        rhs=w2.bitcast(FP4X4), rhs_scale=w2s[:, e * NP + s, :],
+                                        rhs=w2.bitcast(FP4X4), rhs_scale=w2s[0][:, s, :] if e == 0 else w2s[1][:, (e - 1) * NP + s, :],
                                         start=(s == 0), stop=(s == NP - 1))
                 nc.vector.scalar_tensor_tensor(da[:, h, :], dh_ps[:], gcol[:, c : c + 1], relu2[:], MULT, MULT)
             return da

@@ -48,8 +48,8 @@ def tile_moe_rec_mlp_relu2_kernel(
         w3first = keep.tile([P, 2 * K], U8, name="w3first", align_bytes=64)
         w3rest = keep.tile([P, LAST, 2 * K], U8, name="w3rest", align_bytes=64)
         w3s = keep.tile([P, E, K], U8, name="w3s", align_bytes=64)
-        grows = keep.tile([P, P], F32, name="grows", align_bytes=64)
-        gcol = keep.tile([P, S // P], F32, name="gcol")
+        grows = {a: keep.tile([P, P], F32, name="grows%d" % a, align_bytes=64) for a in (0, HALVES)}
+        gcol = {a: keep.tile([P, n], F32, name="gcol%d" % a) for a, n in ((0, HALVES), (HALVES, S // P - HALVES))}
         ident = keep.tile([P, P], F32, name="ident")
         zero = keep.tile([P, 8], F32, name="zero")
         win = [keep.tile([P, T], F32, name="win%d" % kb, align_bytes=64) for kb in range(KB)]
@@ -62,19 +62,23 @@ def tile_moe_rec_mlp_relu2_kernel(
             for r in which:
                 queue.dma_start(out=plane[r:P:32].bitcast(I32), in_=rows[r:16:4].bitcast(I32))
 
+        def load_gate(a, b):
+            nc.sync.dma_start(out=grows[a][a:b, :], in_=gate[0].rearrange("(c p) -> c p", p=P)[a:b])
+
+        def turn_gate(a, b, bank):
+            turned = psum.tile([P, P], F32, name="turned", tag=bank)
+            nc.tensor.transpose(turned[:], grows[a][:], ident[:])
+            nc.scalar.copy(gcol[a][:], turned[:, a:b])
+
         def entries(a, b):
             return offsets[:, a // 16 : b // 16]
 
         nc.gpsimd.memset(dys[:].bitcast(I32), 0)
         nc.gpsimd.memset(xs[:].bitcast(I32), 0)
         nc.vector.memset(zero[:], 0.0)
-        nc.vector.memset(grows[:], 0.0)
-        nc.vector.memset(w1s[0][:].bitcast(I32), 0)
+        for a in (0, HALVES):
+            nc.vector.memset(grows[a][:], 0.0)
         nc.vector.memset(gds[1][:].bitcast(I32), 0)
-        nc.vector.memset(w2s[0][:].bitcast(I32), 0)
-        nc.vector.memset(w3s[:].bitcast(I32), 0)
-        nc.vector.memset(w1s[1][:].bitcast(I32), 0)
-        nc.vector.memset(w2s[1][:].bitcast(I32), 0)
 
         w2_rows = w2t_words.rearrange("e s p n -> p (e s) n").bitcast(I32)
         w1_rows = w1_words.rearrange("e s p n -> p (e s) n").bitcast(I32)
@@ -92,16 +96,15 @@ def tile_moe_rec_mlp_relu2_kernel(
         nc.sync.dma_start(out=w1first[:].bitcast(I32), in_=w1_rows[:, 0, :])
         load_scales(w1s[0], w1_planes[:, :1, :], nc.sync)
         nc.sync.dma_start(out=dyw[1][:], in_=dy_words[1].rearrange("p t d -> p (t d)").bitcast(I32))
-        nc.sync.dma_start(out=grows[: S // P, :], in_=gate[0].rearrange("(c p) -> c p", p=P))
-        gt = psum.tile([P, P], F32, name="gt", tag="X")
-        nc.tensor.transpose(gt[:], grows[:], ident[:])
-        nc.scalar.copy(gcol[:], gt[:, : S // P])
-        nc.sync.dma_start(out=w2first[:].bitcast(I32), in_=w2_rows[:, :NP, :])
         nc.vector.tensor_copy(gds[0][:], dys[:].indirect(offsets[:]))
         nc.sync.dma_start(out=gds[1][0:100, :].bitcast(I32), in_=gds[0][4:104, :].bitcast(I32))
+        load_gate(0, HALVES)
+        turn_gate(0, HALVES, "X")
+        nc.sync.dma_start(out=w2first[:].bitcast(I32), in_=w2_rows[:, :NP, :])
         load_scales(w2s[0], w2_planes[:, :NP, :], nc.sync)
         nc.sync.dma_start(out=w3first[:].bitcast(I32), in_=w3_rows[:, 0, :])
         load_scales(w3s, w1t_scales.rearrange("e s b n -> b (e s) n"), nc.sync)
+        load_gate(HALVES, S // P)
         load_scales(w1s[1], w1_planes[:, 1:, :], nc.sync)
         nc.sync.dma_start(out=w1rest[:].bitcast(I32), in_=w1_rows[:, 1:, :])
         load_scales(w2s[1], w2_planes[:, NP:, :], nc.sync)
@@ -115,7 +118,7 @@ def tile_moe_rec_mlp_relu2_kernel(
 
         gxw = keep.tile([P, S], U32, name="gxw", align_bytes=64)
         nc.vector.tensor_copy(gxw[:], xw[:].bitcast(U32).indirect(offsets[:]))
-        gxsrest = keep.tile([P, S - C], U8, name="gxsrest", align_bytes=64, tag="grows")
+        gxsrest = keep.tile([P, S - C], U8, name="gxsrest", align_bytes=64, tag="grows0")
         gd_place = [["gdA", "gdB"], ["gdC", "gdA"], ["gdB", "grouped0"]]
         a_bank = ["A", "B", "A", "B", "C", "D"]
         dh_bank = ["C", "D", "E", "A", "B", "E"]
@@ -147,7 +150,7 @@ def tile_moe_rec_mlp_relu2_kernel(
                     nc.tensor.matmul_mx(out=dh_ps[:], lhsT=gdw[s][:, cols].bitcast(FP8X4), lhsT_scale=gds[s][:, slots],
                                         rhs=w2.bitcast(FP4X4), rhs_scale=w2s[0][:, s, :] if e == 0 else w2s[1][:, (e - 1) * NP + s, :],
                                         start=(s == 0), stop=(s == NP - 1))
-                nc.vector.scalar_tensor_tensor(da[:, h, :], dh_ps[:], gcol[:, c : c + 1], relu2[:], MULT, MULT)
+                nc.vector.scalar_tensor_tensor(da[:, h, :], dh_ps[:], gcol[0][:, c : c + 1] if e == 0 else gcol[HALVES][:, c - HALVES : c - HALVES + 1], relu2[:], MULT, MULT)
             return da
 
         def pack(da, lo, halves, bank):
@@ -184,9 +187,9 @@ def tile_moe_rec_mlp_relu2_kernel(
         da = front(0)
         pack(da, 0, [0], "X")
         pack(da, P, [1], "Z")
-        sums = back(0, P, [0, 1, 2, 3], "Y")
-        scatter(0, P, [0], sums[:, :1, :], "dxA")
-        scatter(0, P, [1, 2, 3], sums[:, 1:, :], "dxB")
+        turn_gate(HALVES, S // P, "Z")
+        scatter(0, P, [0], back(0, P, [0], "E")[:], "dxA")
+        scatter(0, P, [1, 2, 3], back(0, P, [1, 2, 3], "Y")[:], "dxB")
         da = front(1)
         sums = back(P, C, [0, 1, 2, 3], "X")
         scatter(P, C, [0], sums[:, :1, :], "dxC")

@@ -89,7 +89,7 @@ def tile_moe_rec_mlp_relu2_kernel(
 
         nc.sync.dma_start(offsets[:], offs)
         for q in range(4):
-            nc.sync.dma_start(out=dys[32 * q : 32 * q + 4 * NP, :].bitcast(I32), in_=dy_scales[:, 4 * q : 4 * q + 4, :].bitcast(I32))
+            nc.sync.dma_start(out=dys[q:P:16, :].bitcast(I32), in_=dy_scales.rearrange("s (q r) n -> r q s n", r=4)[q].bitcast(I32))
         nc.sync.dma_start(out=xw[:], in_=x_words[0].rearrange("p t d -> p (t d)").bitcast(I32))
         load_scales(xs, x_scales[0], nc.sync)
         nc.sync.dma_start(out=dyw[0][:], in_=dy_words[0].rearrange("p t d -> p (t d)").bitcast(I32))
@@ -97,7 +97,7 @@ def tile_moe_rec_mlp_relu2_kernel(
         load_scales(w1s[0], w1_planes[:, :1, :], nc.sync)
         nc.sync.dma_start(out=dyw[1][:], in_=dy_words[1].rearrange("p t d -> p (t d)").bitcast(I32))
         nc.vector.tensor_copy(gds[0][:], dys[:].indirect(offsets[:]))
-        nc.sync.dma_start(out=gds[1][0:100, :].bitcast(I32), in_=gds[0][4:104, :].bitcast(I32))
+        nc.sync.dma_start(out=gds[1][0:112, :].bitcast(I32), in_=gds[0][16:P, :].bitcast(I32))
         load_gate(0, HALVES)
         turn_gate(0, HALVES, "X")
         nc.sync.dma_start(out=w2first[:].bitcast(I32), in_=w2_rows[:, :NP, :])

@@ -78,7 +78,6 @@ def tile_moe_rec_mlp_relu2_kernel(
         nc.vector.memset(zero[:], 0.0)
         for a in (0, HALVES):
             nc.vector.memset(grows[a][:], 0.0)
-        nc.vector.memset(gds[1][:].bitcast(I32), 0)
 
         w2_rows = w2t_words.rearrange("e s p n -> p (e s) n").bitcast(I32)
         w1_rows = w1_words.rearrange("e s p n -> p (e s) n").bitcast(I32)
@@ -116,9 +115,11 @@ def tile_moe_rec_mlp_relu2_kernel(
         for kb in range(KB):
             nc.scalar.activation(win[kb][:], zero[:, 0:1].to_broadcast([P, T]), RELU)
 
-        gxw = keep.tile([P, S], U32, name="gxw", align_bytes=64)
-        nc.vector.tensor_copy(gxw[:], xw[:].bitcast(U32).indirect(offsets[:]))
-        gxsrest = keep.tile([P, S - C], U8, name="gxsrest", align_bytes=64, tag="grows0")
+        gxsrest = keep.tile([P, S - C], U8, name="gxsrest", align_bytes=64)
+        nc.vector.tensor_copy(gxsrest[:], xs[:].indirect(entries(C, S)))
+        gxfirst = keep.tile([P, C], U32, name="gxfirst", align_bytes=64)
+        nc.vector.tensor_copy(gxfirst[:], xw[:].bitcast(U32).indirect(entries(0, C)))
+        gxrest = keep.tile([P, S - C], U32, name="gxrest", align_bytes=64, tag="grows0")
         gd_place = [["gdA", "gdB"], ["gdC", "gdA"], ["gdB", "grouped0"]]
         a_bank = ["A", "B", "A", "B", "C", "D"]
         dh_bank = ["C", "D", "E", "A", "B", "E"]
@@ -131,7 +132,7 @@ def tile_moe_rec_mlp_relu2_kernel(
                 nc.vector.tensor_copy(got[:], dyw[s][:].bitcast(U32).indirect(entries(lo, hi)))
                 gdw.append(got)
             if e == 1:
-                nc.vector.tensor_copy(gxsrest[:], xs[:].indirect(entries(C, S)))
+                nc.vector.tensor_copy(gxrest[:], xw[:].bitcast(U32).indirect(entries(C, S)))
             w1 = w1first[:] if e == 0 else w1rest[:, e - 1, :]
             da = keep.tile([P, HALVES, H], BF16, name="da%d" % e, align_bytes=64)
             for h in range(HALVES):
@@ -140,7 +141,8 @@ def tile_moe_rec_mlp_relu2_kernel(
                 slots = slice(c * P, (c + 1) * P)
                 a_ps = psum.tile([P, H], F32, name="a_ps", tag=a_bank[c])
                 gxs = gxsfirst[:, cols] if e == 0 else gxsrest[:, c * P - C : (c + 1) * P - C]
-                nc.tensor.matmul_mx(out=a_ps[:], lhsT=gxw[:, slots].bitcast(FP8X4), lhsT_scale=gxs,
+                gxw = gxfirst[:, cols] if e == 0 else gxrest[:, c * P - C : (c + 1) * P - C]
+                nc.tensor.matmul_mx(out=a_ps[:], lhsT=gxw.bitcast(FP8X4), lhsT_scale=gxs,
                                     rhs=w1.bitcast(FP4X4), rhs_scale=w1s[0][:, 0, :] if e == 0 else w1s[1][:, e - 1, :], start=True, stop=True)
                 relu2 = keep.tile([P, H], F32, name="relu%d" % c, align_bytes=64)
                 nc.scalar.activation(relu2[:], a_ps[:], RELU, scale=2.0)

@@ -16,6 +16,7 @@ U8 = mybir.dt.uint8
 FP8X4 = mybir.dt.float8_e4m3fn_x4
 FP4X4 = mybir.dt.float4_e2m1fn_x4
 MULT = mybir.AluOpType.mult
+COPY = mybir.ActivationFunctionType.Copy
 RELU = mybir.ActivationFunctionType.Relu
 
 P = 128
@@ -40,16 +41,16 @@ def tile_moe_rec_mlp_relu2_kernel(
         dyw = [keep.tile([P, T], I32, name="dyw%d" % s, align_bytes=64) for s in range(NP)]
         dys = keep.tile([P, T], U8, name="dys", align_bytes=64)
         w1first = keep.tile([P, 2 * H], U8, name="w1first", align_bytes=64)
-        w1rest = keep.tile([P, LAST, 2 * H], U8, name="w1rest", align_bytes=64)
-        w1s = [keep.tile([P, n, H], U8, name="w1s%d" % n, align_bytes=64) for n in (1, LAST)]
+        w1rest = [keep.tile([P, 2 * H], U8, name="w1rest%d" % e, align_bytes=64) for e in range(LAST)]
+        w1s = keep.tile([P, E, H], U8, name="w1s", align_bytes=64)
         w2first = keep.tile([P, NP, 2 * H], U8, name="w2first", align_bytes=64)
-        w2rest = keep.tile([P, LAST * NP, 2 * H], U8, name="w2rest", align_bytes=64)
+        w2rest = [keep.tile([P, NP, 2 * H], U8, name="w2rest%d" % e, align_bytes=64) for e in range(LAST)]
         w2s = [keep.tile([P, n * NP, H], U8, name="w2s%d" % n, align_bytes=64) for n in (1, LAST)]
         w3first = keep.tile([P, 2 * K], U8, name="w3first", align_bytes=64)
         w3rest = keep.tile([P, LAST, 2 * K], U8, name="w3rest", align_bytes=64)
         w3s = keep.tile([P, E, K], U8, name="w3s", align_bytes=64)
-        grows = {a: keep.tile([P, P], F32, name="grows%d" % a, align_bytes=64) for a in (0, HALVES)}
-        gcol = {a: keep.tile([P, n], F32, name="gcol%d" % a) for a, n in ((0, HALVES), (HALVES, S // P - HALVES))}
+        grows = keep.tile([P, E, P], F32, name="grows", align_bytes=64)
+        gcol = keep.tile([P, E, HALVES], F32, name="gcol")
         ident = keep.tile([P, P], F32, name="ident")
         zero = keep.tile([P, 8], F32, name="zero")
         win = [keep.tile([P, T], F32, name="win%d" % kb, align_bytes=64) for kb in range(KB)]
@@ -62,22 +63,13 @@ def tile_moe_rec_mlp_relu2_kernel(
             for r in which:
                 queue.dma_start(out=plane[r:P:32].bitcast(I32), in_=rows[r:16:4].bitcast(I32))
 
-        def load_gate(a, b):
-            nc.sync.dma_start(out=grows[a][a:b, :], in_=gate[0].rearrange("(c p) -> c p", p=P)[a:b])
-
-        def turn_gate(a, b, bank):
-            turned = psum.tile([P, P], F32, name="turned", tag=bank)
-            nc.tensor.transpose(turned[:], grows[a][:], ident[:])
-            nc.scalar.copy(gcol[a][:], turned[:, a:b])
-
         def entries(a, b):
             return offsets[:, a // 16 : b // 16]
 
         nc.gpsimd.memset(dys[:].bitcast(I32), 0)
         nc.gpsimd.memset(xs[:].bitcast(I32), 0)
         nc.vector.memset(zero[:], 0.0)
-        for a in (0, HALVES):
-            nc.vector.memset(grows[a][:], 0.0)
+        nc.vector.memset(grows[:], 0.0)
 
         w2_rows = w2t_words.rearrange("e s p n -> p (e s) n").bitcast(I32)
         w1_rows = w1_words.rearrange("e s p n -> p (e s) n").bitcast(I32)
@@ -93,22 +85,25 @@ def tile_moe_rec_mlp_relu2_kernel(
         load_scales(xs, x_scales[0], nc.sync)
         nc.sync.dma_start(out=dyw[0][:], in_=dy_words[0].rearrange("p t d -> p (t d)").bitcast(I32))
         nc.sync.dma_start(out=w1first[:].bitcast(I32), in_=w1_rows[:, 0, :])
-        load_scales(w1s[0], w1_planes[:, :1, :], nc.sync)
+        load_scales(w1s, w1_planes, nc.sync)
         nc.sync.dma_start(out=dyw[1][:], in_=dy_words[1].rearrange("p t d -> p (t d)").bitcast(I32))
         nc.vector.tensor_copy(gds[0][:], dys[:].indirect(offsets[:]))
-        nc.sync.dma_start(out=gds[1][0:112, :].bitcast(I32), in_=gds[0][16:P, :].bitcast(I32))
-        load_gate(0, HALVES)
-        turn_gate(0, HALVES, "X")
+        nc.sync.dma_start(out=gds[1][0:100, :].bitcast(I32), in_=gds[0][16:116, :].bitcast(I32))
+        nc.sync.dma_start(out=grows[0:HALVES], in_=gate[0].rearrange("(e h p) -> h e p", h=HALVES, p=P))
+        turned = psum.tile([P, E, P], F32, name="turned", tag="X")
+        for e in range(E):
+            nc.tensor.transpose(turned[:, e, :], grows[:, e, :], ident[:])
+        nc.scalar.copy(gcol[:], turned[:, :, 0:HALVES])
         nc.sync.dma_start(out=w2first[:].bitcast(I32), in_=w2_rows[:, :NP, :])
         load_scales(w2s[0], w2_planes[:, :NP, :], nc.sync)
+        load_scales(w2s[1], w2_planes[:, NP:, :], nc.sync)
+        nc.sync.dma_start(out=w1rest[0][:].bitcast(I32), in_=w1_rows[:, 1, :])
         nc.sync.dma_start(out=w3first[:].bitcast(I32), in_=w3_rows[:, 0, :])
         load_scales(w3s, w1t_scales.rearrange("e s b n -> b (e s) n"), nc.sync)
-        load_gate(HALVES, S // P)
-        load_scales(w1s[1], w1_planes[:, 1:, :], nc.sync)
-        nc.sync.dma_start(out=w1rest[:].bitcast(I32), in_=w1_rows[:, 1:, :])
-        load_scales(w2s[1], w2_planes[:, NP:, :], nc.sync)
-        nc.sync.dma_start(out=w2rest[:].bitcast(I32), in_=w2_rows[:, NP:, :])
+        nc.sync.dma_start(out=w2rest[0][:].bitcast(I32), in_=w2_rows[:, NP : 2 * NP, :])
         nc.sync.dma_start(out=w3rest[:].bitcast(I32), in_=w3_rows[:, 1:, :])
+        nc.sync.dma_start(out=w1rest[1][:].bitcast(I32), in_=w1_rows[:, 2, :])
+        nc.sync.dma_start(out=w2rest[1][:].bitcast(I32), in_=w2_rows[:, 2 * NP :, :])
         nc.vector.tensor_copy(gxsfirst[:], xs[:].indirect(entries(0, C)))
 
 
@@ -119,51 +114,54 @@ def tile_moe_rec_mlp_relu2_kernel(
         nc.vector.tensor_copy(gxsrest[:], xs[:].indirect(entries(C, S)))
         gxfirst = keep.tile([P, C], U32, name="gxfirst", align_bytes=64)
         nc.vector.tensor_copy(gxfirst[:], xw[:].bitcast(U32).indirect(entries(0, C)))
-        gxrest = keep.tile([P, S - C], U32, name="gxrest", align_bytes=64, tag="grows0")
+        gxrest = keep.tile([P, S - C], U32, name="gxrest", align_bytes=64, tag="grows")
         gd_place = [["gdA", "gdB"], ["gdC", "gdA"], ["gdB", "grouped0"]]
-        a_bank = ["A", "B", "A", "B", "C", "D"]
-        dh_bank = ["C", "D", "E", "A", "B", "E"]
+        a_bank = "ABAEBA"
+        dh_bank = "CDCDXD"
+        gdw = {}
 
-        def front(e):
-            lo, hi = e * C, (e + 1) * C
-            gdw = []
+        def gather_dy(e):
             for s in range(NP):
-                got = keep.tile([P, C], U32, name="gd%d_%d" % (s, e), align_bytes=64, tag=gd_place[e][s])
-                nc.vector.tensor_copy(got[:], dyw[s][:].bitcast(U32).indirect(entries(lo, hi)))
-                gdw.append(got)
-            if e == 1:
-                nc.vector.tensor_copy(gxrest[:], xw[:].bitcast(U32).indirect(entries(C, S)))
-            w1 = w1first[:] if e == 0 else w1rest[:, e - 1, :]
-            da = keep.tile([P, HALVES, H], BF16, name="da%d" % e, align_bytes=64)
-            for h in range(HALVES):
-                c = e * HALVES + h
-                cols = slice(h * P, (h + 1) * P)
-                slots = slice(c * P, (c + 1) * P)
-                a_ps = psum.tile([P, H], F32, name="a_ps", tag=a_bank[c])
-                gxs = gxsfirst[:, cols] if e == 0 else gxsrest[:, c * P - C : (c + 1) * P - C]
-                gxw = gxfirst[:, cols] if e == 0 else gxrest[:, c * P - C : (c + 1) * P - C]
-                nc.tensor.matmul_mx(out=a_ps[:], lhsT=gxw.bitcast(FP8X4), lhsT_scale=gxs,
-                                    rhs=w1.bitcast(FP4X4), rhs_scale=w1s[0][:, 0, :] if e == 0 else w1s[1][:, e - 1, :], start=True, stop=True)
-                relu2 = keep.tile([P, H], F32, name="relu%d" % c, align_bytes=64)
-                nc.scalar.activation(relu2[:], a_ps[:], RELU, scale=2.0)
-                dh_ps = psum.tile([P, H], F32, name="dh_ps", tag=dh_bank[c])
-                for s in range(NP):
-                    w2 = w2first[:, s, :] if e == 0 else w2rest[:, (e - 1) * NP + s, :]
-                    nc.tensor.matmul_mx(out=dh_ps[:], lhsT=gdw[s][:, cols].bitcast(FP8X4), lhsT_scale=gds[s][:, slots],
-                                        rhs=w2.bitcast(FP4X4), rhs_scale=w2s[0][:, s, :] if e == 0 else w2s[1][:, (e - 1) * NP + s, :],
-                                        start=(s == 0), stop=(s == NP - 1))
-                nc.vector.scalar_tensor_tensor(da[:, h, :], dh_ps[:], gcol[0][:, c : c + 1] if e == 0 else gcol[HALVES][:, c - HALVES : c - HALVES + 1], relu2[:], MULT, MULT)
+                gdw[e, s] = keep.tile([P, C], U32, name="gd%d_%d" % (s, e), align_bytes=64, tag=gd_place[e][s])
+                nc.vector.tensor_copy(gdw[e, s][:], dyw[s][:].bitcast(U32).indirect(entries(e * C, (e + 1) * C)))
+
+        def front(c):
+            e, h = divmod(c, HALVES)
+            w1 = w1first[:] if e == 0 else w1rest[e - 1][:]
+            cols = slice(h * P, (h + 1) * P)
+            slots = slice(c * P, (c + 1) * P)
+            a_ps = psum.tile([P, H], F32, name="a_ps", tag=a_bank[c])
+            gxs = gxsfirst[:, cols] if e == 0 else gxsrest[:, c * P - C : (c + 1) * P - C]
+            gxw = gxfirst[:, cols] if e == 0 else gxrest[:, c * P - C : (c + 1) * P - C]
+            nc.tensor.matmul_mx(out=a_ps[:], lhsT=gxw.bitcast(FP8X4), lhsT_scale=gxs,
+                                rhs=w1.bitcast(FP4X4), rhs_scale=w1s[:, e, :], start=True, stop=True)
+            relu2 = keep.tile([P, H], F32, name="relu%d" % c, align_bytes=64)
+            nc.scalar.activation(relu2[:], a_ps[:], RELU, scale=2.0)
+            dh_ps = psum.tile([P, H], F32, name="dh_ps", tag=dh_bank[c])
+            for s in range(NP):
+                w2 = w2first[:, s, :] if e == 0 else w2rest[e - 1][:, s, :]
+                nc.tensor.matmul_mx(out=dh_ps[:], lhsT=gdw[e, s][:, cols].bitcast(FP8X4), lhsT_scale=gds[s][:, slots],
+                                    rhs=w2.bitcast(FP4X4), rhs_scale=w2s[0][:, s, :] if e == 0 else w2s[1][:, (e - 1) * NP + s, :],
+                                    start=(s == 0), stop=(s == NP - 1))
+            g = gcol[:, e, h : h + 1]
+            da = keep.tile([P, H], BF16, name="da%d" % c, align_bytes=64)
+            if c < 2:
+                nc.vector.scalar_tensor_tensor(da[:], dh_ps[:], g, relu2[:], MULT, MULT)
+            else:
+                dh = keep.tile([P, H], F32, name="dh%d" % c, align_bytes=64)
+                nc.scalar.activation(dh[:], dh_ps[:], COPY, scale=g)
+                nc.gpsimd.tensor_tensor(da[:], dh[:], relu2[:], MULT)
             return da
 
-        def pack(da, lo, halves, bank):
-            hi = lo + P * len(halves)
-            xt = psum.tile([P, len(halves), 2, P], F32, name="xt", tag=bank)
-            for n, h in enumerate(halves):
-                pairs = da[:, h, :].bitcast(F32)
+        def pack(das_in, lo, bank):
+            hi = lo + P * len(das_in)
+            xt = psum.tile([P, len(das_in), 2, P], F32, name="xt", tag=bank)
+            for n, da in enumerate(das_in):
+                pairs = da[:].bitcast(F32)
                 for u in range(2):
                     nc.tensor.transpose(xt[:, n, u, :], pairs[:, u : H // 2 : 2], ident[:])
             grouped = keep.tile([P, hi - lo, 4], BF16, name="grouped%d" % lo, align_bytes=64)
-            nc.scalar.copy(grouped[:].bitcast(F32).rearrange("p (h j) u -> p h j u", h=len(halves)),
+            nc.scalar.copy(grouped[:].bitcast(F32).rearrange("p (h j) u -> p h j u", h=len(das_in)),
                            xt[:].rearrange("p h u j -> p h j u"))
             nc.vector.quantize_mx(out=daw[:, lo:hi].bitcast(FP8X4), scales=das[:, lo:hi],
                                   in_=grouped[:].rearrange("p j t -> p (j t)"))
@@ -186,21 +184,31 @@ def tile_moe_rec_mlp_relu2_kernel(
                 if hi == S:
                     nc.sync.dma_start(out=out[kb * P : (kb + 1) * P, :], in_=win[kb][:])
 
-        da = front(0)
-        pack(da, 0, [0], "X")
-        pack(da, P, [1], "Z")
-        turn_gate(HALVES, S // P, "Z")
+        gather_dy(0)
+        da0 = front(0)
+        da1 = front(1)
+        pack([da0], 0, "X")
+        pack([da1], P, "Z")
         scatter(0, P, [0], back(0, P, [0], "E")[:], "dxA")
         scatter(0, P, [1, 2, 3], back(0, P, [1, 2, 3], "Y")[:], "dxB")
-        da = front(1)
-        sums = back(P, C, [0, 1, 2, 3], "X")
-        scatter(P, C, [0], sums[:, :1, :], "dxC")
-        scatter(P, C, [1], sums[:, 1:2, :], "relu2")
-        pack(da, C, [0, 1], "Y")
-        scatter(P, C, [2, 3], sums[:, 2:, :], "da1")
-        da = front(2)
-        scatter(C, 2 * C, [0, 1], back(C, 2 * C, [0, 1], "Z")[:], "dxD")
-        pack(da, 2 * C, [0, 1], "Z")
-        scatter(C, 2 * C, [2, 3], back(C, 2 * C, [2, 3], "X")[:], "da2")
-        scatter(2 * C, S, [0, 1], back(2 * C, S, [0, 1], "Y")[:], "dxE")
-        scatter(2 * C, S, [2, 3], back(2 * C, S, [2, 3], "X")[:], "dxF")
+        gather_dy(1)
+        nc.vector.tensor_copy(gxrest[:], xw[:].bitcast(U32).indirect(entries(C, S)))
+        gather_dy(2)
+        da2 = front(2)
+        sums1 = back(P, C, [0, 1, 2, 3], "C")
+        scatter(P, C, [0, 1], sums1[:, :2, :], "dxC")
+        da3 = front(3)
+        pack([da2], 2 * P, "Z")
+        scatter(P, C, [2, 3], sums1[:, 2:, :], "da2")
+        da4 = front(4)
+        sums2 = back(2 * P, 3 * P, [0, 1, 2, 3], "Y")
+        scatter(2 * P, 3 * P, [0, 1], sums2[:, :2, :], "dxD")
+        pack([da3], 3 * P, "Z")
+        scatter(2 * P, 3 * P, [2, 3], sums2[:, 2:, :], "da3")
+        da5 = front(5)
+        sums3 = back(3 * P, 4 * P, [0, 1, 2, 3], "X")
+        scatter(3 * P, 4 * P, [0, 1], sums3[:, :2, :], "dxE")
+        pack([da4, da5], 4 * P, "Z")
+        scatter(3 * P, 4 * P, [2, 3], sums3[:, 2:, :], "da5")
+        scatter(2 * C, S, [0, 1], back(2 * C, S, [0, 1], "Y")[:], "dxF")
+        scatter(2 * C, S, [2, 3], back(2 * C, S, [2, 3], "E")[:], "dxG")

@@ -114,25 +114,28 @@ def tile_moe_rec_mlp_relu2_kernel(
         nc.vector.tensor_copy(gxsrest[:], xs[:].indirect(entries(C, S)))
         gxfirst = keep.tile([P, C], U32, name="gxfirst", align_bytes=64)
         nc.vector.tensor_copy(gxfirst[:], xw[:].bitcast(U32).indirect(entries(0, C)))
-        gxrest = keep.tile([P, S - C], U32, name="gxrest", align_bytes=64, tag="grows")
-        gd_place = [["gdA", "gdB"], ["gdC", "gdA"], ["gdB", "grouped0"]]
-        a_bank = "ABAEBA"
+        gxw_of = {0: gxfirst}
+
+        def gather_x(e, place):
+            gxw_of[e] = keep.tile([P, C], U32, name="gx%d" % e, align_bytes=64, tag=place)
+            nc.vector.tensor_copy(gxw_of[e][:], xw[:].bitcast(U32).indirect(entries(e * C, (e + 1) * C)))
+
+        a_bank = "ABAYBA"
         dh_bank = "CDCDXD"
         gdw = {}
 
-        def gather_dy(e):
-            for s in range(NP):
-                gdw[e, s] = keep.tile([P, C], U32, name="gd%d_%d" % (s, e), align_bytes=64, tag=gd_place[e][s])
-                nc.vector.tensor_copy(gdw[e, s][:], dyw[s][:].bitcast(U32).indirect(entries(e * C, (e + 1) * C)))
+        def gather_dy(e, s, place):
+            gdw[e, s] = keep.tile([P, C], U32, name="gd%d_%d" % (s, e), align_bytes=64, tag=place)
+            nc.vector.tensor_copy(gdw[e, s][:], dyw[s][:].bitcast(U32).indirect(entries(e * C, (e + 1) * C)))
 
-        def front(c):
+        def front(c, place=None):
             e, h = divmod(c, HALVES)
             w1 = w1first[:] if e == 0 else w1rest[e - 1][:]
             cols = slice(h * P, (h + 1) * P)
             slots = slice(c * P, (c + 1) * P)
             a_ps = psum.tile([P, H], F32, name="a_ps", tag=a_bank[c])
             gxs = gxsfirst[:, cols] if e == 0 else gxsrest[:, c * P - C : (c + 1) * P - C]
-            gxw = gxfirst[:, cols] if e == 0 else gxrest[:, c * P - C : (c + 1) * P - C]
+            gxw = gxw_of[e][:, cols]
             nc.tensor.matmul_mx(out=a_ps[:], lhsT=gxw.bitcast(FP8X4), lhsT_scale=gxs,
                                 rhs=w1.bitcast(FP4X4), rhs_scale=w1s[:, e, :], start=True, stop=True)
             relu2 = keep.tile([P, H], F32, name="relu%d" % c, align_bytes=64)
@@ -144,7 +147,7 @@ def tile_moe_rec_mlp_relu2_kernel(
                                     rhs=w2.bitcast(FP4X4), rhs_scale=w2s[0][:, s, :] if e == 0 else w2s[1][:, (e - 1) * NP + s, :],
                                     start=(s == 0), stop=(s == NP - 1))
             g = gcol[:, e, h : h + 1]
-            da = keep.tile([P, H], BF16, name="da%d" % c, align_bytes=64)
+            da = keep.tile([P, H], BF16, name="da%d" % c, align_bytes=64, tag=place or "da%d" % c)
             if c < 2:
                 nc.vector.scalar_tensor_tensor(da[:], dh_ps[:], g, relu2[:], MULT, MULT)
             else:
@@ -184,31 +187,37 @@ def tile_moe_rec_mlp_relu2_kernel(
                 if hi == S:
                     nc.sync.dma_start(out=out[kb * P : (kb + 1) * P, :], in_=win[kb][:])
 
-        gather_dy(0)
+        gather_dy(0, 0, "gdA")
+        gather_dy(0, 1, "gdB")
+        gather_dy(1, 1, "gdC")
+        gather_x(1, "grows")
         da0 = front(0)
         da1 = front(1)
+        gather_dy(1, 0, "relu0")
+        gather_x(2, "gdB")
         pack([da0], 0, "X")
         pack([da1], P, "Z")
         scatter(0, P, [0], back(0, P, [0], "E")[:], "dxA")
         scatter(0, P, [1, 2, 3], back(0, P, [1, 2, 3], "Y")[:], "dxB")
-        gather_dy(1)
-        nc.vector.tensor_copy(gxrest[:], xw[:].bitcast(U32).indirect(entries(C, S)))
-        gather_dy(2)
+        gather_dy(2, 0, "da1")
+        gather_dy(2, 1, "grouped0")
         da2 = front(2)
         sums1 = back(P, C, [0, 1, 2, 3], "C")
         scatter(P, C, [0, 1], sums1[:, :2, :], "dxC")
         da3 = front(3)
         pack([da2], 2 * P, "Z")
         scatter(P, C, [2, 3], sums1[:, 2:, :], "da2")
-        da4 = front(4)
-        sums2 = back(2 * P, 3 * P, [0, 1, 2, 3], "Y")
-        scatter(2 * P, 3 * P, [0, 1], sums2[:, :2, :], "dxD")
-        pack([da3], 3 * P, "Z")
-        scatter(2 * P, 3 * P, [2, 3], sums2[:, 2:, :], "da3")
+        da4 = front(4, "grouped256")
         da5 = front(5)
-        sums3 = back(3 * P, 4 * P, [0, 1, 2, 3], "X")
-        scatter(3 * P, 4 * P, [0, 1], sums3[:, :2, :], "dxE")
+        scatter(2 * P, 3 * P, [0, 1], back(2 * P, 3 * P, [0, 1], "Z")[:], "dxD")
+        sums2 = back(2 * P, 3 * P, [2, 3], "E")
+        pack([da3], 3 * P, "Z")
+        scatter(2 * P, 3 * P, [2, 3], sums2[:], "da3")
+        scatter(3 * P, 4 * P, [0, 1], back(3 * P, 4 * P, [0, 1], "X")[:], "dxE")
+        sums3 = back(3 * P, 4 * P, [2, 3], "E")
         pack([da4, da5], 4 * P, "Z")
-        scatter(3 * P, 4 * P, [2, 3], sums3[:, 2:, :], "da5")
-        scatter(2 * C, S, [0, 1], back(2 * C, S, [0, 1], "Y")[:], "dxF")
-        scatter(2 * C, S, [2, 3], back(2 * C, S, [2, 3], "E")[:], "dxG")
+        scatter(3 * P, 4 * P, [2, 3], sums3[:], "da5")
+        sums4 = back(2 * C, S, [0, 1], "Y")
+        scatter(2 * C, S, [0], sums4[:, :1, :], "dxF")
+        scatter(2 * C, S, [1], sums4[:, 1:, :], "dxG")
+        scatter(2 * C, S, [2, 3], back(2 * C, S, [2, 3], "B")[:], "dxH")

@@ -79,12 +79,12 @@ def tile_moe_rec_mlp_relu2_kernel(
         w3_rows = w1t_words.rearrange("e s p n -> p (e s) n").bitcast(I32)
 
         nc.sync.dma_start(offsets[:], offs)
+        nc.sync.dma_start(out=w1first[:].bitcast(I32), in_=w1_rows[:, 0, :])
         for q in range(4):
             nc.sync.dma_start(out=dys[q:P:16, :].bitcast(I32), in_=dy_scales.rearrange("s (q r) n -> r q s n", r=4)[q].bitcast(I32))
         nc.sync.dma_start(out=xw[:], in_=x_words[0].rearrange("p t d -> p (t d)").bitcast(I32))
         load_scales(xs, x_scales[0], nc.sync)
         nc.sync.dma_start(out=dyw[0][:], in_=dy_words[0].rearrange("p t d -> p (t d)").bitcast(I32))
-        nc.sync.dma_start(out=w1first[:].bitcast(I32), in_=w1_rows[:, 0, :])
         load_scales(w1s, w1_planes, nc.sync)
         nc.sync.dma_start(out=dyw[1][:], in_=dy_words[1].rearrange("p t d -> p (t d)").bitcast(I32))
         nc.vector.tensor_copy(gds[0][:], dys[:].indirect(offsets[:]))
@@ -112,9 +112,9 @@ def tile_moe_rec_mlp_relu2_kernel(
 
         gxsrest = keep.tile([P, S - C], U8, name="gxsrest", align_bytes=64)
         nc.vector.tensor_copy(gxsrest[:], xs[:].indirect(entries(C, S)))
-        gxfirst = keep.tile([P, C], U32, name="gxfirst", align_bytes=64)
-        nc.vector.tensor_copy(gxfirst[:], xw[:].bitcast(U32).indirect(entries(0, C)))
-        gxw_of = {0: gxfirst}
+        gxfirst = keep.tile([P, 2 * C], U32, name="gxfirst", align_bytes=64)
+        nc.vector.tensor_copy(gxfirst[:], xw[:].bitcast(U32).indirect(entries(0, 2 * C)))
+        gxw_of = {0: gxfirst[:, :C], 1: gxfirst[:, C:]}
 
         def gather_x(e, place):
             gxw_of[e] = keep.tile([P, C], U32, name="gx%d" % e, align_bytes=64, tag=place)
@@ -124,9 +124,12 @@ def tile_moe_rec_mlp_relu2_kernel(
         dh_bank = "CDCDXD"
         gdw = {}
 
-        def gather_dy(e, s, place):
-            gdw[e, s] = keep.tile([P, C], U32, name="gd%d_%d" % (s, e), align_bytes=64, tag=place)
-            nc.vector.tensor_copy(gdw[e, s][:], dyw[s][:].bitcast(U32).indirect(entries(e * C, (e + 1) * C)))
+        def gather_dy(experts, s, place):
+            lo, hi = experts[0] * C, (experts[-1] + 1) * C
+            got = keep.tile([P, hi - lo], U32, name="gd%d_%d" % (s, lo), align_bytes=64, tag=place)
+            nc.vector.tensor_copy(got[:], dyw[s][:].bitcast(U32).indirect(entries(lo, hi)))
+            for e in experts:
+                gdw[e, s] = got[:, e * C - lo : (e + 1) * C - lo]
 
         def front(c, place=None):
             e, h = divmod(c, HALVES)
@@ -187,20 +190,18 @@ def tile_moe_rec_mlp_relu2_kernel(
                 if hi == S:
                     nc.sync.dma_start(out=out[kb * P : (kb + 1) * P, :], in_=win[kb][:])
 
-        gather_dy(0, 0, "gdA")
-        gather_dy(0, 1, "gdB")
-        gather_dy(1, 1, "gdC")
-        gather_x(1, "grows")
+        gather_dy([0], 0, "gdA")
+        gather_dy([0], 1, "gdB")
+        gather_dy([1, 2], 1, "gdC")
         da0 = front(0)
         da1 = front(1)
-        gather_dy(1, 0, "relu0")
-        gather_x(2, "gdB")
+        gather_dy([1], 0, "relu0")
         pack([da0], 0, "X")
         pack([da1], P, "Z")
         scatter(0, P, [0], back(0, P, [0], "E")[:], "dxA")
         scatter(0, P, [1, 2, 3], back(0, P, [1, 2, 3], "Y")[:], "dxB")
-        gather_dy(2, 0, "da1")
-        gather_dy(2, 1, "grouped0")
+        gather_dy([2], 0, "da1")
+        gather_x(2, "grouped0")
         da2 = front(2)
         sums1 = back(P, C, [0, 1, 2, 3], "C")
         scatter(P, C, [0, 1], sums1[:, :2, :], "dxC")
@@ -209,14 +210,16 @@ def tile_moe_rec_mlp_relu2_kernel(
         scatter(P, C, [2, 3], sums1[:, 2:, :], "da2")
         da4 = front(4, "grouped256")
         da5 = front(5)
-        scatter(2 * P, 3 * P, [0, 1], back(2 * P, 3 * P, [0, 1], "Z")[:], "dxD")
+        sums = back(2 * P, 3 * P, [0, 1], "Z")
+        scatter(2 * P, 3 * P, [0], sums[:, :1, :], "dxD")
+        scatter(2 * P, 3 * P, [1], sums[:, 1:, :], "dxI")
         sums2 = back(2 * P, 3 * P, [2, 3], "E")
         pack([da3], 3 * P, "Z")
         scatter(2 * P, 3 * P, [2, 3], sums2[:], "da3")
-        scatter(3 * P, 4 * P, [0, 1], back(3 * P, 4 * P, [0, 1], "X")[:], "dxE")
-        sums3 = back(3 * P, 4 * P, [2, 3], "E")
+        scatter(3 * P, 4 * P, [0], back(3 * P, 4 * P, [0], "X")[:], "dxE")
+        sums3 = back(3 * P, 4 * P, [1, 2, 3], "E")
         pack([da4, da5], 4 * P, "Z")
-        scatter(3 * P, 4 * P, [2, 3], sums3[:], "da5")
+        scatter(3 * P, 4 * P, [1, 2, 3], sums3[:], "da5")
         sums4 = back(2 * C, S, [0, 1], "Y")
         scatter(2 * C, S, [0], sums4[:, :1, :], "dxF")
         scatter(2 * C, S, [1], sums4[:, 1:, :], "dxG")

@@ -40,8 +40,8 @@ def tile_moe_rec_mlp_relu2_kernel(
         xs = keep.tile([P, T], U8, name="xs", align_bytes=64)
         dyw = [keep.tile([P, T], I32, name="dyw%d" % s, align_bytes=64) for s in range(NP)]
         dys = keep.tile([P, T], U8, name="dys", align_bytes=64)
-        w1first = keep.tile([P, 2 * H], U8, name="w1first", align_bytes=64)
-        w1rest = [keep.tile([P, 2 * H], U8, name="w1rest%d" % e, align_bytes=64) for e in range(LAST)]
+        w1first = keep.tile([P, 2, 2 * H], U8, name="w1first", align_bytes=64)
+        w1rest = {1: keep.tile([P, 2 * H], U8, name="w1last", align_bytes=64)}
         w1s = keep.tile([P, E, H], U8, name="w1s", align_bytes=64)
         w2first = keep.tile([P, NP, 2 * H], U8, name="w2first", align_bytes=64)
         w2rest = [keep.tile([P, NP, 2 * H], U8, name="w2rest%d" % e, align_bytes=64) for e in range(LAST)]
@@ -79,25 +79,24 @@ def tile_moe_rec_mlp_relu2_kernel(
         w3_rows = w1t_words.rearrange("e s p n -> p (e s) n").bitcast(I32)
 
         nc.sync.dma_start(offsets[:], offs)
-        nc.sync.dma_start(out=w1first[:].bitcast(I32), in_=w1_rows[:, 0, :])
+        nc.sync.dma_start(out=w1first[:].bitcast(I32), in_=w1_rows[:, :2, :])
         for q in range(4):
             nc.sync.dma_start(out=dys[q:P:16, :].bitcast(I32), in_=dy_scales.rearrange("s (q r) n -> r q s n", r=4)[q].bitcast(I32))
         nc.sync.dma_start(out=xw[:], in_=x_words[0].rearrange("p t d -> p (t d)").bitcast(I32))
         load_scales(xs, x_scales[0], nc.sync)
-        nc.sync.dma_start(out=dyw[0][:], in_=dy_words[0].rearrange("p t d -> p (t d)").bitcast(I32))
-        load_scales(w1s, w1_planes, nc.sync)
-        nc.sync.dma_start(out=dyw[1][:], in_=dy_words[1].rearrange("p t d -> p (t d)").bitcast(I32))
-        nc.vector.tensor_copy(gds[0][:], dys[:].indirect(offsets[:]))
-        nc.sync.dma_start(out=gds[1][0:100, :].bitcast(I32), in_=gds[0][16:116, :].bitcast(I32))
         nc.sync.dma_start(out=grows[0:HALVES], in_=gate[0].rearrange("(e h p) -> h e p", h=HALVES, p=P))
         turned = psum.tile([P, E, P], F32, name="turned", tag="X")
         for e in range(E):
             nc.tensor.transpose(turned[:, e, :], grows[:, e, :], ident[:])
         nc.scalar.copy(gcol[:], turned[:, :, 0:HALVES])
+        nc.sync.dma_start(out=dyw[0][:], in_=dy_words[0].rearrange("p t d -> p (t d)").bitcast(I32))
+        load_scales(w1s, w1_planes, nc.sync)
+        nc.sync.dma_start(out=dyw[1][:], in_=dy_words[1].rearrange("p t d -> p (t d)").bitcast(I32))
+        nc.vector.tensor_copy(gds[0][:], dys[:].indirect(offsets[:]))
+        nc.sync.dma_start(out=gds[1][0:100, :].bitcast(I32), in_=gds[0][16:116, :].bitcast(I32))
         nc.sync.dma_start(out=w2first[:].bitcast(I32), in_=w2_rows[:, :NP, :])
         load_scales(w2s[0], w2_planes[:, :NP, :], nc.sync)
         load_scales(w2s[1], w2_planes[:, NP:, :], nc.sync)
-        nc.sync.dma_start(out=w1rest[0][:].bitcast(I32), in_=w1_rows[:, 1, :])
         nc.sync.dma_start(out=w3first[:].bitcast(I32), in_=w3_rows[:, 0, :])
         load_scales(w3s, w1t_scales.rearrange("e s b n -> b (e s) n"), nc.sync)
         nc.sync.dma_start(out=w2rest[0][:].bitcast(I32), in_=w2_rows[:, NP : 2 * NP, :])
@@ -120,7 +119,7 @@ def tile_moe_rec_mlp_relu2_kernel(
             gxw_of[e] = keep.tile([P, C], U32, name="gx%d" % e, align_bytes=64, tag=place)
             nc.vector.tensor_copy(gxw_of[e][:], xw[:].bitcast(U32).indirect(entries(e * C, (e + 1) * C)))
 
-        a_bank = "ABAYBA"
+        a_bank = "ABEYBA"
         dh_bank = "CDCDXD"
         gdw = {}
 
@@ -131,18 +130,31 @@ def tile_moe_rec_mlp_relu2_kernel(
             for e in experts:
                 gdw[e, s] = got[:, e * C - lo : (e + 1) * C - lo]
 
-        def front(c, place=None):
+        slopes = {}
+
+        def by_half(ps):
+            return ps[:].rearrange("p (w u e) -> p u w e", u=2, e=2)
+
+        def slope(c):
             e, h = divmod(c, HALVES)
-            w1 = w1first[:] if e == 0 else w1rest[e - 1][:]
+            w1 = w1first[:, e, :] if e < 2 else w1rest[1][:]
             cols = slice(h * P, (h + 1) * P)
-            slots = slice(c * P, (c + 1) * P)
             a_ps = psum.tile([P, H], F32, name="a_ps", tag=a_bank[c])
             gxs = gxsfirst[:, cols] if e == 0 else gxsrest[:, c * P - C : (c + 1) * P - C]
             gxw = gxw_of[e][:, cols]
             nc.tensor.matmul_mx(out=a_ps[:], lhsT=gxw.bitcast(FP8X4), lhsT_scale=gxs,
                                 rhs=w1.bitcast(FP4X4), rhs_scale=w1s[:, e, :], start=True, stop=True)
             relu2 = keep.tile([P, H], F32, name="relu%d" % c, align_bytes=64)
-            nc.scalar.activation(relu2[:], a_ps[:], RELU, scale=2.0)
+            nc.scalar.activation(relu2[:].rearrange("p (u w e) -> p u w e", u=2, e=2), by_half(a_ps), RELU, scale=2.0)
+            slopes[c] = relu2
+
+        def front(c, place=None):
+            if c not in slopes:
+                slope(c)
+            relu2 = slopes[c]
+            e, h = divmod(c, HALVES)
+            cols = slice(h * P, (h + 1) * P)
+            slots = slice(c * P, (c + 1) * P)
             dh_ps = psum.tile([P, H], F32, name="dh_ps", tag=dh_bank[c])
             for s in range(NP):
                 w2 = w2first[:, s, :] if e == 0 else w2rest[e - 1][:, s, :]
@@ -151,26 +163,36 @@ def tile_moe_rec_mlp_relu2_kernel(
                                     start=(s == 0), stop=(s == NP - 1))
             g = gcol[:, e, h : h + 1]
             da = keep.tile([P, H], BF16, name="da%d" % c, align_bytes=64, tag=place or "da%d" % c)
-            if c < 2:
-                nc.vector.scalar_tensor_tensor(da[:], dh_ps[:], g, relu2[:], MULT, MULT)
-            else:
-                dh = keep.tile([P, H], F32, name="dh%d" % c, align_bytes=64)
-                nc.scalar.activation(dh[:], dh_ps[:], COPY, scale=g)
-                nc.gpsimd.tensor_tensor(da[:], dh[:], relu2[:], MULT)
+            dh = None if c < 2 else keep.tile([P, H], F32, name="dh%d" % c, align_bytes=64)
+            for u in range(2):
+                half = slice(u * H // 2, (u + 1) * H // 2)
+                if dh is None:
+                    nc.vector.scalar_tensor_tensor(da[:, half].rearrange("p (w e) -> p w e", e=2), by_half(dh_ps)[:, u], g,
+                                                   relu2[:, half].rearrange("p (w e) -> p w e", e=2), MULT, MULT)
+                else:
+                    nc.scalar.activation(dh[:, half].rearrange("p (w e) -> p w e", e=2), by_half(dh_ps)[:, u], COPY, scale=g)
+                    nc.gpsimd.tensor_tensor(da[:, half], dh[:, half], relu2[:, half], MULT)
             return da
 
-        def pack(das_in, lo, bank):
-            hi = lo + P * len(das_in)
+        def turn(das_in, bank):
             xt = psum.tile([P, len(das_in), 2, P], F32, name="xt", tag=bank)
             for n, da in enumerate(das_in):
                 pairs = da[:].bitcast(F32)
                 for u in range(2):
-                    nc.tensor.transpose(xt[:, n, u, :], pairs[:, u : H // 2 : 2], ident[:])
+                    nc.tensor.transpose(xt[:, n, u, :], pairs[:, u * P : (u + 1) * P], ident[:])
+            return xt
+
+        def quantise(xt, lo):
+            chunks = xt.shape[1]
+            hi = lo + P * chunks
             grouped = keep.tile([P, hi - lo, 4], BF16, name="grouped%d" % lo, align_bytes=64)
-            nc.scalar.copy(grouped[:].bitcast(F32).rearrange("p (h j) u -> p h j u", h=len(das_in)),
+            nc.scalar.copy(grouped[:].bitcast(F32).rearrange("p (h j) u -> p h j u", h=chunks),
                            xt[:].rearrange("p h u j -> p h j u"))
             nc.vector.quantize_mx(out=daw[:, lo:hi].bitcast(FP8X4), scales=das[:, lo:hi],
                                   in_=grouped[:].rearrange("p j t -> p (j t)"))
+
+        def pack(das_in, lo, bank):
+            quantise(turn(das_in, bank), lo)
 
         def back(lo, hi, blocks, bank):
             e = lo // C
@@ -193,6 +215,8 @@ def tile_moe_rec_mlp_relu2_kernel(
         gather_dy([0], 0, "gdA")
         gather_dy([0], 1, "gdB")
         gather_dy([1, 2], 1, "gdC")
+        for c in range(4):
+            slope(c)
         da0 = front(0)
         da1 = front(1)
         gather_dy([1], 0, "relu0")
@@ -216,9 +240,10 @@ def tile_moe_rec_mlp_relu2_kernel(
         sums2 = back(2 * P, 3 * P, [2, 3], "E")
         pack([da3], 3 * P, "Z")
         scatter(2 * P, 3 * P, [2, 3], sums2[:], "da3")
+        turned45 = turn([da4, da5], "Z")
         scatter(3 * P, 4 * P, [0], back(3 * P, 4 * P, [0], "X")[:], "dxE")
         sums3 = back(3 * P, 4 * P, [1, 2, 3], "E")
-        pack([da4, da5], 4 * P, "Z")
+        quantise(turned45, 4 * P)
         scatter(3 * P, 4 * P, [1, 2, 3], sums3[:], "da5")
         sums4 = back(2 * C, S, [0, 1], "Y")
         scatter(2 * C, S, [0], sums4[:, :1, :], "dxF")

@@ -100,9 +100,9 @@ def tile_moe_rec_mlp_relu2_kernel(
         nc.sync.dma_start(out=w3first[:].bitcast(I32), in_=w3_rows[:, 0, :])
         load_scales(w3s, w1t_scales.rearrange("e s b n -> b (e s) n"), nc.sync)
         nc.sync.dma_start(out=w2rest[0][:].bitcast(I32), in_=w2_rows[:, NP : 2 * NP, :])
-        nc.sync.dma_start(out=w3rest[:].bitcast(I32), in_=w3_rows[:, 1:, :])
         nc.sync.dma_start(out=w1rest[1][:].bitcast(I32), in_=w1_rows[:, 2, :])
         nc.sync.dma_start(out=w2rest[1][:].bitcast(I32), in_=w2_rows[:, 2 * NP :, :])
+        nc.sync.dma_start(out=w3rest[:].bitcast(I32), in_=w3_rows[:, 1:, :])
         nc.vector.tensor_copy(gxsfirst[:], xs[:].indirect(entries(0, C)))
 
 
@@ -119,8 +119,8 @@ def tile_moe_rec_mlp_relu2_kernel(
             gxw_of[e] = keep.tile([P, C], U32, name="gx%d" % e, align_bytes=64, tag=place)
             nc.vector.tensor_copy(gxw_of[e][:], xw[:].bitcast(U32).indirect(entries(e * C, (e + 1) * C)))
 
-        a_bank = "ABEYBA"
-        dh_bank = "CDCDXD"
+        a_bank = "ABEYAD"
+        dh_bank = "CDCDXB"
         gdw = {}
 
         def gather_dy(experts, s, place):
@@ -130,6 +130,7 @@ def tile_moe_rec_mlp_relu2_kernel(
             for e in experts:
                 gdw[e, s] = got[:, e * C - lo : (e + 1) * C - lo]
 
+        VEC = 2
         slopes = {}
 
         def by_half(ps):
@@ -148,10 +149,15 @@ def tile_moe_rec_mlp_relu2_kernel(
             nc.scalar.activation(relu2[:].rearrange("p (u w e) -> p u w e", u=2, e=2), by_half(a_ps), RELU, scale=2.0)
             slopes[c] = relu2
 
-        def front(c, place=None):
+        grads = {}
+
+        def parts_of(c):
+            parts = 2 if c <= 2 else 1
+            return [(slice(n * H // parts, (n + 1) * H // parts), slice(n * 2 // parts, (n + 1) * 2 // parts)) for n in range(parts)]
+
+        def grad(c):
             if c not in slopes:
                 slope(c)
-            relu2 = slopes[c]
             e, h = divmod(c, HALVES)
             cols = slice(h * P, (h + 1) * P)
             slots = slice(c * P, (c + 1) * P)
@@ -161,17 +167,25 @@ def tile_moe_rec_mlp_relu2_kernel(
                 nc.tensor.matmul_mx(out=dh_ps[:], lhsT=gdw[e, s][:, cols].bitcast(FP8X4), lhsT_scale=gds[s][:, slots],
                                     rhs=w2.bitcast(FP4X4), rhs_scale=w2s[0][:, s, :] if e == 0 else w2s[1][:, (e - 1) * NP + s, :],
                                     start=(s == 0), stop=(s == NP - 1))
-            g = gcol[:, e, h : h + 1]
+            if c < VEC:
+                grads[c] = dh_ps
+                return
+            grads[c] = keep.tile([P, H], F32, name="dh%d" % c, align_bytes=64)
+            for half, us in parts_of(c):
+                nc.scalar.activation(grads[c][:, half].rearrange("p (u w e) -> p u w e", w=P, e=2), by_half(dh_ps)[:, us],
+                                     COPY, scale=gcol[:, e, h : h + 1])
+
+        def front(c, place=None):
+            if c not in grads:
+                grad(c)
+            e, h = divmod(c, HALVES)
             da = keep.tile([P, H], BF16, name="da%d" % c, align_bytes=64, tag=place or "da%d" % c)
-            dh = None if c < 2 else keep.tile([P, H], F32, name="dh%d" % c, align_bytes=64)
-            for u in range(2):
-                half = slice(u * H // 2, (u + 1) * H // 2)
-                if dh is None:
-                    nc.vector.scalar_tensor_tensor(da[:, half].rearrange("p (w e) -> p w e", e=2), by_half(dh_ps)[:, u], g,
-                                                   relu2[:, half].rearrange("p (w e) -> p w e", e=2), MULT, MULT)
+            for half, us in parts_of(c):
+                if c < VEC:
+                    nc.vector.scalar_tensor_tensor(da[:, half].rearrange("p (w e) -> p w e", e=2), by_half(grads[c])[:, us.start],
+                                                   gcol[:, e, h : h + 1], slopes[c][:, half].rearrange("p (w e) -> p w e", e=2), MULT, MULT)
                 else:
-                    nc.scalar.activation(dh[:, half].rearrange("p (w e) -> p w e", e=2), by_half(dh_ps)[:, u], COPY, scale=g)
-                    nc.gpsimd.tensor_tensor(da[:, half], dh[:, half], relu2[:, half], MULT)
+                    nc.gpsimd.tensor_tensor(da[:, half], grads[c][:, half], slopes[c][:, half], MULT)
             return da
 
         def turn(das_in, bank):
@@ -227,25 +241,24 @@ def tile_moe_rec_mlp_relu2_kernel(
         gather_dy([2], 0, "da1")
         gather_x(2, "grouped0")
         da2 = front(2)
-        sums1 = back(P, C, [0, 1, 2, 3], "C")
+        sums1 = back(P, C, [0, 1, 2, 3], "Y")
         scatter(P, C, [0, 1], sums1[:, :2, :], "dxC")
         da3 = front(3)
+        grad(4)
         pack([da2], 2 * P, "Z")
         scatter(P, C, [2, 3], sums1[:, 2:, :], "da2")
         da4 = front(4, "grouped256")
-        da5 = front(5)
-        sums = back(2 * P, 3 * P, [0, 1], "Z")
+        grad(5)
+        pack([da3], 3 * P, "C")
+        sums = back(2 * P, 3 * P, [0, 1, 2, 3], "Z")
         scatter(2 * P, 3 * P, [0], sums[:, :1, :], "dxD")
-        scatter(2 * P, 3 * P, [1], sums[:, 1:, :], "dxI")
-        sums2 = back(2 * P, 3 * P, [2, 3], "E")
-        pack([da3], 3 * P, "Z")
-        scatter(2 * P, 3 * P, [2, 3], sums2[:], "da3")
-        turned45 = turn([da4, da5], "Z")
+        scatter(2 * P, 3 * P, [1, 2, 3], sums[:, 1:, :], "dxI")
+        da5 = front(5, "grouped384")
         scatter(3 * P, 4 * P, [0], back(3 * P, 4 * P, [0], "X")[:], "dxE")
         sums3 = back(3 * P, 4 * P, [1, 2, 3], "E")
-        quantise(turned45, 4 * P)
-        scatter(3 * P, 4 * P, [1, 2, 3], sums3[:], "da5")
+        pack([da4, da5], 4 * P, "C")
+        scatter(3 * P, 4 * P, [1, 2, 3], sums3[:], "grouped384")
         sums4 = back(2 * C, S, [0, 1], "Y")
         scatter(2 * C, S, [0], sums4[:, :1, :], "dxF")
         scatter(2 * C, S, [1], sums4[:, 1:, :], "dxG")
-        scatter(2 * C, S, [2, 3], back(2 * C, S, [2, 3], "B")[:], "dxH")
+        scatter(2 * C, S, [2, 3], back(2 * C, S, [2, 3], "A")[:], "dxH")

@@ -73,7 +73,6 @@ def tile_moe_rec_mlp_relu2_kernel(
 
         w2_rows = w2t_words.rearrange("e s p n -> p (e s) n").bitcast(I32)
         w1_rows = w1_words.rearrange("e s p n -> p (e s) n").bitcast(I32)
-        make_identity(nc, ident[:])
         w1_planes = w1_scales.rearrange("e s b n -> b (e s) n")
         w2_planes = w2t_scales.rearrange("e s b n -> b (e s) n")
         w3_rows = w1t_words.rearrange("e s p n -> p (e s) n").bitcast(I32)
@@ -84,13 +83,15 @@ def tile_moe_rec_mlp_relu2_kernel(
             nc.sync.dma_start(out=dys[q:P:16, :].bitcast(I32), in_=dy_scales.rearrange("s (q r) n -> r q s n", r=4)[q].bitcast(I32))
         nc.sync.dma_start(out=xw[:], in_=x_words[0].rearrange("p t d -> p (t d)").bitcast(I32))
         load_scales(xs, x_scales[0], nc.sync)
-        nc.sync.dma_start(out=grows[0:HALVES], in_=gate[0].rearrange("(e h p) -> h e p", h=HALVES, p=P))
+        nc.gpsimd.dma_start(out=grows[0:HALVES], in_=gate[0].rearrange("(e h p) -> h e p", h=HALVES, p=P))
+        make_identity(nc, ident[:])
         turned = psum.tile([P, E, P], F32, name="turned", tag="X")
         for e in range(E):
             nc.tensor.transpose(turned[:, e, :], grows[:, e, :], ident[:])
         nc.scalar.copy(gcol[:], turned[:, :, 0:HALVES])
         nc.sync.dma_start(out=dyw[0][:], in_=dy_words[0].rearrange("p t d -> p (t d)").bitcast(I32))
-        load_scales(w1s, w1_planes, nc.sync)
+        load_scales(w1s, w1_planes, nc.gpsimd, range(1))
+        load_scales(w1s, w1_planes, nc.sync, range(1, 4))
         nc.sync.dma_start(out=dyw[1][:], in_=dy_words[1].rearrange("p t d -> p (t d)").bitcast(I32))
         nc.vector.tensor_copy(gds[0][:], dys[:].indirect(offsets[:]))
         nc.sync.dma_start(out=gds[1][0:100, :].bitcast(I32), in_=gds[0][16:116, :].bitcast(I32))

@@ -83,6 +83,7 @@ def tile_moe_rec_mlp_relu2_kernel(
             nc.sync.dma_start(out=dys[q:P:16, :].bitcast(I32), in_=dy_scales.rearrange("s (q r) n -> r q s n", r=4)[q].bitcast(I32))
         nc.sync.dma_start(out=xw[:], in_=x_words[0].rearrange("p t d -> p (t d)").bitcast(I32))
         load_scales(xs, x_scales[0], nc.sync)
+        load_scales(w1s, w1_planes, nc.gpsimd, range(1))
         nc.gpsimd.dma_start(out=grows[0:HALVES], in_=gate[0].rearrange("(e h p) -> h e p", h=HALVES, p=P))
         make_identity(nc, ident[:])
         turned = psum.tile([P, E, P], F32, name="turned", tag="X")
@@ -90,7 +91,6 @@ def tile_moe_rec_mlp_relu2_kernel(
             nc.tensor.transpose(turned[:, e, :], grows[:, e, :], ident[:])
         nc.scalar.copy(gcol[:], turned[:, :, 0:HALVES])
         nc.sync.dma_start(out=dyw[0][:], in_=dy_words[0].rearrange("p t d -> p (t d)").bitcast(I32))
-        load_scales(w1s, w1_planes, nc.gpsimd, range(1))
         load_scales(w1s, w1_planes, nc.sync, range(1, 4))
         nc.sync.dma_start(out=dyw[1][:], in_=dy_words[1].rearrange("p t d -> p (t d)").bitcast(I32))
         nc.vector.tensor_copy(gds[0][:], dys[:].indirect(offsets[:]))

@@ -54,7 +54,6 @@ def tile_moe_rec_mlp_relu2_kernel(
         ident = keep.tile([P, P], F32, name="ident")
         zero = keep.tile([P, 8], F32, name="zero")
         win = [keep.tile([P, T], F32, name="win%d" % kb, align_bytes=64) for kb in range(KB)]
-        gxsfirst = keep.tile([P, C], U8, name="gxsfirst", align_bytes=64)
         gds = [keep.tile([P, S], U8, name="gds%d" % s, align_bytes=64) for s in range(NP)]
         daw = keep.tile([P, S], U32, name="daw", align_bytes=64)
         das = keep.tile([P, S], U8, name="das", align_bytes=64)
@@ -91,27 +90,35 @@ def tile_moe_rec_mlp_relu2_kernel(
             nc.tensor.transpose(turned[:, e, :], grows[:, e, :], ident[:])
         nc.scalar.copy(gcol[:], turned[:, :, 0:HALVES])
         nc.sync.dma_start(out=dyw[0][:], in_=dy_words[0].rearrange("p t d -> p (t d)").bitcast(I32))
-        load_scales(w1s, w1_planes, nc.sync, range(1, 4))
+        load_scales(w1s, w1_planes, nc.sync, range(1, 2))
         nc.sync.dma_start(out=dyw[1][:], in_=dy_words[1].rearrange("p t d -> p (t d)").bitcast(I32))
+        load_scales(w1s, w1_planes, nc.sync, range(2, 4))
         nc.vector.tensor_copy(gds[0][:], dys[:].indirect(offsets[:]))
         nc.sync.dma_start(out=gds[1][0:100, :].bitcast(I32), in_=gds[0][16:116, :].bitcast(I32))
         nc.sync.dma_start(out=w2first[:].bitcast(I32), in_=w2_rows[:, :NP, :])
         load_scales(w2s[0], w2_planes[:, :NP, :], nc.sync)
-        load_scales(w2s[1], w2_planes[:, NP:, :], nc.sync)
-        nc.sync.dma_start(out=w3first[:].bitcast(I32), in_=w3_rows[:, 0, :])
-        load_scales(w3s, w1t_scales.rearrange("e s b n -> b (e s) n"), nc.sync)
-        nc.sync.dma_start(out=w2rest[0][:].bitcast(I32), in_=w2_rows[:, NP : 2 * NP, :])
         nc.sync.dma_start(out=w1rest[1][:].bitcast(I32), in_=w1_rows[:, 2, :])
+        nc.sync.dma_start(out=w3first[:].bitcast(I32), in_=w3_rows[:, 0, :])
+        load_scales(w2s[1], w2_planes[:, NP:, :], nc.sync)
+        nc.sync.dma_start(out=w2rest[0][:].bitcast(I32), in_=w2_rows[:, NP : 2 * NP, :])
+        load_scales(w3s, w1t_scales.rearrange("e s b n -> b (e s) n"), nc.sync)
         nc.sync.dma_start(out=w2rest[1][:].bitcast(I32), in_=w2_rows[:, 2 * NP :, :])
         nc.sync.dma_start(out=w3rest[:].bitcast(I32), in_=w3_rows[:, 1:, :])
-        nc.vector.tensor_copy(gxsfirst[:], xs[:].indirect(entries(0, C)))
 
 
         for kb in range(KB):
             nc.scalar.activation(win[kb][:], zero[:, 0:1].to_broadcast([P, T]), RELU)
 
-        gxsrest = keep.tile([P, S - C], U8, name="gxsrest", align_bytes=64)
-        nc.vector.tensor_copy(gxsrest[:], xs[:].indirect(entries(C, S)))
+        gxs_of = {}
+
+        def gather_xs(chunks, place):
+            got = keep.tile([P, P * len(chunks)], U8, name="gxs%d" % chunks[0], align_bytes=64, tag=place)
+            nc.vector.tensor_copy(got[:], xs[:].indirect(entries(chunks[0] * P, (chunks[-1] + 1) * P)))
+            for n, c in enumerate(chunks):
+                gxs_of[c] = got[:, n * P : (n + 1) * P]
+
+        gather_xs([0], "gxsA")
+        gather_xs([1, 2, 3], "gxsB")
         gxfirst = keep.tile([P, 2 * C], U32, name="gxfirst", align_bytes=64)
         nc.vector.tensor_copy(gxfirst[:], xw[:].bitcast(U32).indirect(entries(0, 2 * C)))
         gxw_of = {0: gxfirst[:, :C], 1: gxfirst[:, C:]}
@@ -120,29 +127,23 @@ def tile_moe_rec_mlp_relu2_kernel(
             gxw_of[e] = keep.tile([P, C], U32, name="gx%d" % e, align_bytes=64, tag=place)
             nc.vector.tensor_copy(gxw_of[e][:], xw[:].bitcast(U32).indirect(entries(e * C, (e + 1) * C)))
 
-        a_bank = "ABEYAD"
-        dh_bank = "CDCDXB"
         gdw = {}
 
-        def gather_dy(experts, s, place):
-            lo, hi = experts[0] * C, (experts[-1] + 1) * C
-            got = keep.tile([P, hi - lo], U32, name="gd%d_%d" % (s, lo), align_bytes=64, tag=place)
-            nc.vector.tensor_copy(got[:], dyw[s][:].bitcast(U32).indirect(entries(lo, hi)))
-            for e in experts:
-                gdw[e, s] = got[:, e * C - lo : (e + 1) * C - lo]
+        def gather_dy(e, s, place):
+            gdw[e, s] = keep.tile([P, C], U32, name="gd%d_%d" % (s, e), align_bytes=64, tag=place)
+            nc.vector.tensor_copy(gdw[e, s][:], dyw[s][:].bitcast(U32).indirect(entries(e * C, (e + 1) * C)))
 
-        VEC = 2
         slopes = {}
 
         def by_half(ps):
             return ps[:].rearrange("p (w u e) -> p u w e", u=2, e=2)
 
-        def slope(c):
+        def slope(c, bank):
             e, h = divmod(c, HALVES)
             w1 = w1first[:, e, :] if e < 2 else w1rest[1][:]
             cols = slice(h * P, (h + 1) * P)
-            a_ps = psum.tile([P, H], F32, name="a_ps", tag=a_bank[c])
-            gxs = gxsfirst[:, cols] if e == 0 else gxsrest[:, c * P - C : (c + 1) * P - C]
+            a_ps = psum.tile([P, H], F32, name="a_ps", tag=bank)
+            gxs = gxs_of[c]
             gxw = gxw_of[e][:, cols]
             nc.tensor.matmul_mx(out=a_ps[:], lhsT=gxw.bitcast(FP8X4), lhsT_scale=gxs,
                                 rhs=w1.bitcast(FP4X4), rhs_scale=w1s[:, e, :], start=True, stop=True)
@@ -150,43 +151,25 @@ def tile_moe_rec_mlp_relu2_kernel(
             nc.scalar.activation(relu2[:].rearrange("p (u w e) -> p u w e", u=2, e=2), by_half(a_ps), RELU, scale=2.0)
             slopes[c] = relu2
 
-        grads = {}
-
-        def parts_of(c):
-            parts = 2 if c <= 2 else 1
-            return [(slice(n * H // parts, (n + 1) * H // parts), slice(n * 2 // parts, (n + 1) * 2 // parts)) for n in range(parts)]
-
-        def grad(c):
-            if c not in slopes:
-                slope(c)
+        def grad(c, bank, passes=(0, 1)):
             e, h = divmod(c, HALVES)
             cols = slice(h * P, (h + 1) * P)
             slots = slice(c * P, (c + 1) * P)
-            dh_ps = psum.tile([P, H], F32, name="dh_ps", tag=dh_bank[c])
-            for s in range(NP):
+            dh_ps = psum.tile([P, H], F32, name="dh_ps", tag=bank)
+            for s in passes:
                 w2 = w2first[:, s, :] if e == 0 else w2rest[e - 1][:, s, :]
                 nc.tensor.matmul_mx(out=dh_ps[:], lhsT=gdw[e, s][:, cols].bitcast(FP8X4), lhsT_scale=gds[s][:, slots],
                                     rhs=w2.bitcast(FP4X4), rhs_scale=w2s[0][:, s, :] if e == 0 else w2s[1][:, (e - 1) * NP + s, :],
-                                    start=(s == 0), stop=(s == NP - 1))
-            if c < VEC:
-                grads[c] = dh_ps
-                return
-            grads[c] = keep.tile([P, H], F32, name="dh%d" % c, align_bytes=64)
-            for half, us in parts_of(c):
-                nc.scalar.activation(grads[c][:, half].rearrange("p (u w e) -> p u w e", w=P, e=2), by_half(dh_ps)[:, us],
-                                     COPY, scale=gcol[:, e, h : h + 1])
+                                    start=(s == passes[0]), stop=(s == passes[-1]))
+            return dh_ps
 
-        def front(c, place=None):
-            if c not in grads:
-                grad(c)
+        def product(c, dh_ps):
             e, h = divmod(c, HALVES)
-            da = keep.tile([P, H], BF16, name="da%d" % c, align_bytes=64, tag=place or "da%d" % c)
-            for half, us in parts_of(c):
-                if c < VEC:
-                    nc.vector.scalar_tensor_tensor(da[:, half].rearrange("p (w e) -> p w e", e=2), by_half(grads[c])[:, us.start],
-                                                   gcol[:, e, h : h + 1], slopes[c][:, half].rearrange("p (w e) -> p w e", e=2), MULT, MULT)
-                else:
-                    nc.gpsimd.tensor_tensor(da[:, half], grads[c][:, half], slopes[c][:, half], MULT)
+            da = keep.tile([P, H], BF16, name="da%d" % c, align_bytes=64)
+            for u in range(2):
+                half = slice(u * H // 2, (u + 1) * H // 2)
+                nc.vector.scalar_tensor_tensor(da[:, half].rearrange("p (w e) -> p w e", e=2), by_half(dh_ps)[:, u],
+                                               gcol[:, e, h : h + 1], slopes[c][:, half].rearrange("p (w e) -> p w e", e=2), MULT, MULT)
             return da
 
         def turn(das_in, bank):
@@ -197,69 +180,85 @@ def tile_moe_rec_mlp_relu2_kernel(
                     nc.tensor.transpose(xt[:, n, u, :], pairs[:, u * P : (u + 1) * P], ident[:])
             return xt
 
-        def quantise(xt, lo):
+        def copy_on(engine):
+            return nc.scalar.copy if engine == "S" else nc.vector.tensor_copy
+
+        def quantise(xt, lo, engine):
             chunks = xt.shape[1]
             hi = lo + P * chunks
             grouped = keep.tile([P, hi - lo, 4], BF16, name="grouped%d" % lo, align_bytes=64)
-            nc.scalar.copy(grouped[:].bitcast(F32).rearrange("p (h j) u -> p h j u", h=chunks),
-                           xt[:].rearrange("p h u j -> p h j u"))
+            copy_on(engine)(grouped[:].bitcast(F32).rearrange("p (h j) u -> p h j u", h=chunks),
+                            xt[:].rearrange("p h u j -> p h j u"))
             nc.vector.quantize_mx(out=daw[:, lo:hi].bitcast(FP8X4), scales=das[:, lo:hi],
                                   in_=grouped[:].rearrange("p j t -> p (j t)"))
 
-        def pack(das_in, lo, bank):
-            quantise(turn(das_in, bank), lo)
-
-        def back(lo, hi, blocks, bank):
-            e = lo // C
-            w3 = w3first[:] if e == 0 else w3rest[:, e - 1, :]
-            dx_ps = psum.tile([P, len(blocks), hi - lo], F32, name="dx_ps", tag=bank)
-            for v, kb in enumerate(blocks):
-                nc.tensor.matmul_mx(out=dx_ps[:, v, :], lhsT=w3[:, 2 * P * kb : 2 * P * (kb + 1)].bitcast(FP4X4),
+        def back(pieces, bank):
+            dx_ps = psum.tile([P, sum(hi - lo for kb, lo, hi in pieces)], F32, name="dx_ps", tag=bank)
+            at = 0
+            for kb, lo, hi in pieces:
+                e = lo // C
+                w3 = w3first[:] if e == 0 else w3rest[:, e - 1, :]
+                nc.tensor.matmul_mx(out=dx_ps[:, at : at + hi - lo], lhsT=w3[:, 2 * P * kb : 2 * P * (kb + 1)].bitcast(FP4X4),
                                     lhsT_scale=w3s[:, e, P * kb : P * (kb + 1)],
                                     rhs=daw[:, lo:hi].bitcast(FP8X4), rhs_scale=das[:, lo:hi], start=True, stop=True)
+                at = at + hi - lo
             return dx_ps
 
-        def scatter(lo, hi, blocks, sums, place):
-            dx = keep.tile([P, len(blocks), hi - lo], F32, name="dx", align_bytes=64, tag=place)
-            nc.scalar.copy(dx[:], sums)
-            for v, kb in enumerate(blocks):
-                nc.vector.tensor_copy(win[kb][:].indirect(entries(lo, hi)), dx[:, v, :])
+        def fetch(engine, dx_ps, place):
+            dx = keep.tile(dx_ps.shape, F32, name="dx", align_bytes=64, tag=place)
+            copy_on(engine)(dx[:], dx_ps)
+            return dx
+
+        def scatter(engine, dx, pieces):
+            at = 0
+            for kb, lo, hi in pieces:
+                if engine == "S":
+                    nc.scalar.activation(win[kb][:].indirect(entries(lo, hi)), dx[:, at : at + hi - lo], COPY)
+                else:
+                    nc.vector.tensor_copy(win[kb][:].indirect(entries(lo, hi)), dx[:, at : at + hi - lo])
+                at = at + hi - lo
                 if hi == S:
                     nc.sync.dma_start(out=out[kb * P : (kb + 1) * P, :], in_=win[kb][:])
 
-        gather_dy([0], 0, "gdA")
-        gather_dy([0], 1, "gdB")
-        gather_dy([1, 2], 1, "gdC")
-        for c in range(4):
-            slope(c)
-        da0 = front(0)
-        da1 = front(1)
-        gather_dy([1], 0, "relu0")
-        pack([da0], 0, "X")
-        pack([da1], P, "Z")
-        scatter(0, P, [0], back(0, P, [0], "E")[:], "dxA")
-        scatter(0, P, [1, 2, 3], back(0, P, [1, 2, 3], "Y")[:], "dxB")
-        gather_dy([2], 0, "da1")
-        gather_x(2, "grouped0")
-        da2 = front(2)
-        sums1 = back(P, C, [0, 1, 2, 3], "Y")
-        scatter(P, C, [0, 1], sums1[:, :2, :], "dxC")
-        da3 = front(3)
-        grad(4)
-        pack([da2], 2 * P, "Z")
-        scatter(P, C, [2, 3], sums1[:, 2:, :], "da2")
-        da4 = front(4, "grouped256")
-        grad(5)
-        pack([da3], 3 * P, "C")
-        sums = back(2 * P, 3 * P, [0, 1, 2, 3], "Z")
-        scatter(2 * P, 3 * P, [0], sums[:, :1, :], "dxD")
-        scatter(2 * P, 3 * P, [1, 2, 3], sums[:, 1:, :], "dxI")
-        da5 = front(5, "grouped384")
-        scatter(3 * P, 4 * P, [0], back(3 * P, 4 * P, [0], "X")[:], "dxE")
-        sums3 = back(3 * P, 4 * P, [1, 2, 3], "E")
-        pack([da4, da5], 4 * P, "C")
-        scatter(3 * P, 4 * P, [1, 2, 3], sums3[:], "grouped384")
-        sums4 = back(2 * C, S, [0, 1], "Y")
-        scatter(2 * C, S, [0], sums4[:, :1, :], "dxF")
-        scatter(2 * C, S, [1], sums4[:, 1:, :], "dxG")
-        scatter(2 * C, S, [2, 3], back(2 * C, S, [2, 3], "A")[:], "dxH")
+        def send(engine, pieces, bank, place, merged=None):
+            scatter(engine, fetch(engine, back(pieces, bank)[:], place), merged or pieces)
+
+        gather_dy(0, 0, "gdA")
+        gather_dy(0, 1, "gdB")
+        slope(0, "A")
+        gather_x(2, "gxsA")
+        for c in range(1, 4):
+            slope(c, "ABEY"[c])
+        gather_xs([4, 5], "gxsB")
+        dh0 = grad(0, "C")
+        dh1 = grad(1, "D")
+        slope(4, "A")
+        da0 = product(0, dh0)
+        da1 = product(1, dh1)
+        gather_dy(1, 1, "relu0")
+        quantise(turn([da0], "X"), 0, "S")
+        gather_dy(1, 0, "da0")
+        slope(5, "B")
+        quantise(turn([da1], "Z"), P, "S")
+        gather_dy(2, 0, "grouped0")
+        gather_dy(2, 1, "grouped128")
+        send("S", [(2, 0, P)], "E", "dxA")
+        send("S", [(3, 0, P)], "Y", "dxB")
+        dh2 = grad(2, "C", (1, 0))
+        dh3 = grad(3, "D", (1, 0))
+        dx1 = fetch("S", back([(2, P, C), (3, P, C)], "X")[:], "dxC")
+        scatter("S", dx1[:, :P], [(2, P, C)])
+        send("S", [(0, 0, C), (1, 0, C)], "Z", "dxD")
+        da2 = product(2, dh2)
+        da3 = product(3, dh3)
+        da4 = product(4, grad(4, "A"))
+        dh5 = grad(5, "B")
+        quantise(turn([da2, da3], "E"), C, "V")
+        da5 = product(5, dh5)
+        scatter("V", dx1[:, P:], [(3, P, C)])
+        quantise(turn([da4, da5], "Y"), 2 * C, "V")
+        send("V", [(2, C, 2 * C)], "C", "dxE")
+        send("V", [(2, 2 * C, S)], "D", "dxF")
+        send("S", [(0, C, 2 * C), (0, 2 * C, S)], "X", "dxG")
+        send("V", [(3, C, 2 * C), (3, 2 * C, S)], "A", "dxH", [(3, C, S)])
+        send("S", [(1, C, 2 * C), (1, 2 * C, S)], "B", "dxI")

@@ -56,7 +56,7 @@ def tile_moe_rec_mlp_relu2_kernel(
         win = [keep.tile([P, T], F32, name="win%d" % kb, align_bytes=64) for kb in range(KB)]
         gds = [keep.tile([P, S], U8, name="gds%d" % s, align_bytes=64) for s in range(NP)]
         daw = keep.tile([P, S], U32, name="daw", align_bytes=64)
-        das = keep.tile([P, S], U8, name="das", align_bytes=64)
+        das = {}
 
         def load_scales(plane, rows, queue, which=range(4)):
             for r in which:
@@ -100,8 +100,8 @@ def tile_moe_rec_mlp_relu2_kernel(
         nc.sync.dma_start(out=w1rest[1][:].bitcast(I32), in_=w1_rows[:, 2, :])
         nc.sync.dma_start(out=w3first[:].bitcast(I32), in_=w3_rows[:, 0, :])
         load_scales(w2s[1], w2_planes[:, NP:, :], nc.sync)
-        nc.sync.dma_start(out=w2rest[0][:].bitcast(I32), in_=w2_rows[:, NP : 2 * NP, :])
         load_scales(w3s, w1t_scales.rearrange("e s b n -> b (e s) n"), nc.sync)
+        nc.sync.dma_start(out=w2rest[0][:].bitcast(I32), in_=w2_rows[:, NP : 2 * NP, :])
         nc.sync.dma_start(out=w2rest[1][:].bitcast(I32), in_=w2_rows[:, 2 * NP :, :])
         nc.sync.dma_start(out=w3rest[:].bitcast(I32), in_=w3_rows[:, 1:, :])
 
@@ -118,7 +118,8 @@ def tile_moe_rec_mlp_relu2_kernel(
                 gxs_of[c] = got[:, n * P : (n + 1) * P]
 
         gather_xs([0], "gxsA")
-        gather_xs([1, 2, 3], "gxsB")
+        gather_xs([1], "gxsB")
+        gather_xs([2, 3], "gxsC")
         gxfirst = keep.tile([P, 2 * C], U32, name="gxfirst", align_bytes=64)
         nc.vector.tensor_copy(gxfirst[:], xw[:].bitcast(U32).indirect(entries(0, 2 * C)))
         gxw_of = {0: gxfirst[:, :C], 1: gxfirst[:, C:]}
@@ -163,9 +164,9 @@ def tile_moe_rec_mlp_relu2_kernel(
                                     start=(s == passes[0]), stop=(s == passes[-1]))
             return dh_ps
 
-        def product(c, dh_ps):
+        def product(c, dh_ps, place=None):
             e, h = divmod(c, HALVES)
-            da = keep.tile([P, H], BF16, name="da%d" % c, align_bytes=64)
+            da = keep.tile([P, H], BF16, name="da%d" % c, align_bytes=64, tag=place or "da%d" % c)
             for u in range(2):
                 half = slice(u * H // 2, (u + 1) * H // 2)
                 nc.vector.scalar_tensor_tensor(da[:, half].rearrange("p (w e) -> p w e", e=2), by_half(dh_ps)[:, u],
@@ -183,13 +184,19 @@ def tile_moe_rec_mlp_relu2_kernel(
         def copy_on(engine):
             return nc.scalar.copy if engine == "S" else nc.vector.tensor_copy
 
-        def quantise(xt, lo, engine):
+        def regroup(xt, lo, engine, place):
             chunks = xt.shape[1]
-            hi = lo + P * chunks
-            grouped = keep.tile([P, hi - lo, 4], BF16, name="grouped%d" % lo, align_bytes=64)
+            grouped = keep.tile([P, P * chunks, 4], BF16, name="grouped%d" % lo, align_bytes=64, tag=place)
             copy_on(engine)(grouped[:].bitcast(F32).rearrange("p (h j) u -> p h j u", h=chunks),
                             xt[:].rearrange("p h u j -> p h j u"))
-            nc.vector.quantize_mx(out=daw[:, lo:hi].bitcast(FP8X4), scales=das[:, lo:hi],
+            return grouped
+
+        def quantise(grouped, lo, place):
+            hi = lo + grouped.shape[1]
+            e = lo // C
+            if e not in das:
+                das[e] = keep.tile([P, C], U8, name="das%d" % e, align_bytes=64, tag=place)
+            nc.vector.quantize_mx(out=daw[:, lo:hi].bitcast(FP8X4), scales=das[e][:, lo - e * C : hi - e * C],
                                   in_=grouped[:].rearrange("p j t -> p (j t)"))
 
         def back(pieces, bank):
@@ -200,7 +207,7 @@ def tile_moe_rec_mlp_relu2_kernel(
                 w3 = w3first[:] if e == 0 else w3rest[:, e - 1, :]
                 nc.tensor.matmul_mx(out=dx_ps[:, at : at + hi - lo], lhsT=w3[:, 2 * P * kb : 2 * P * (kb + 1)].bitcast(FP4X4),
                                     lhsT_scale=w3s[:, e, P * kb : P * (kb + 1)],
-                                    rhs=daw[:, lo:hi].bitcast(FP8X4), rhs_scale=das[:, lo:hi], start=True, stop=True)
+                                    rhs=daw[:, lo:hi].bitcast(FP8X4), rhs_scale=das[e][:, lo - e * C : hi - e * C], start=True, stop=True)
                 at = at + hi - lo
             return dx_ps
 
@@ -218,7 +225,7 @@ def tile_moe_rec_mlp_relu2_kernel(
                     nc.vector.tensor_copy(win[kb][:].indirect(entries(lo, hi)), dx[:, at : at + hi - lo])
                 at = at + hi - lo
                 if hi == S:
-                    nc.sync.dma_start(out=out[kb * P : (kb + 1) * P, :], in_=win[kb][:])
+                    (nc.scalar if engine == "S" else nc.sync).dma_start(out=out[kb * P : (kb + 1) * P, :], in_=win[kb][:])
 
         def send(engine, pieces, bank, place, merged=None):
             scatter(engine, fetch(engine, back(pieces, bank)[:], place), merged or pieces)
@@ -227,38 +234,61 @@ def tile_moe_rec_mlp_relu2_kernel(
         gather_dy(0, 1, "gdB")
         slope(0, "A")
         gather_x(2, "gxsA")
-        for c in range(1, 4):
-            slope(c, "ABEY"[c])
+        slope(1, "B")
         gather_xs([4, 5], "gxsB")
+        slope(2, "E")
+        slope(3, "Y")
         dh0 = grad(0, "C")
         dh1 = grad(1, "D")
         slope(4, "A")
         da0 = product(0, dh0)
         da1 = product(1, dh1)
         gather_dy(1, 1, "relu0")
-        quantise(turn([da0], "X"), 0, "S")
-        gather_dy(1, 0, "da0")
-        slope(5, "B")
-        quantise(turn([da1], "Z"), P, "S")
+        quantise(regroup(turn([da0], "X"), 0, "S", "grouped0"), 0, "das0")
+        xt1 = turn([da1], "Z")
+        gather_dy(1, 0, "da1")
+        slope(5, "X")
+        quantise(regroup(xt1, P, "S", "grouped1"), P, "das0")
         gather_dy(2, 0, "grouped0")
-        gather_dy(2, 1, "grouped128")
+        gather_dy(2, 1, "gxsB")
         send("S", [(2, 0, P)], "E", "dxA")
-        send("S", [(3, 0, P)], "Y", "dxB")
+        send("S", [(3, 0, P), (0, 0, P), (1, 0, P)], "Y", "dxB")
         dh2 = grad(2, "C", (1, 0))
         dh3 = grad(3, "D", (1, 0))
-        dx1 = fetch("S", back([(2, P, C), (3, P, C)], "X")[:], "dxC")
-        scatter("S", dx1[:, :P], [(2, P, C)])
-        send("S", [(0, 0, C), (1, 0, C)], "Z", "dxD")
-        da2 = product(2, dh2)
-        da3 = product(3, dh3)
-        da4 = product(4, grad(4, "A"))
+        dh4 = grad(4, "A")
         dh5 = grad(5, "B")
-        quantise(turn([da2, da3], "E"), C, "V")
-        da5 = product(5, dh5)
-        scatter("V", dx1[:, P:], [(3, P, C)])
-        quantise(turn([da4, da5], "Y"), 2 * C, "V")
-        send("V", [(2, C, 2 * C)], "C", "dxE")
-        send("V", [(2, 2 * C, S)], "D", "dxF")
-        send("S", [(0, C, 2 * C), (0, 2 * C, S)], "X", "dxG")
-        send("V", [(3, C, 2 * C), (3, 2 * C, S)], "A", "dxH", [(3, C, S)])
-        send("S", [(1, C, 2 * C), (1, 2 * C, S)], "B", "dxI")
+        da2 = product(2, dh2)
+        sums = back([(2, P, C), (1, P, C)], "C")
+        first = fetch("S", sums[:, :P], "dxC")
+        dx1a = keep.tile([P, C], F32, name="dx1a", align_bytes=64)
+        nc.scalar.copy(dx1a[:, :P], sums[:, P:])
+        scatter("S", first, [(2, P, C)])
+        da3 = product(3, dh3)
+        xt23 = turn([da2, da3], "E")
+        da4 = product(4, dh4)
+        g23 = regroup(xt23, C, "V", "grouped2")
+        da5 = product(5, dh5, "da3")
+        xt45 = turn([da4, da5], "Y")
+        dx3 = fetch("V", back([(3, P, C), (0, P, C)], "E")[:], "dxE")
+        quantise(g23, C, "das1")
+        scatter("V", dx3[:, :P], [(3, P, C)])
+        g45 = regroup(xt45, 2 * C, "V", "grouped4")
+        scatter("V", dx3[:, P:], [(0, P, C)])
+        mid3 = back([(3, C, 2 * C), (1, C, 3 * P)], "Z")
+        mid2 = back([(2, C, 2 * C)], "A")
+        mid0 = back([(0, C, 2 * C)], "D")
+        dx21 = fetch("V", mid2[:], "dxF")
+        quantise(g45, 2 * C, "das2")
+        scatter("V", dx21, [(2, C, 2 * C)])
+        dx31 = fetch("S", mid3[:, :C], "dxI")
+        nc.scalar.copy(dx1a[:, P:], mid3[:, C:])
+        scatter("S", dx31, [(3, C, 2 * C)])
+        dx01 = fetch("S", mid0[:], "dxG")
+        scatter("S", dx1a, [(1, P, 3 * P)])
+        dx22 = fetch("V", back([(2, 2 * C, S)], "X")[:], "dxJ")
+        rest = fetch("V", back([(3, 2 * C, S), (0, 2 * C, S)], "B")[:], "dxK")
+        dx1b = fetch("S", back([(1, 3 * P, 2 * C), (1, 2 * C, S)], "C")[:], "dxL")
+        scatter("S", dx01, [(0, C, 2 * C)])
+        scatter("S", dx1b, [(1, 3 * P, S)])
+        scatter("V", dx22, [(2, 2 * C, S)])
+        scatter("V", rest, [(3, 2 * C, S), (0, 2 * C, S)])

@@ -225,7 +225,7 @@ def tile_moe_rec_mlp_relu2_kernel(
                     nc.vector.tensor_copy(win[kb][:].indirect(entries(lo, hi)), dx[:, at : at + hi - lo])
                 at = at + hi - lo
                 if hi == S:
-                    (nc.scalar if engine == "S" else nc.sync).dma_start(out=out[kb * P : (kb + 1) * P, :], in_=win[kb][:])
+                    nc.sync.dma_start(out=out[kb * P : (kb + 1) * P, :], in_=win[kb][:])
 
         def send(engine, pieces, bank, place, merged=None):
             scatter(engine, fetch(engine, back(pieces, bank)[:], place), merged or pieces)
@@ -258,37 +258,36 @@ def tile_moe_rec_mlp_relu2_kernel(
         dh4 = grad(4, "A")
         dh5 = grad(5, "B")
         da2 = product(2, dh2)
-        sums = back([(2, P, C), (1, P, C)], "C")
+        sums = back([(2, P, C), (0, P, C), (1, P, C)], "C")
         first = fetch("S", sums[:, :P], "dxC")
+        second = fetch("S", sums[:, P:C], "dxD")
         dx1a = keep.tile([P, C], F32, name="dx1a", align_bytes=64)
-        nc.scalar.copy(dx1a[:, :P], sums[:, P:])
+        nc.scalar.copy(dx1a[:, :P], sums[:, C:])
         scatter("S", first, [(2, P, C)])
+        scatter("S", second, [(0, P, C)])
         da3 = product(3, dh3)
         xt23 = turn([da2, da3], "E")
         da4 = product(4, dh4)
         g23 = regroup(xt23, C, "V", "grouped2")
         da5 = product(5, dh5, "da3")
         xt45 = turn([da4, da5], "Y")
-        dx3 = fetch("V", back([(3, P, C), (0, P, C)], "E")[:], "dxE")
+        dx3 = fetch("V", back([(3, P, C)], "E")[:], "dxE")
         quantise(g23, C, "das1")
-        scatter("V", dx3[:, :P], [(3, P, C)])
+        scatter("V", dx3, [(3, P, C)])
         g45 = regroup(xt45, 2 * C, "V", "grouped4")
-        scatter("V", dx3[:, P:], [(0, P, C)])
         mid3 = back([(3, C, 2 * C), (1, C, 3 * P)], "Z")
-        mid2 = back([(2, C, 2 * C)], "A")
-        mid0 = back([(0, C, 2 * C)], "D")
-        dx21 = fetch("V", mid2[:], "dxF")
+        dx21 = fetch("V", back([(2, C, 2 * C)], "A")[:], "dxF")
         quantise(g45, 2 * C, "das2")
         scatter("V", dx21, [(2, C, 2 * C)])
         dx31 = fetch("S", mid3[:, :C], "dxI")
         nc.scalar.copy(dx1a[:, P:], mid3[:, C:])
         scatter("S", dx31, [(3, C, 2 * C)])
-        dx01 = fetch("S", mid0[:], "dxG")
-        scatter("S", dx1a, [(1, P, 3 * P)])
         dx22 = fetch("V", back([(2, 2 * C, S)], "X")[:], "dxJ")
-        rest = fetch("V", back([(3, 2 * C, S), (0, 2 * C, S)], "B")[:], "dxK")
+        dx32 = fetch("S", back([(3, 2 * C, S)], "D")[:], "dxG")
+        scatter("S", dx1a, [(1, P, 3 * P)])
         dx1b = fetch("S", back([(1, 3 * P, 2 * C), (1, 2 * C, S)], "C")[:], "dxL")
-        scatter("S", dx01, [(0, C, 2 * C)])
-        scatter("S", dx1b, [(1, 3 * P, S)])
+        dx0 = fetch("V", back([(0, C, 2 * C), (0, 2 * C, S)], "B")[:], "dxK")
         scatter("V", dx22, [(2, 2 * C, S)])
-        scatter("V", rest, [(3, 2 * C, S), (0, 2 * C, S)])
+        scatter("S", dx32, [(3, 2 * C, S)])
+        scatter("V", dx0, [(0, C, S)])
+        scatter("S", dx1b, [(1, 3 * P, S)])

@@ -49,8 +49,8 @@ def tile_moe_rec_mlp_relu2_kernel(
         w3first = keep.tile([P, 2 * K], U8, name="w3first", align_bytes=64)
         w3rest = keep.tile([P, LAST, 2 * K], U8, name="w3rest", align_bytes=64)
         w3s = keep.tile([P, E, K], U8, name="w3s", align_bytes=64)
-        grows = keep.tile([P, E, P], F32, name="grows", align_bytes=64)
-        gcol = keep.tile([P, E, HALVES], F32, name="gcol")
+        grows = keep.tile([P, P], F32, name="grows", align_bytes=64)
+        gcol = keep.tile([P, E * HALVES], F32, name="gcol")
         ident = keep.tile([P, P], F32, name="ident")
         zero = keep.tile([P, 8], F32, name="zero")
         win = [keep.tile([P, T], F32, name="win%d" % kb, align_bytes=64) for kb in range(KB)]
@@ -82,13 +82,12 @@ def tile_moe_rec_mlp_relu2_kernel(
             nc.sync.dma_start(out=dys[q:P:16, :].bitcast(I32), in_=dy_scales.rearrange("s (q r) n -> r q s n", r=4)[q].bitcast(I32))
         nc.sync.dma_start(out=xw[:], in_=x_words[0].rearrange("p t d -> p (t d)").bitcast(I32))
         load_scales(xs, x_scales[0], nc.sync)
+        nc.gpsimd.dma_start(out=grows[0 : E * HALVES], in_=gate[0].rearrange("(c p) -> c p", p=P))
         load_scales(w1s, w1_planes, nc.gpsimd, range(1))
-        nc.gpsimd.dma_start(out=grows[0:HALVES], in_=gate[0].rearrange("(e h p) -> h e p", h=HALVES, p=P))
         make_identity(nc, ident[:])
-        turned = psum.tile([P, E, P], F32, name="turned", tag="X")
-        for e in range(E):
-            nc.tensor.transpose(turned[:, e, :], grows[:, e, :], ident[:])
-        nc.scalar.copy(gcol[:], turned[:, :, 0:HALVES])
+        turned = psum.tile([P, P], F32, name="turned", tag="X")
+        nc.tensor.transpose(turned[:], grows[:], ident[:])
+        nc.scalar.copy(gcol[:], turned[:, 0 : E * HALVES])
         nc.sync.dma_start(out=dyw[0][:], in_=dy_words[0].rearrange("p t d -> p (t d)").bitcast(I32))
         load_scales(w1s, w1_planes, nc.sync, range(1, 2))
         nc.sync.dma_start(out=dyw[1][:], in_=dy_words[1].rearrange("p t d -> p (t d)").bitcast(I32))
@@ -123,6 +122,15 @@ def tile_moe_rec_mlp_relu2_kernel(
         gxfirst = keep.tile([P, 2 * C], U32, name="gxfirst", align_bytes=64)
         nc.vector.tensor_copy(gxfirst[:], xw[:].bitcast(U32).indirect(entries(0, 2 * C)))
         gxw_of = {0: gxfirst[:, :C], 1: gxfirst[:, C:]}
+
+        def warm_up(bank, passes):
+            warm = psum.tile([P, H], F32, name="warm", tag=bank)
+            for n in range(passes):
+                nc.tensor.matmul_mx(out=warm[:], lhsT=gxfirst[:, :P].bitcast(FP8X4), lhsT_scale=gds[0][:, :P],
+                                    rhs=w1first[:, 0, :].bitcast(FP4X4), rhs_scale=gds[0][:, :H],
+                                    start=(n == 0), stop=(n == passes - 1))
+
+        warm_up("C", 2)
 
         def gather_x(e, place):
             gxw_of[e] = keep.tile([P, C], U32, name="gx%d" % e, align_bytes=64, tag=place)
@@ -165,12 +173,11 @@ def tile_moe_rec_mlp_relu2_kernel(
             return dh_ps
 
         def product(c, dh_ps, place=None):
-            e, h = divmod(c, HALVES)
             da = keep.tile([P, H], BF16, name="da%d" % c, align_bytes=64, tag=place or "da%d" % c)
             for u in range(2):
                 half = slice(u * H // 2, (u + 1) * H // 2)
                 nc.vector.scalar_tensor_tensor(da[:, half].rearrange("p (w e) -> p w e", e=2), by_half(dh_ps)[:, u],
-                                               gcol[:, e, h : h + 1], slopes[c][:, half].rearrange("p (w e) -> p w e", e=2), MULT, MULT)
+                                               gcol[:, c : c + 1], slopes[c][:, half].rearrange("p (w e) -> p w e", e=2), MULT, MULT)
             return da
 
         def turn(das_in, bank):
@@ -246,8 +253,9 @@ def tile_moe_rec_mlp_relu2_kernel(
         gather_dy(1, 1, "relu0")
         quantise(regroup(turn([da0], "X"), 0, "S", "grouped0"), 0, "das0")
         xt1 = turn([da1], "Z")
+        warm_up("C", 1)
+        slope(5, "D")
         gather_dy(1, 0, "da1")
-        slope(5, "X")
         quantise(regroup(xt1, P, "S", "grouped1"), P, "das0")
         gather_dy(2, 0, "grouped0")
         gather_dy(2, 1, "gxsB")
@@ -281,12 +289,14 @@ def tile_moe_rec_mlp_relu2_kernel(
         scatter("V", dx21, [(2, C, 2 * C)])
         dx31 = fetch("S", mid3[:, :C], "dxI")
         nc.scalar.copy(dx1a[:, P:], mid3[:, C:])
+        dx0 = keep.tile([P, 2 * C], F32, name="dx0", align_bytes=64)
+        nc.scalar.copy(dx0[:, :C], back([(0, C, 2 * C)], "D")[:])
         scatter("S", dx31, [(3, C, 2 * C)])
         dx22 = fetch("V", back([(2, 2 * C, S)], "X")[:], "dxJ")
-        dx32 = fetch("S", back([(3, 2 * C, S)], "D")[:], "dxG")
+        dx32 = fetch("S", back([(3, 2 * C, S)], "E")[:], "dxG")
         scatter("S", dx1a, [(1, P, 3 * P)])
         dx1b = fetch("S", back([(1, 3 * P, 2 * C), (1, 2 * C, S)], "C")[:], "dxL")
-        dx0 = fetch("V", back([(0, C, 2 * C), (0, 2 * C, S)], "B")[:], "dxK")
+        nc.vector.tensor_copy(dx0[:, C:], back([(0, 2 * C, S)], "B")[:])
         scatter("V", dx22, [(2, 2 * C, S)])
         scatter("S", dx32, [(3, 2 * C, S)])
         scatter("V", dx0, [(0, C, S)])

@@ -89,9 +89,9 @@ def tile_moe_rec_mlp_relu2_kernel(
         nc.tensor.transpose(turned[:], grows[:], ident[:])
         nc.scalar.copy(gcol[:], turned[:, 0 : E * HALVES])
         nc.sync.dma_start(out=dyw[0][:], in_=dy_words[0].rearrange("p t d -> p (t d)").bitcast(I32))
-        load_scales(w1s, w1_planes, nc.sync, range(1, 2))
+        load_scales(w1s, w1_planes, nc.sync, range(1, 3))
         nc.sync.dma_start(out=dyw[1][:], in_=dy_words[1].rearrange("p t d -> p (t d)").bitcast(I32))
-        load_scales(w1s, w1_planes, nc.sync, range(2, 4))
+        load_scales(w1s, w1_planes, nc.sync, range(3, 4))
         nc.vector.tensor_copy(gds[0][:], dys[:].indirect(offsets[:]))
         nc.sync.dma_start(out=gds[1][0:100, :].bitcast(I32), in_=gds[0][16:116, :].bitcast(I32))
         nc.sync.dma_start(out=w2first[:].bitcast(I32), in_=w2_rows[:, :NP, :])
@@ -119,9 +119,13 @@ def tile_moe_rec_mlp_relu2_kernel(
         gather_xs([0], "gxsA")
         gather_xs([1], "gxsB")
         gather_xs([2, 3], "gxsC")
-        gxfirst = keep.tile([P, 2 * C], U32, name="gxfirst", align_bytes=64)
-        nc.vector.tensor_copy(gxfirst[:], xw[:].bitcast(U32).indirect(entries(0, 2 * C)))
-        gxw_of = {0: gxfirst[:, :C], 1: gxfirst[:, C:]}
+        gxfirst = keep.tile([P, P], U32, name="gxfirst", align_bytes=64)
+        nc.vector.tensor_copy(gxfirst[:], xw[:].bitcast(U32).indirect(entries(0, P)))
+        gxmid = keep.tile([P, 2 * C - P], U32, name="gxmid", align_bytes=64)
+        nc.vector.tensor_copy(gxmid[:], xw[:].bitcast(U32).indirect(entries(P, 2 * C)))
+        gxw_of = {0: gxfirst[:]}
+        for c in range(1, 2 * HALVES):
+            gxw_of[c] = gxmid[:, (c - 1) * P : c * P]
 
         def warm_up(bank, passes):
             warm = psum.tile([P, H], F32, name="warm", tag=bank)
@@ -130,11 +134,13 @@ def tile_moe_rec_mlp_relu2_kernel(
                                     rhs=w1first[:, 0, :].bitcast(FP4X4), rhs_scale=gds[0][:, :H],
                                     start=(n == 0), stop=(n == passes - 1))
 
-        warm_up("C", 2)
+        warm_up("C", 3)
 
         def gather_x(e, place):
-            gxw_of[e] = keep.tile([P, C], U32, name="gx%d" % e, align_bytes=64, tag=place)
-            nc.vector.tensor_copy(gxw_of[e][:], xw[:].bitcast(U32).indirect(entries(e * C, (e + 1) * C)))
+            got = keep.tile([P, C], U32, name="gx%d" % e, align_bytes=64, tag=place)
+            nc.vector.tensor_copy(got[:], xw[:].bitcast(U32).indirect(entries(e * C, (e + 1) * C)))
+            for h in range(HALVES):
+                gxw_of[e * HALVES + h] = got[:, h * P : (h + 1) * P]
 
         gdw = {}
 
@@ -153,7 +159,7 @@ def tile_moe_rec_mlp_relu2_kernel(
             cols = slice(h * P, (h + 1) * P)
             a_ps = psum.tile([P, H], F32, name="a_ps", tag=bank)
             gxs = gxs_of[c]
-            gxw = gxw_of[e][:, cols]
+            gxw = gxw_of[c]
             nc.tensor.matmul_mx(out=a_ps[:], lhsT=gxw.bitcast(FP8X4), lhsT_scale=gxs,
                                 rhs=w1.bitcast(FP4X4), rhs_scale=w1s[:, e, :], start=True, stop=True)
             relu2 = keep.tile([P, H], F32, name="relu%d" % c, align_bytes=64)
@@ -264,40 +270,38 @@ def tile_moe_rec_mlp_relu2_kernel(
         dh2 = grad(2, "C", (1, 0))
         dh3 = grad(3, "D", (1, 0))
         dh4 = grad(4, "A")
-        dh5 = grad(5, "B")
         da2 = product(2, dh2)
-        sums = back([(2, P, C), (0, P, C), (1, P, C)], "C")
-        first = fetch("S", sums[:, :P], "dxC")
-        second = fetch("S", sums[:, P:C], "dxD")
-        dx1a = keep.tile([P, C], F32, name="dx1a", align_bytes=64)
-        nc.scalar.copy(dx1a[:, :P], sums[:, C:])
-        scatter("S", first, [(2, P, C)])
-        scatter("S", second, [(0, P, C)])
         da3 = product(3, dh3)
         xt23 = turn([da2, da3], "E")
+        dh5 = grad(5, "B")
+        sums = back([(2, P, C), (0, P, C), (1, P, C)], "C")
+        first = fetch("S", sums[:, :P], "dxC")
+        row = keep.tile([P, 3 * P + 2 * C], F32, name="row", align_bytes=64)
+        nc.scalar.copy(row[:, :C], sums[:, P:])
+        scatter("S", first, [(2, P, C)])
+        scatter("S", row[:, :P], [(0, P, C)])
         da4 = product(4, dh4)
+        sums3 = back([(3, P, C)], "A")
         g23 = regroup(xt23, C, "V", "grouped2")
         da5 = product(5, dh5, "da3")
         xt45 = turn([da4, da5], "Y")
-        dx3 = fetch("V", back([(3, P, C)], "E")[:], "dxE")
+        dx3 = fetch("V", sums3[:], "dxE")
         quantise(g23, C, "das1")
         scatter("V", dx3, [(3, P, C)])
         g45 = regroup(xt45, 2 * C, "V", "grouped4")
-        mid3 = back([(3, C, 2 * C), (1, C, 3 * P)], "Z")
-        dx21 = fetch("V", back([(2, C, 2 * C)], "A")[:], "dxF")
+        mid3 = back([(3, C, 2 * C)], "Z")
+        dx21 = fetch("V", back([(2, C, 2 * C)], "E")[:], "dxF")
         quantise(g45, 2 * C, "das2")
         scatter("V", dx21, [(2, C, 2 * C)])
-        dx31 = fetch("S", mid3[:, :C], "dxI")
-        nc.scalar.copy(dx1a[:, P:], mid3[:, C:])
-        dx0 = keep.tile([P, 2 * C], F32, name="dx0", align_bytes=64)
-        nc.scalar.copy(dx0[:, :C], back([(0, C, 2 * C)], "D")[:])
+        dx31 = fetch("S", mid3[:], "dxI")
+        nc.scalar.copy(row[:, C : C + 3 * P], back([(1, C, 3 * P), (0, C, 2 * C)], "D")[:])
         scatter("S", dx31, [(3, C, 2 * C)])
         dx22 = fetch("V", back([(2, 2 * C, S)], "X")[:], "dxJ")
-        dx32 = fetch("S", back([(3, 2 * C, S)], "E")[:], "dxG")
-        scatter("S", dx1a, [(1, P, 3 * P)])
+        dx32 = fetch("S", back([(3, 2 * C, S)], "A")[:], "dxG")
+        scatter("S", row[:, P : 3 * P], [(1, P, 3 * P)])
         dx1b = fetch("S", back([(1, 3 * P, 2 * C), (1, 2 * C, S)], "C")[:], "dxL")
-        nc.vector.tensor_copy(dx0[:, C:], back([(0, 2 * C, S)], "B")[:])
+        nc.vector.tensor_copy(row[:, C + 3 * P :], back([(0, 2 * C, S)], "B")[:])
         scatter("V", dx22, [(2, 2 * C, S)])
         scatter("S", dx32, [(3, 2 * C, S)])
-        scatter("V", dx0, [(0, C, S)])
+        scatter("V", row[:, 3 * P :], [(0, C, S)])
         scatter("S", dx1b, [(1, 3 * P, S)])

from contextlib import ExitStack

import concourse.mybir as mybir
from concourse.masks import make_identity

K, T, E, C, H, N = 512, 1024, 3, 256, 512, 1024
S = E * C
FLOPS = 2 * S * (K * H + N * H + H * K)

F32 = mybir.dt.float32
BF16 = mybir.dt.bfloat16
I32 = mybir.dt.int32
U32 = mybir.dt.uint32
U16 = mybir.dt.uint16
U8 = mybir.dt.uint8
FP8X4 = mybir.dt.float8_e4m3fn_x4
FP4X4 = mybir.dt.float4_e2m1fn_x4
MULT = mybir.AluOpType.mult
COPY = mybir.ActivationFunctionType.Copy
RELU = mybir.ActivationFunctionType.Relu

P = 128
NP = N // 512
HALVES = C // P
KB = K // P
LAST = E - 1


def tile_moe_rec_mlp_relu2_kernel(
    tc, x_words, x_scales, dy_words, dy_scales, w1_words, w1_scales, w2t_words, w2t_scales,
    w1t_words, w1t_scales, gate, offs, out
):
    nc = tc.nc
    with ExitStack() as ctx:
        keep = ctx.enter_context(tc.tile_pool(name="keep", bufs=1))
        psum = ctx.enter_context(tc.psum_pool(name="psum", bufs=1))

        offsets = keep.tile([P, S // 16], U16, name="offsets")
        xw = keep.tile([P, T], I32, name="xw", align_bytes=64)
        xs = keep.tile([P, T], U8, name="xs", align_bytes=64)
        dyw = [keep.tile([P, T], I32, name="dyw%d" % s, align_bytes=64) for s in range(NP)]
        dys = keep.tile([P, T], U8, name="dys", align_bytes=64)
        w1first = keep.tile([P, 2, 2 * H], U8, name="w1first", align_bytes=64)
        w1rest = {1: keep.tile([P, 2 * H], U8, name="w1last", align_bytes=64)}
        w1s = keep.tile([P, E, H], U8, name="w1s", align_bytes=64)
        w2first = keep.tile([P, NP, 2 * H], U8, name="w2first", align_bytes=64)
        w2rest = [keep.tile([P, NP, 2 * H], U8, name="w2rest%d" % e, align_bytes=64) for e in range(LAST)]
        w2s = [keep.tile([P, n * NP, H], U8, name="w2s%d" % n, align_bytes=64) for n in (1, LAST)]
        w3first = keep.tile([P, 2 * K], U8, name="w3first", align_bytes=64)
        w3rest = keep.tile([P, LAST, 2 * K], U8, name="w3rest", align_bytes=64)
        w3s = keep.tile([P, E, K], U8, name="w3s", align_bytes=64)
        grows = keep.tile([P, P], F32, name="grows", align_bytes=64)
        gcol = keep.tile([P, E * HALVES], F32, name="gcol")
        ident = keep.tile([P, P], F32, name="ident")
        zero = keep.tile([P, 8], F32, name="zero")
        win = [keep.tile([P, T], F32, name="win%d" % kb, align_bytes=64) for kb in range(KB)]
        gds = [keep.tile([P, S], U8, name="gds%d" % s, align_bytes=64) for s in range(NP)]
        daw = keep.tile([P, S], U32, name="daw", align_bytes=64)
        das = {}

        def load_scales(plane, rows, queue, which=range(4)):
            for r in which:
                queue.dma_start(out=plane[r:P:32].bitcast(I32), in_=rows[r:16:4].bitcast(I32))

        def entries(a, b):
            return offsets[:, a // 16 : b // 16]

        nc.gpsimd.memset(dys[:].bitcast(I32), 0)
        nc.gpsimd.memset(xs[:].bitcast(I32), 0)
        nc.vector.memset(zero[:], 0.0)
        nc.vector.memset(grows[:], 0.0)

        w2_rows = w2t_words.rearrange("e s p n -> p (e s) n").bitcast(I32)
        w1_rows = w1_words.rearrange("e s p n -> p (e s) n").bitcast(I32)
        w1_planes = w1_scales.rearrange("e s b n -> b (e s) n")
        w2_planes = w2t_scales.rearrange("e s b n -> b (e s) n")
        w3_rows = w1t_words.rearrange("e s p n -> p (e s) n").bitcast(I32)

        nc.sync.dma_start(offsets[:], offs)
        nc.sync.dma_start(out=w1first[:].bitcast(I32), in_=w1_rows[:, :2, :])
        for q in range(4):
            nc.sync.dma_start(out=dys[q:P:16, :].bitcast(I32), in_=dy_scales.rearrange("s (q r) n -> r q s n", r=4)[q].bitcast(I32))
        nc.sync.dma_start(out=xw[:], in_=x_words[0].rearrange("p t d -> p (t d)").bitcast(I32))
        load_scales(xs, x_scales[0], nc.sync)
        nc.gpsimd.dma_start(out=grows[0 : E * HALVES], in_=gate[0].rearrange("(c p) -> c p", p=P))
        load_scales(w1s, w1_planes, nc.gpsimd, range(1))
        make_identity(nc, ident[:])
        turned = psum.tile([P, P], F32, name="turned", tag="X")
        nc.tensor.transpose(turned[:], grows[:], ident[:])
        nc.scalar.copy(gcol[:], turned[:, 0 : E * HALVES])
        nc.sync.dma_start(out=dyw[0][:], in_=dy_words[0].rearrange("p t d -> p (t d)").bitcast(I32))
        load_scales(w1s, w1_planes, nc.sync, range(1, 3))
        nc.sync.dma_start(out=dyw[1][:], in_=dy_words[1].rearrange("p t d -> p (t d)").bitcast(I32))
        load_scales(w1s, w1_planes, nc.sync, range(3, 4))
        nc.vector.tensor_copy(gds[0][:], dys[:].indirect(offsets[:]))
        nc.sync.dma_start(out=gds[1][0:100, :].bitcast(I32), in_=gds[0][16:116, :].bitcast(I32))
        nc.sync.dma_start(out=w2first[:].bitcast(I32), in_=w2_rows[:, :NP, :])
        load_scales(w2s[0], w2_planes[:, :NP, :], nc.sync)
        nc.sync.dma_start(out=w1rest[1][:].bitcast(I32), in_=w1_rows[:, 2, :])
        nc.sync.dma_start(out=w3first[:].bitcast(I32), in_=w3_rows[:, 0, :])
        load_scales(w2s[1], w2_planes[:, NP:, :], nc.sync)
        load_scales(w3s, w1t_scales.rearrange("e s b n -> b (e s) n"), nc.sync)
        nc.sync.dma_start(out=w2rest[0][:].bitcast(I32), in_=w2_rows[:, NP : 2 * NP, :])
        nc.sync.dma_start(out=w2rest[1][:].bitcast(I32), in_=w2_rows[:, 2 * NP :, :])
        nc.sync.dma_start(out=w3rest[:].bitcast(I32), in_=w3_rows[:, 1:, :])


        for kb in range(KB):
            nc.scalar.activation(win[kb][:], zero[:, 0:1].to_broadcast([P, T]), RELU)

        gxs_of = {}

        def gather_xs(chunks, place):
            got = keep.tile([P, P * len(chunks)], U8, name="gxs%d" % chunks[0], align_bytes=64, tag=place)
            nc.vector.tensor_copy(got[:], xs[:].indirect(entries(chunks[0] * P, (chunks[-1] + 1) * P)))
            for n, c in enumerate(chunks):
                gxs_of[c] = got[:, n * P : (n + 1) * P]

        gather_xs([0], "gxsA")
        gather_xs([1], "gxsB")
        gather_xs([2, 3], "gxsC")
        gxfirst = keep.tile([P, P], U32, name="gxfirst", align_bytes=64)
        nc.vector.tensor_copy(gxfirst[:], xw[:].bitcast(U32).indirect(entries(0, P)))
        gxmid = keep.tile([P, 2 * C - P], U32, name="gxmid", align_bytes=64)
        nc.vector.tensor_copy(gxmid[:], xw[:].bitcast(U32).indirect(entries(P, 2 * C)))
        gxw_of = {0: gxfirst[:]}
        for c in range(1, 2 * HALVES):
            gxw_of[c] = gxmid[:, (c - 1) * P : c * P]

        def warm_up(bank, passes):
            warm = psum.tile([P, H], F32, name="warm", tag=bank)
            for n in range(passes):
                nc.tensor.matmul_mx(out=warm[:], lhsT=gxfirst[:, :P].bitcast(FP8X4), lhsT_scale=gds[0][:, :P],
                                    rhs=w1first[:, 0, :].bitcast(FP4X4), rhs_scale=gds[0][:, :H],
                                    start=(n == 0), stop=(n == passes - 1))

        warm_up("C", 3)

        def gather_x(e, place):
            got = keep.tile([P, C], U32, name="gx%d" % e, align_bytes=64, tag=place)
            nc.vector.tensor_copy(got[:], xw[:].bitcast(U32).indirect(entries(e * C, (e + 1) * C)))
            for h in range(HALVES):
                gxw_of[e * HALVES + h] = got[:, h * P : (h + 1) * P]

        gdw = {}

        def gather_dy(e, s, place):
            gdw[e, s] = keep.tile([P, C], U32, name="gd%d_%d" % (s, e), align_bytes=64, tag=place)
            nc.vector.tensor_copy(gdw[e, s][:], dyw[s][:].bitcast(U32).indirect(entries(e * C, (e + 1) * C)))

        slopes = {}

        def by_half(ps):
            return ps[:].rearrange("p (w u e) -> p u w e", u=2, e=2)

        def slope(c, bank):
            e, h = divmod(c, HALVES)
            w1 = w1first[:, e, :] if e < 2 else w1rest[1][:]
            cols = slice(h * P, (h + 1) * P)
            a_ps = psum.tile([P, H], F32, name="a_ps", tag=bank)
            gxs = gxs_of[c]
            gxw = gxw_of[c]
            nc.tensor.matmul_mx(out=a_ps[:], lhsT=gxw.bitcast(FP8X4), lhsT_scale=gxs,
                                rhs=w1.bitcast(FP4X4), rhs_scale=w1s[:, e, :], start=True, stop=True)
            relu2 = keep.tile([P, H], F32, name="relu%d" % c, align_bytes=64)
            nc.scalar.activation(relu2[:].rearrange("p (u w e) -> p u w e", u=2, e=2), by_half(a_ps), RELU, scale=2.0)
            slopes[c] = relu2

        def grad(c, bank, passes=(0, 1)):
            e, h = divmod(c, HALVES)
            cols = slice(h * P, (h + 1) * P)
            slots = slice(c * P, (c + 1) * P)
            dh_ps = psum.tile([P, H], F32, name="dh_ps", tag=bank)
            for s in passes:
                w2 = w2first[:, s, :] if e == 0 else w2rest[e - 1][:, s, :]
                nc.tensor.matmul_mx(out=dh_ps[:], lhsT=gdw[e, s][:, cols].bitcast(FP8X4), lhsT_scale=gds[s][:, slots],
                                    rhs=w2.bitcast(FP4X4), rhs_scale=w2s[0][:, s, :] if e == 0 else w2s[1][:, (e - 1) * NP + s, :],
                                    start=(s == passes[0]), stop=(s == passes[-1]))
            return dh_ps

        def product(c, dh_ps, place=None):
            da = keep.tile([P, H], BF16, name="da%d" % c, align_bytes=64, tag=place or "da%d" % c)
            for u in range(2):
                half = slice(u * H // 2, (u + 1) * H // 2)
                nc.vector.scalar_tensor_tensor(da[:, half].rearrange("p (w e) -> p w e", e=2), by_half(dh_ps)[:, u],
                                               gcol[:, c : c + 1], slopes[c][:, half].rearrange("p (w e) -> p w e", e=2), MULT, MULT)
            return da

        def turn(das_in, bank):
            xt = psum.tile([P, len(das_in), 2, P], F32, name="xt", tag=bank)
            for n, da in enumerate(das_in):
                pairs = da[:].bitcast(F32)
                for u in range(2):
                    nc.tensor.transpose(xt[:, n, u, :], pairs[:, u * P : (u + 1) * P], ident[:])
            return xt

        def copy_on(engine):
            return nc.scalar.copy if engine == "S" else nc.vector.tensor_copy

        def regroup(xt, lo, engine, place):
            chunks = xt.shape[1]
            grouped = keep.tile([P, P * chunks, 4], BF16, name="grouped%d" % lo, align_bytes=64, tag=place)
            copy_on(engine)(grouped[:].bitcast(F32).rearrange("p (h j) u -> p h j u", h=chunks),
                            xt[:].rearrange("p h u j -> p h j u"))
            return grouped

        def quantise(grouped, lo, place):
            hi = lo + grouped.shape[1]
            e = lo // C
            if e not in das:
                das[e] = keep.tile([P, C], U8, name="das%d" % e, align_bytes=64, tag=place)
            nc.vector.quantize_mx(out=daw[:, lo:hi].bitcast(FP8X4), scales=das[e][:, lo - e * C : hi - e * C],
                                  in_=grouped[:].rearrange("p j t -> p (j t)"))

        def back(pieces, bank):
            dx_ps = psum.tile([P, sum(hi - lo for kb, lo, hi in pieces)], F32, name="dx_ps", tag=bank)
            at = 0
            for kb, lo, hi in pieces:
                e = lo // C
                w3 = w3first[:] if e == 0 else w3rest[:, e - 1, :]
                nc.tensor.matmul_mx(out=dx_ps[:, at : at + hi - lo], lhsT=w3[:, 2 * P * kb : 2 * P * (kb + 1)].bitcast(FP4X4),
                                    lhsT_scale=w3s[:, e, P * kb : P * (kb + 1)],
                                    rhs=daw[:, lo:hi].bitcast(FP8X4), rhs_scale=das[e][:, lo - e * C : hi - e * C], start=True, stop=True)
                at = at + hi - lo
            return dx_ps

        def fetch(engine, dx_ps, place):
            dx = keep.tile(dx_ps.shape, F32, name="dx", align_bytes=64, tag=place)
            copy_on(engine)(dx[:], dx_ps)
            return dx

        def scatter(engine, dx, pieces):
            at = 0
            for kb, lo, hi in pieces:
                if engine == "S":
                    nc.scalar.activation(win[kb][:].indirect(entries(lo, hi)), dx[:, at : at + hi - lo], COPY)
                else:
                    nc.vector.tensor_copy(win[kb][:].indirect(entries(lo, hi)), dx[:, at : at + hi - lo])
                at = at + hi - lo
                if hi == S:
                    nc.sync.dma_start(out=out[kb * P : (kb + 1) * P, :], in_=win[kb][:])

        def send(engine, pieces, bank, place, merged=None):
            scatter(engine, fetch(engine, back(pieces, bank)[:], place), merged or pieces)

        gather_dy(0, 0, "gdA")
        gather_dy(0, 1, "gdB")
        slope(0, "A")
        gather_x(2, "gxsA")
        slope(1, "B")
        gather_xs([4, 5], "gxsB")
        slope(2, "E")
        slope(3, "Y")
        dh0 = grad(0, "C")
        dh1 = grad(1, "D")
        slope(4, "A")
        da0 = product(0, dh0)
        da1 = product(1, dh1)
        gather_dy(1, 1, "relu0")
        quantise(regroup(turn([da0], "X"), 0, "S", "grouped0"), 0, "das0")
        xt1 = turn([da1], "Z")
        warm_up("C", 1)
        slope(5, "D")
        gather_dy(1, 0, "da1")
        quantise(regroup(xt1, P, "S", "grouped1"), P, "das0")
        gather_dy(2, 0, "grouped0")
        gather_dy(2, 1, "gxsB")
        send("S", [(2, 0, P)], "E", "dxA")
        send("S", [(3, 0, P), (0, 0, P), (1, 0, P)], "Y", "dxB")
        dh2 = grad(2, "C", (1, 0))
        dh3 = grad(3, "D", (1, 0))
        dh4 = grad(4, "A")
        da2 = product(2, dh2)
        da3 = product(3, dh3)
        xt23 = turn([da2, da3], "E")
        dh5 = grad(5, "B")
        sums = back([(2, P, C), (0, P, C), (1, P, C)], "C")
        first = fetch("S", sums[:, :P], "dxC")
        row = keep.tile([P, 3 * P + 2 * C], F32, name="row", align_bytes=64)
        nc.scalar.copy(row[:, :C], sums[:, P:])
        scatter("S", first, [(2, P, C)])
        scatter("S", row[:, :P], [(0, P, C)])
        da4 = product(4, dh4)
        sums3 = back([(3, P, C)], "A")
        g23 = regroup(xt23, C, "V", "grouped2")
        da5 = product(5, dh5, "da3")
        xt45 = turn([da4, da5], "Y")
        dx3 = fetch("V", sums3[:], "dxE")
        quantise(g23, C, "das1")
        scatter("V", dx3, [(3, P, C)])
        g45 = regroup(xt45, 2 * C, "V", "grouped4")
        mid3 = back([(3, C, 2 * C)], "Z")
        dx21 = fetch("V", back([(2, C, 2 * C)], "E")[:], "dxF")
        quantise(g45, 2 * C, "das2")
        scatter("V", dx21, [(2, C, 2 * C)])
        dx31 = fetch("S", mid3[:], "dxI")
        nc.scalar.copy(row[:, C : C + 3 * P], back([(1, C, 3 * P), (0, C, 2 * C)], "D")[:])
        scatter("S", dx31, [(3, C, 2 * C)])
        dx22 = fetch("V", back([(2, 2 * C, S)], "X")[:], "dxJ")
        dx32 = fetch("S", back([(3, 2 * C, S)], "A")[:], "dxG")
        scatter("S", row[:, P : 3 * P], [(1, P, 3 * P)])
        dx1b = fetch("S", back([(1, 3 * P, 2 * C), (1, 2 * C, S)], "C")[:], "dxL")
        nc.vector.tensor_copy(row[:, C + 3 * P :], back([(0, 2 * C, S)], "B")[:])
        scatter("V", dx22, [(2, 2 * C, S)])
        scatter("S", dx32, [(3, 2 * C, S)])
        scatter("V", row[:, 3 * P :], [(0, C, S)])
        scatter("S", dx1b, [(1, 3 * P, S)])
